import numpy as np
import ml_dtypes


def mxq(x, axis, fmt="e4m3"):
    dtype, down = {"e4m3": (ml_dtypes.float8_e4m3fn, 7), "e5m2": (ml_dtypes.float8_e5m2, 14)}[fmt]
    v = np.moveaxis(np.asarray(x, np.float32).astype(ml_dtypes.bfloat16).astype(np.float64), axis, -1)
    blocks = v.reshape(v.shape[:-1] + (-1, 32))
    amax = np.abs(blocks).max(-1, keepdims=True)
    byte = np.maximum(np.where(amax > 0, np.frexp(amax)[1] - 1 + 127, 0) - down, 1)
    scale = np.exp2(byte - 127.0)
    codes = (blocks / scale).astype(np.float32).astype(dtype).astype(np.float64)
    return np.moveaxis((codes * scale).reshape(v.shape), -1, axis)


WIDE = False


def mx_kscale(k):
    if not WIDE:
        return np.ones(k)
    levels = np.array([30, -30])
    if k % 512:
        return np.exp2(np.random.permutation(np.resize(levels, k // 32))).repeat(32)
    a = np.empty((k // 512, 16))
    for p in range(k // 512):
        a[p, :8] = np.random.permutation(np.resize(levels, 8))
        for g in range(8):
            far = levels[np.abs(levels - a[p, g]) >= 10]
            a[p, g + 8] = far[np.random.randint(len(far))]
    return np.exp2(a.ravel()).repeat(32)


def f64(x):
    return np.asarray(x).astype(np.float64)


def striped(idx):
    return np.tile(idx.reshape(-1, 16).T, (8, 1)).astype(np.uint16)


def unstriped(offs):
    return offs[:16].T.reshape(-1).astype(np.int64)


E2M1 = np.array([0.0, 0.5, 1.0, 1.5, 2.0, 3.0, 4.0, 6.0, -0.0, -0.5, -1.0, -1.5, -2.0, -3.0, -4.0, -6.0])


def pack_weight(w, fmt):
    k, n = w.shape
    w = f64(np.asarray(w, np.float32).astype(ml_dtypes.bfloat16)).reshape(k // 32, 32, n)
    amax = np.abs(w).max(1)
    if fmt == "e4m3":
        byte = np.frexp(amax)[1] - 1 + 127 - 7
    else:
        mant, ex = np.frexp(amax / 6.0)
        byte = np.where(mant > 0.5, ex, ex - 1) + 127
    byte = np.clip(np.where(amax > 0, byte, 1), 1, 254)
    scaled = (w * np.exp2(127.0 - byte)[:, None, :]).reshape(k, n).astype(np.float32)
    by_word = np.ascontiguousarray(scaled.reshape(k // 512, 128, 4, n).transpose(0, 1, 3, 2))
    if fmt == "e4m3":
        words = by_word.astype(ml_dtypes.float8_e4m3fn).view(np.uint8)
    else:
        c = by_word.astype(ml_dtypes.float4_e2m1fn).view(np.uint8) & 0xF
        words = (c[..., 0::2] | (c[..., 1::2] << 4)).reshape(k // 512, 128, 2 * n)
    return np.ascontiguousarray(words), np.ascontiguousarray(byte.astype(np.uint8).reshape(k // 512, 16, n))


def unpack_weight(words, scales, fmt):
    g, _, n = scales.shape
    words = np.ascontiguousarray(words).reshape(g, 128, n, -1)
    if fmt == "e4m3":
        vals = words.view(ml_dtypes.float8_e4m3fn).astype(np.float64)
    else:
        nib = np.empty((g, 128, n, 4), np.uint8)
        nib[..., 0::2] = words & 0xF
        nib[..., 1::2] = words >> 4
        vals = E2M1[nib]
    vals = vals * np.repeat(np.exp2(scales.astype(np.float64) - 127.0), 8, axis=1)[..., None]
    return vals.transpose(0, 1, 3, 2).reshape(g * 512, n)


def d_relu(v):
    return (v > 0).astype(np.float64)


K, T, E, C, H, N = 768, 1536, 2, 512, 512, 1024


def by_expert(wq, xq):
    return np.concatenate([wq[e].T @ xq[:, e * C:(e + 1) * C] for e in range(E)], axis=1)


def setup_inputs():
    n = np.random.standard_normal
    s = mx_kscale(N)[:, None]
    u = mx_kscale(H)
    w2 = [pack_weight(m, "e2m1") for m in n((E, N, H)) / np.sqrt(N) / s[None] * u[None, None, :]]
    w1 = [pack_weight(m, "e2m1") for m in n((E, H, K)) / np.sqrt(H) / u[None, :, None]]
    return {
        "dyT": (n((N, T)) * s).astype(np.float32),
        "a": n((H, E * C)).astype(np.float32),
        "w2_words": np.stack([m[0] for m in w2]),
        "w2_scales": np.stack([m[1] for m in w2]),
        "w1_words": np.stack([m[0] for m in w1]),
        "w1_scales": np.stack([m[1] for m in w1]),
        "gate": np.tile(np.random.uniform(0.2, 1.0, E * C), (N, 1)).astype(np.float32),
        "offs": striped(np.random.permutation(T)[:E * C]),
    }


def reference(dyT, a, w2_words, w2_scales, w1_words, w1_scales, gate, offs):
    idx = unstriped(offs)
    w2 = np.stack([unpack_weight(w2_words[e], w2_scales[e], "e2m1") for e in range(E)])
    w1 = np.stack([unpack_weight(w1_words[e], w1_scales[e], "e2m1") for e in range(E)])
    gq = mxq(f64(gate) * f64(dyT)[:, idx], 0, "e5m2")
    dh = by_expert(w2, gq)
    da = dh * d_relu(f64(a))
    dx = by_expert(w1, mxq(da, 0, "e5m2"))
    out = np.zeros((K, T))
    out[:, idx] = dx
    return out

@@ -1,0 +1,186 @@
+from contextlib import ExitStack
+
+import concourse.mybir as mybir
+
+K, T, E, C, H, N = 768, 1536, 2, 512, 512, 1024
+S = E * C
+P = 128
+PACK = 4
+N_PASSES = N // (P * PACK)
+K_BLOCKS = K // P
+JOINT = 2
+
+FLOPS = 2 * S * H * (N + K)
+BYTES = 4 * N * T + 4 * H * S + E * (N * H + H * K) // 2 + E * (N * H + H * K) // 32 + 4 * S + 2 * P * S // 16 + 4 * K * T
+
+F32 = mybir.dt.float32
+BF16 = mybir.dt.bfloat16
+I32 = mybir.dt.int32
+U32 = mybir.dt.uint32
+U16 = mybir.dt.uint16
+U8 = mybir.dt.uint8
+FP4X4 = mybir.dt.float4_e2m1fn_x4
+FP8X4 = mybir.dt.float8_e5m2_x4
+MULT = mybir.AluOpType.mult
+IS_GT = mybir.AluOpType.is_gt
+SIGN = mybir.ActivationFunctionType.Sign
+RELU = mybir.ActivationFunctionType.Relu
+
+
+def tile_moe_bdx_mlp_relu_kernel(tc, dyT, a, w2_words, w2_scales, w1_words, w1_scales, gate, offs, out):
+    nc = tc.nc
+    with ExitStack() as ctx:
+        keep = ctx.enter_context(tc.tile_pool(name="keep", bufs=1))
+        psum_h = ctx.enter_context(tc.psum_pool(name="psum_h", bufs=4))
+        psum_x = ctx.enter_context(tc.psum_pool(name="psum_x", bufs=4))
+
+        offs_sb = keep.tile([P, S // 16], U16, name="offs_sb")
+        gate_sb = keep.tile([P, S], F32, name="gate_sb")
+        planes = [[keep.tile([P, T], F32, name=f"dy_{s}_{t}") for t in range(PACK)] for s in range(N_PASSES)]
+        a_sb = [keep.tile([P, PACK, C], F32, name=f"a_{e}") for e in range(E)]
+        w2_raw = [keep.tile([P, N_PASSES, 2 * H], U8, name=f"w2_raw_{e}", align_bytes=64) for e in range(E)]
+        w2_sb = [keep.tile([P, N_PASSES, 2 * H], U8, name=f"w2_{e}", align_bytes=64) for e in range(E)]
+        s2_raw = keep.tile([P, E * N_PASSES, H], U8, name="s2_raw", align_bytes=64)
+        s2_sb = keep.tile([P, E * N_PASSES, H], U8, name="s2_sb", align_bytes=64)
+        w1_sb = keep.tile([P, E, 2 * K], U8, name="w1_sb", align_bytes=64)
+        s1_sb = keep.tile([P, E, K], U8, name="s1_sb", align_bytes=64)
+        windows = [keep.tile([P, T], F32, name=f"window_{b}") for b in range(K_BLOCKS)]
+        g0 = keep.tile([P, PACK, S], F32, name="g0")
+        codes = [[keep.tile([P, C], U32, name=f"codes_{s}_{e}", align_bytes=64) for e in range(E)] for s in range(N_PASSES)]
+        scales = [[keep.tile([P, C], U8, name=f"scales_{s}_{e}", align_bytes=64) for e in range(E)] for s in range(N_PASSES)]
+
+        s2_view = w2_scales.rearrange("e s f i -> f (e s) i")
+        s1_view = w1_scales.rearrange("e s f k -> f (e s) k")
+        w2_view = w2_words.rearrange("e s p b -> e p s b")
+        dy_view = dyT.rearrange("(s p t) c -> s t p c", p=P, t=PACK)
+        a_view = a.rearrange("(p t) c -> p t c", t=PACK)
+        nc.vector.memset(s2_raw[:].rearrange("p q i -> p (q i)").bitcast(I32), 0)
+        nc.vector.memset(s1_sb[:].rearrange("p e k -> p (e k)").bitcast(I32), 0)
+        for q in range(4):
+            nc.sync.dma_start(s2_raw[32 * q : 32 * q + 4, :, :].bitcast(I32), s2_view[4 * q : 4 * q + 4].bitcast(I32))
+        nc.sync.dma_start(offs_sb[:], offs)
+        nc.sync.dma_start(w2_raw[0][:].bitcast(I32), w2_view[0].bitcast(I32))
+        nc.sync.dma_start(gate_sb[:, 0:C], gate[0:P, 0:C])
+        for s in range(N_PASSES):
+            for t in range(PACK):
+                nc.sync.dma_start(planes[s][t][:], dy_view[s, t])
+                if s == 0 and t == 0:
+                    nc.sync.dma_start(gate_sb[:, C:S], gate[0:P, C:S])
+        nc.sync.dma_start(w2_raw[1][:].bitcast(I32), w2_view[1].bitcast(I32))
+        nc.sync.dma_start(a_sb[0][:], a_view[:, :, 0:C])
+        for q in range(4):
+            nc.sync.dma_start(s1_sb[32 * q : 32 * q + 4, :, :].bitcast(I32), s1_view[4 * q : 4 * q + 4].bitcast(I32))
+        nc.sync.dma_start(w1_sb[:].bitcast(I32), w1_words.rearrange("e s p b -> p (e s) b").bitcast(I32))
+        nc.sync.dma_start(a_sb[1][:], a_view[:, :, C : 2 * C])
+
+        for b in range(K_BLOCKS):
+            if b < 1:
+                nc.vector.memset(windows[b][:], 0.0)
+            else:
+                nc.scalar.copy(windows[b][:], windows[0][:])
+
+        def permute_words(e):
+            nc.vector.tensor_copy(
+                w2_sb[e][:].rearrange("p s b -> p (s b)").bitcast(U16).rearrange("p (s t m) -> p s t m", s=N_PASSES, t=PACK),
+                w2_raw[e][:].rearrange("p s b -> p (s b)").bitcast(U16).rearrange("p (s m t) -> p s t m", s=N_PASSES, t=PACK),
+            )
+
+        def permute_scales():
+            nc.vector.tensor_copy(
+                s2_sb[:].rearrange("p q (t m) -> p q t m", t=PACK),
+                s2_raw[:].rearrange("p q (m t) -> p q t m", t=PACK),
+            )
+
+        def quantize(grouped, words, scale_bytes):
+            nc.vector.quantize_mx(out=words[:].bitcast(FP8X4), scales=scale_bytes[:], in_=grouped[:].rearrange("p c t -> p (c t)"))
+
+        def interleave(grouped, rows):
+            nc.scalar.copy(grouped[:].rearrange("p (c i) t -> p c t i", i=4), rows.rearrange("p t (c i) -> p c t i", i=4))
+
+        def gather(s, t, e0, e1, rows):
+            slots = slice(e0 * C, e1 * C)
+            cols = slice(slots.start // 16, slots.stop // 16)
+            nc.vector.tensor_tensor(rows, planes[s][t][:].indirect(offs_sb[:, cols]), gate_sb[:, slots], MULT)
+
+        permute_scales()
+        permute_words(0)
+        gather(0, 0, 0, 1, g0[:, 0, 0:C])
+        gather(0, 0, 1, 2, g0[:, 0, C:S])
+        for t in range(1, JOINT):
+            gather(0, t, 0, 2, g0[:, t, :])
+
+
+        def slot_gradients(e):
+            for t in range(JOINT, PACK):
+                gather(0, t, e, e + 1, g0[:, t, e * C : (e + 1) * C])
+            g1 = keep.tile([P, PACK, C], F32, name=f"g1_{e}")
+            for t in range(PACK):
+                gather(1, t, e, e + 1, g1[:, t, :])
+            gi0 = keep.tile([P, C, PACK], BF16, name=f"gi0_{e}", align_bytes=64)
+            interleave(gi0, g0[:, :, e * C : (e + 1) * C])
+            quantize(gi0, codes[0][e], scales[0][e])
+            gi1 = keep.tile([P, C, PACK], BF16, name=f"gi1_{e}", align_bytes=64)
+            interleave(gi1, g1[:])
+            quantize(gi1, codes[1][e], scales[1][e])
+
+        def first_product(e, t):
+            dh = psum_h.tile([P, C], F32, name="dh")
+            for s in range(N_PASSES):
+                nc.tensor.matmul_mx(
+                    out=dh[:],
+                    lhsT=w2_sb[e][:, s, 256 * t : 256 * (t + 1)].bitcast(FP4X4),
+                    lhsT_scale=s2_sb[:, N_PASSES * e + s, P * t : P * (t + 1)],
+                    rhs=codes[s][e][:].bitcast(FP8X4),
+                    rhs_scale=scales[s][e][:],
+                    start=(s == 0),
+                    stop=(s == N_PASSES - 1),
+                )
+            return dh
+
+        def second_product(e, b, pool):
+            dx = pool.tile([P, C], F32, name="dx" if pool is psum_x else "dh")
+            nc.tensor.matmul_mx(
+                out=dx[:],
+                lhsT=w1_sb[:, e, 256 * b : 256 * (b + 1)].bitcast(FP4X4),
+                lhsT_scale=s1_sb[:, e, P * b : P * (b + 1)],
+                rhs=da_codes[e][:].bitcast(FP8X4),
+                rhs_scale=da_scales[e][:],
+                start=True,
+                stop=True,
+            )
+            x = keep.tile([P, C], F32, name=f"x_{e}_{b}", tag="late" if (e, b) == (0, 5) else f"x_{e}_{b}", align_bytes=64)
+            nc.scalar.copy(x[:], dx[:])
+            x_sb[(e, b)] = x
+
+        da_codes = [keep.tile([P, C], U32, name=f"da_codes_{e}", align_bytes=64) for e in range(E)]
+        da_scales = [keep.tile([P, C], U8, name=f"da_scales_{e}", align_bytes=64) for e in range(E)]
+        dai = [keep.tile([P, C, PACK], BF16, name=f"dai_{e}", align_bytes=64) for e in range(E)]
+        x_sb = {}
+
+        slot_gradients(0)
+        da0 = keep.tile([P, PACK, C], BF16, name="da0", align_bytes=64)
+        for t in range(PACK):
+            dh = first_product(0, t)
+            nc.vector.scalar_tensor_tensor(da0[:, t, :], a_sb[0][:, t, :], 0.0, dh[:], op0=IS_GT, op1=MULT)
+        interleave(dai[0], da0[:])
+        quantize(dai[0], da_codes[0], da_scales[0])
+        for b in range(5):
+            second_product(0, b, psum_x)
+
+        permute_words(1)
+        slot_gradients(1)
+        da1 = keep.tile([P, PACK, C], BF16, name="da1", tag="late", align_bytes=64)
+        for t in range(PACK):
+            dh = first_product(1, t)
+            nc.vector.scalar_tensor_tensor(da1[:, t, :], a_sb[1][:, t, :], 0.0, dh[:], op0=IS_GT, op1=MULT)
+        interleave(dai[1], da1[:])
+        quantize(dai[1], da_codes[1], da_scales[1])
+        second_product(0, 5, psum_x)
+        for b in range(K_BLOCKS):
+            second_product(1, b, psum_x)
+
+        for e in range(E):
+            for b in range(K_BLOCKS):
+                nc.vector.tensor_copy(windows[b][:].indirect(offs_sb[:, 32 * e : 32 * e + 32]), x_sb[(e, b)][:])
+                if e == E - 1:
+                    nc.sync.dma_start(out[P * b : P * (b + 1), :], windows[b][:])

@@ -1,6 +1,7 @@
 from contextlib import ExitStack
 
 import concourse.mybir as mybir
+from concourse.masks import make_identity
 
 K, T, E, C, H, N = 768, 1536, 2, 512, 512, 1024
 S = E * C
@@ -8,7 +9,8 @@ P = 128
 PACK = 4
 N_PASSES = N // (P * PACK)
 K_BLOCKS = K // P
-JOINT = 2
+HALF = C // 2
+HELD = 4
 
 FLOPS = 2 * S * H * (N + K)
 BYTES = 4 * N * T + 4 * H * S + E * (N * H + H * K) // 2 + E * (N * H + H * K) // 32 + 4 * S + 2 * P * S // 16 + 4 * K * T
@@ -32,155 +34,179 @@ def tile_moe_bdx_mlp_relu_kernel(tc, dyT, a, w2_words, w2_scales, w1_words, w1_s
     with ExitStack() as ctx:
         keep = ctx.enter_context(tc.tile_pool(name="keep", bufs=1))
         psum_h = ctx.enter_context(tc.psum_pool(name="psum_h", bufs=4))
-        psum_x = ctx.enter_context(tc.psum_pool(name="psum_x", bufs=4))
+        psum_t = ctx.enter_context(tc.psum_pool(name="psum_t", bufs=2))
+        psum_x = ctx.enter_context(tc.psum_pool(name="psum_x", bufs=2))
 
         offs_sb = keep.tile([P, S // 16], U16, name="offs_sb")
-        gate_sb = keep.tile([P, S], F32, name="gate_sb")
+        arena = keep.tile([P, PACK * 2 * C], F32, name="arena", align_bytes=64)
+        gate_late = keep.tile([P, C], F32, name="gate_late")
+        gate_sb = [arena[:, 0:C], gate_late[:]]
+        late_rows = arena[:].rearrange("p (t c) -> p t c", t=PACK)[:, :, 0:C]
         planes = [[keep.tile([P, T], F32, name=f"dy_{s}_{t}") for t in range(PACK)] for s in range(N_PASSES)]
         a_sb = [keep.tile([P, PACK, C], F32, name=f"a_{e}") for e in range(E)]
-        w2_raw = [keep.tile([P, N_PASSES, 2 * H], U8, name=f"w2_raw_{e}", align_bytes=64) for e in range(E)]
         w2_sb = [keep.tile([P, N_PASSES, 2 * H], U8, name=f"w2_{e}", align_bytes=64) for e in range(E)]
-        s2_raw = keep.tile([P, E * N_PASSES, H], U8, name="s2_raw", align_bytes=64)
         s2_sb = keep.tile([P, E * N_PASSES, H], U8, name="s2_sb", align_bytes=64)
         w1_sb = keep.tile([P, E, 2 * K], U8, name="w1_sb", align_bytes=64)
         s1_sb = keep.tile([P, E, K], U8, name="s1_sb", align_bytes=64)
         windows = [keep.tile([P, T], F32, name=f"window_{b}") for b in range(K_BLOCKS)]
-        g0 = keep.tile([P, PACK, S], F32, name="g0")
-        codes = [[keep.tile([P, C], U32, name=f"codes_{s}_{e}", align_bytes=64) for e in range(E)] for s in range(N_PASSES)]
-        scales = [[keep.tile([P, C], U8, name=f"scales_{s}_{e}", align_bytes=64) for e in range(E)] for s in range(N_PASSES)]
+        identity = keep.tile([P, P], F32, name="identity")
 
         s2_view = w2_scales.rearrange("e s f i -> f (e s) i")
         s1_view = w1_scales.rearrange("e s f k -> f (e s) k")
         w2_view = w2_words.rearrange("e s p b -> e p s b")
         dy_view = dyT.rearrange("(s p t) c -> s t p c", p=P, t=PACK)
         a_view = a.rearrange("(p t) c -> p t c", t=PACK)
-        nc.vector.memset(s2_raw[:].rearrange("p q i -> p (q i)").bitcast(I32), 0)
+        nc.vector.memset(s2_sb[:].rearrange("p q i -> p (q i)").bitcast(I32), 0)
         nc.vector.memset(s1_sb[:].rearrange("p e k -> p (e k)").bitcast(I32), 0)
-        for q in range(4):
-            nc.sync.dma_start(s2_raw[32 * q : 32 * q + 4, :, :].bitcast(I32), s2_view[4 * q : 4 * q + 4].bitcast(I32))
         nc.sync.dma_start(offs_sb[:], offs)
-        nc.sync.dma_start(w2_raw[0][:].bitcast(I32), w2_view[0].bitcast(I32))
-        nc.sync.dma_start(gate_sb[:, 0:C], gate[0:P, 0:C])
+        nc.sync.dma_start(gate_sb[0], gate[0:P, 0:C])
         for s in range(N_PASSES):
             for t in range(PACK):
                 nc.sync.dma_start(planes[s][t][:], dy_view[s, t])
                 if s == 0 and t == 0:
-                    nc.sync.dma_start(gate_sb[:, C:S], gate[0:P, C:S])
-        nc.sync.dma_start(w2_raw[1][:].bitcast(I32), w2_view[1].bitcast(I32))
-        nc.sync.dma_start(a_sb[0][:], a_view[:, :, 0:C])
+                    nc.sync.dma_start(gate_sb[1], gate[0:P, C:S])
+                if s == 0 and t == 2:
+                    nc.sync.dma_start(a_sb[0][:], a_view[:, :, 0:C])
+        nc.sync.dma_start(w2_sb[0][:].bitcast(I32), w2_view[0].bitcast(I32))
+        for q in range(4):
+            nc.sync.dma_start(s2_sb[32 * q : 32 * q + 4, :, :].bitcast(I32), s2_view[4 * q : 4 * q + 4].bitcast(I32))
         for q in range(4):
             nc.sync.dma_start(s1_sb[32 * q : 32 * q + 4, :, :].bitcast(I32), s1_view[4 * q : 4 * q + 4].bitcast(I32))
         nc.sync.dma_start(w1_sb[:].bitcast(I32), w1_words.rearrange("e s p b -> p (e s) b").bitcast(I32))
+        nc.sync.dma_start(w2_sb[1][:].bitcast(I32), w2_view[1].bitcast(I32))
         nc.sync.dma_start(a_sb[1][:], a_view[:, :, C : 2 * C])
 
-        for b in range(K_BLOCKS):
-            if b < 1:
-                nc.vector.memset(windows[b][:], 0.0)
-            else:
-                nc.scalar.copy(windows[b][:], windows[0][:])
+        make_identity(nc, identity[:])
+        nc.vector.memset(windows[K_BLOCKS - 1][:], 0.0)
+        nc.vector.memset(windows[0][:], 0.0)
+        for b in range(1, K_BLOCKS - 1):
+            nc.sync.dma_start(windows[b][:], windows[K_BLOCKS - 1][:])
 
-        def permute_words(e):
-            nc.vector.tensor_copy(
-                w2_sb[e][:].rearrange("p s b -> p (s b)").bitcast(U16).rearrange("p (s t m) -> p s t m", s=N_PASSES, t=PACK),
-                w2_raw[e][:].rearrange("p s b -> p (s b)").bitcast(U16).rearrange("p (s m t) -> p s t m", s=N_PASSES, t=PACK),
-            )
+        def by_four(grouped):
+            return grouped.rearrange("p (c i) t -> p c t i", i=4)
 
-        def permute_scales():
-            nc.vector.tensor_copy(
-                s2_sb[:].rearrange("p q (t m) -> p q t m", t=PACK),
-                s2_raw[:].rearrange("p q (m t) -> p q t m", t=PACK),
-            )
+        def rows_by_four(rows):
+            return rows.rearrange("p t (c i) -> p c t i", i=4)
 
-        def quantize(grouped, words, scale_bytes):
+        def gather(s, t, first, count, rows):
+            cols = slice(first // 16, (first + count) // 16)
+            nc.vector.tensor_tensor(rows, planes[s][t][:].indirect(offs_sb[:, cols]), gate_sb[first // C][:, first % C : first % C + count], MULT)
+
+        def quantize(grouped, label, tag=None):
+            width = grouped.shape[1]
+            words = keep.tile([P, width], U32, name=f"codes_{label}", tag=tag or f"codes_{label}", align_bytes=64)
+            scale_bytes = keep.tile([P, width], U8, name=f"scales_{label}", align_bytes=64)
             nc.vector.quantize_mx(out=words[:].bitcast(FP8X4), scales=scale_bytes[:], in_=grouped[:].rearrange("p c t -> p (c t)"))
+            return words, scale_bytes
 
-        def interleave(grouped, rows):
-            nc.scalar.copy(grouped[:].rearrange("p (c i) t -> p c t i", i=4), rows.rearrange("p t (c i) -> p c t i", i=4))
+        def interleave(rows, label, tag=None):
+            grouped = keep.tile([P, rows.shape[2], PACK], BF16, name=f"gi_{label}", tag=tag or f"gi_{label}", align_bytes=64)
+            nc.scalar.copy(by_four(grouped[:]), rows_by_four(rows))
+            return grouped
 
-        def gather(s, t, e0, e1, rows):
-            slots = slice(e0 * C, e1 * C)
-            cols = slice(slots.start // 16, slots.stop // 16)
-            nc.vector.tensor_tensor(rows, planes[s][t][:].indirect(offs_sb[:, cols]), gate_sb[:, slots], MULT)
-
-        permute_scales()
-        permute_words(0)
-        gather(0, 0, 0, 1, g0[:, 0, 0:C])
-        gather(0, 0, 1, 2, g0[:, 0, C:S])
-        for t in range(1, JOINT):
-            gather(0, t, 0, 2, g0[:, t, :])
-
-
-        def slot_gradients(e):
-            for t in range(JOINT, PACK):
-                gather(0, t, e, e + 1, g0[:, t, e * C : (e + 1) * C])
-            g1 = keep.tile([P, PACK, C], F32, name=f"g1_{e}")
-            for t in range(PACK):
-                gather(1, t, e, e + 1, g1[:, t, :])
-            gi0 = keep.tile([P, C, PACK], BF16, name=f"gi0_{e}", align_bytes=64)
-            interleave(gi0, g0[:, :, e * C : (e + 1) * C])
-            quantize(gi0, codes[0][e], scales[0][e])
-            gi1 = keep.tile([P, C, PACK], BF16, name=f"gi1_{e}", align_bytes=64)
-            interleave(gi1, g1[:])
-            quantize(gi1, codes[1][e], scales[1][e])
-
-        def first_product(e, t):
-            dh = psum_h.tile([P, C], F32, name="dh")
-            for s in range(N_PASSES):
-                nc.tensor.matmul_mx(
-                    out=dh[:],
-                    lhsT=w2_sb[e][:, s, 256 * t : 256 * (t + 1)].bitcast(FP4X4),
-                    lhsT_scale=s2_sb[:, N_PASSES * e + s, P * t : P * (t + 1)],
-                    rhs=codes[s][e][:].bitcast(FP8X4),
-                    rhs_scale=scales[s][e][:],
-                    start=(s == 0),
-                    stop=(s == N_PASSES - 1),
+        def first_product(e, h, operands):
+            turned = psum_t.tile([P, 2, HALF], F32, name="turned")
+            for blk in range(2):
+                dh = psum_h.tile([P, H], F32, name="dh")
+                for s in range(N_PASSES):
+                    words, scale_bytes, first = operands[s]
+                    cols = slice(first + P * blk, first + P * (blk + 1))
+                    nc.tensor.matmul_mx(
+                        out=dh[:],
+                        lhsT=words[:, cols].bitcast(FP8X4),
+                        lhsT_scale=scale_bytes[:, cols],
+                        rhs=w2_sb[e][:, s, :].bitcast(FP4X4),
+                        rhs_scale=s2_sb[:, N_PASSES * e + s, :],
+                        start=(s == 0),
+                        stop=(s == N_PASSES - 1),
+                    )
+                if (e, h, blk) == (0, 0, 1):
+                    rounded = arena[:, 6 * C : 6 * C + H // 2].bitcast(BF16)
+                else:
+                    rounded = keep.tile([P, H], BF16, name=f"rounded_{e}_{h}_{blk}", tag=f"rounded_{e}_{h}_{blk}", align_bytes=64)[:]
+                nc.scalar.copy(
+                    rounded.rearrange("r (u p v) -> r u p v", u=2, v=2),
+                    dh[:].rearrange("r (p u v) -> r u p v", u=2, v=2),
                 )
-            return dh
+                for u in range(2):
+                    nc.tensor.transpose(turned[:, u, P * blk : P * (blk + 1)], rounded.bitcast(F32)[:, P * u : P * (u + 1)], identity[:])
+            return turned
 
-        def second_product(e, b, pool):
-            dx = pool.tile([P, C], F32, name="dx" if pool is psum_x else "dh")
+        def apply_mask(da, mask, h, turned):
+            cols = slice(HALF * h, HALF * (h + 1))
+            nc.vector.tensor_tensor(
+                da[:, cols, :].rearrange("p r (u v) -> p r u v", u=2),
+                turned[:].rearrange("p u r -> p (u r)").bitcast(BF16).rearrange("p (u r v) -> p r u v", u=2, v=2),
+                mask[:, cols, :].rearrange("p r (u v) -> p r u v", u=2),
+                MULT,
+            )
+
+        x_sb = {}
+
+        def make_mask(e, tag):
+            signs = keep.tile([P, C, PACK], BF16, name=f"signs_{e}", tag=tag, align_bytes=64)
+            nc.scalar.activation(by_four(signs[:]), rows_by_four(a_sb[e][:]), SIGN)
+            mask = keep.tile([P, C, PACK], BF16, name=f"mask_{e}", tag=f"mask_{e}", align_bytes=64)
+            nc.scalar.activation(mask[:].rearrange("p c t -> p (c t)"), signs[:].rearrange("p c t -> p (c t)"), RELU)
+            return mask
+
+        def second_product(e, b, da_q, tag):
+            dx = psum_x.tile([P, C], F32, name="dx")
             nc.tensor.matmul_mx(
                 out=dx[:],
                 lhsT=w1_sb[:, e, 256 * b : 256 * (b + 1)].bitcast(FP4X4),
                 lhsT_scale=s1_sb[:, e, P * b : P * (b + 1)],
-                rhs=da_codes[e][:].bitcast(FP8X4),
-                rhs_scale=da_scales[e][:],
+                rhs=da_q[0][:].bitcast(FP8X4),
+                rhs_scale=da_q[1][:],
                 start=True,
                 stop=True,
             )
-            x = keep.tile([P, C], F32, name=f"x_{e}_{b}", tag="late" if (e, b) == (0, 5) else f"x_{e}_{b}", align_bytes=64)
-            nc.scalar.copy(x[:], dx[:])
+            x = arena[:, 0:C] if tag is None else keep.tile([P, C], F32, name=f"x_{e}_{b}", tag=tag, align_bytes=64)[:]
+            nc.scalar.copy(x, dx[:])
             x_sb[(e, b)] = x
 
-        da_codes = [keep.tile([P, C], U32, name=f"da_codes_{e}", align_bytes=64) for e in range(E)]
-        da_scales = [keep.tile([P, C], U8, name=f"da_scales_{e}", align_bytes=64) for e in range(E)]
-        dai = [keep.tile([P, C, PACK], BF16, name=f"dai_{e}", align_bytes=64) for e in range(E)]
-        x_sb = {}
+        def scatter(e, b):
+            nc.vector.tensor_copy(windows[b][:].indirect(offs_sb[:, 32 * e : 32 * e + 32]), x_sb[(e, b)])
 
-        slot_gradients(0)
-        da0 = keep.tile([P, PACK, C], BF16, name="da0", align_bytes=64)
+        g0 = [keep.tile([P, PACK, C], F32, name=f"g0_{e}") for e in range(E)]
         for t in range(PACK):
-            dh = first_product(0, t)
-            nc.vector.scalar_tensor_tensor(da0[:, t, :], a_sb[0][:, t, :], 0.0, dh[:], op0=IS_GT, op1=MULT)
-        interleave(dai[0], da0[:])
-        quantize(dai[0], da_codes[0], da_scales[0])
-        for b in range(5):
-            second_product(0, b, psum_x)
+            for e in range(E):
+                gather(0, t, e * C, C, g0[e][:, t, :])
+        mask0 = make_mask(0, "signs_0")
+        q00 = quantize(interleave(g0[0][:], "0_0"), "0_0")
 
-        permute_words(1)
-        slot_gradients(1)
-        da1 = keep.tile([P, PACK, C], BF16, name="da1", tag="late", align_bytes=64)
+        g1 = [arena[:, 2 * C * (h + 1) : 2 * C * (h + 2)].rearrange("p (t c) -> p t c", t=PACK) for h in range(2)]
         for t in range(PACK):
-            dh = first_product(1, t)
-            nc.vector.scalar_tensor_tensor(da1[:, t, :], a_sb[1][:, t, :], 0.0, dh[:], op0=IS_GT, op1=MULT)
-        interleave(dai[1], da1[:])
-        quantize(dai[1], da_codes[1], da_scales[1])
-        second_product(0, 5, psum_x)
+            for h in range(2):
+                gather(1, t, HALF * h, HALF, g1[h][:, t, :])
+        da0 = keep.tile([P, C, PACK], BF16, name="da0", align_bytes=64)
+        turned0 = []
+        for h in range(2):
+            q1 = quantize(interleave(g1[h], f"1_0_{h}"), f"1_0_{h}")
+            turned0.append(first_product(0, h, [(q00[0], q00[1], HALF * h), (q1[0], q1[1], 0)]))
+        for h in range(2):
+            apply_mask(da0, mask0, h, turned0[h])
+        da0_q = quantize(da0, "da0")
+        q01 = quantize(interleave(g0[1][:], "0_1", tag="rounded_0_1_1"), "0_1")
+        second_product(0, 0, da0_q, "after_first")
+        scatter(0, 0)
+
+        for t in range(PACK):
+            gather(1, t, C, C, late_rows[:, t, :])
+        q11 = [quantize(interleave(late_rows[:, :, HALF * h : HALF * (h + 1)], f"1_1_{h}"), f"1_1_{h}") for h in range(2)]
+        for b in range(1, HELD):
+            second_product(0, b, da0_q, None if b == 1 else f"x_0_{b}")
+            scatter(0, b)
+        turned1 = [first_product(1, h, [(q01[0], q01[1], HALF * h), (q11[h][0], q11[h][1], 0)]) for h in range(2)]
+        mask1 = make_mask(1, "after_first")
+        da1 = keep.tile([P, C, PACK], BF16, name="da1", align_bytes=64)
+        for h in range(2):
+            apply_mask(da1, mask1, h, turned1[h])
+        da1_q = quantize(da1, "da1")
+        for b in range(HELD, K_BLOCKS):
+            second_product(0, b, da0_q, "after_first" if b == HELD else "mask_1")
+            scatter(0, b)
         for b in range(K_BLOCKS):
-            second_product(1, b, psum_x)
-
-        for e in range(E):
-            for b in range(K_BLOCKS):
-                nc.vector.tensor_copy(windows[b][:].indirect(offs_sb[:, 32 * e : 32 * e + 32]), x_sb[(e, b)][:])
-                if e == E - 1:
-                    nc.sync.dma_start(out[P * b : P * (b + 1), :], windows[b][:])
+            second_product(1, b, da1_q, f"x_1_{b}")
+            scatter(1, b)
+            nc.sync.dma_start(out[P * b : P * (b + 1), :], windows[b][:])

@@ -38,10 +38,10 @@ def tile_moe_bdx_mlp_relu_kernel(tc, dyT, a, w2_words, w2_scales, w1_words, w1_s
         psum_x = ctx.enter_context(tc.psum_pool(name="psum_x", bufs=2))
 
         offs_sb = keep.tile([P, S // 16], U16, name="offs_sb")
-        arena = keep.tile([P, PACK * 2 * C], F32, name="arena", align_bytes=64)
+        arena = keep.tile([P, PACK * 2 * C + HALF], F32, name="arena", align_bytes=64)
         gate_late = keep.tile([P, C], F32, name="gate_late")
         gate_sb = [arena[:, 0:C], gate_late[:]]
-        late_rows = arena[:].rearrange("p (t c) -> p t c", t=PACK)[:, :, 0:C]
+        late_rows = arena[:, 0 : PACK * 2 * C].rearrange("p (t c) -> p t c", t=PACK)[:, :, 0:C]
         planes = [[keep.tile([P, T], F32, name=f"dy_{s}_{t}") for t in range(PACK)] for s in range(N_PASSES)]
         a_sb = [keep.tile([P, PACK, C], F32, name=f"a_{e}") for e in range(E)]
         w2_sb = [keep.tile([P, N_PASSES, 2 * H], U8, name=f"w2_{e}", align_bytes=64) for e in range(E)]
@@ -59,17 +59,17 @@ def tile_moe_bdx_mlp_relu_kernel(tc, dyT, a, w2_words, w2_scales, w1_words, w1_s
         nc.vector.memset(s2_sb[:].rearrange("p q i -> p (q i)").bitcast(I32), 0)
         nc.vector.memset(s1_sb[:].rearrange("p e k -> p (e k)").bitcast(I32), 0)
         nc.sync.dma_start(offs_sb[:], offs)
-        nc.sync.dma_start(gate_sb[0], gate[0:P, 0:C])
+        nc.sync.dma_start(gate_sb[0][:, 0:HALF], gate[0:P, 0:HALF])
         for s in range(N_PASSES):
             for t in range(PACK):
                 nc.sync.dma_start(planes[s][t][:], dy_view[s, t])
                 if s == 0 and t == 0:
+                    nc.sync.dma_start(gate_sb[0][:, HALF:C], gate[0:P, HALF:C])
                     nc.sync.dma_start(gate_sb[1], gate[0:P, C:S])
-                if s == 0 and t == 2:
-                    nc.sync.dma_start(a_sb[0][:], a_view[:, :, 0:C])
         nc.sync.dma_start(w2_sb[0][:].bitcast(I32), w2_view[0].bitcast(I32))
         for q in range(4):
             nc.sync.dma_start(s2_sb[32 * q : 32 * q + 4, :, :].bitcast(I32), s2_view[4 * q : 4 * q + 4].bitcast(I32))
+        nc.sync.dma_start(a_sb[0][:], a_view[:, :, 0:C])
         for q in range(4):
             nc.sync.dma_start(s1_sb[32 * q : 32 * q + 4, :, :].bitcast(I32), s1_view[4 * q : 4 * q + 4].bitcast(I32))
         nc.sync.dma_start(w1_sb[:].bitcast(I32), w1_words.rearrange("e s p b -> p (e s) b").bitcast(I32))
@@ -77,10 +77,9 @@ def tile_moe_bdx_mlp_relu_kernel(tc, dyT, a, w2_words, w2_scales, w1_words, w1_s
         nc.sync.dma_start(a_sb[1][:], a_view[:, :, C : 2 * C])
 
         make_identity(nc, identity[:])
-        nc.vector.memset(windows[K_BLOCKS - 1][:], 0.0)
         nc.vector.memset(windows[0][:], 0.0)
-        for b in range(1, K_BLOCKS - 1):
-            nc.sync.dma_start(windows[b][:], windows[K_BLOCKS - 1][:])
+        for b in range(1, K_BLOCKS):
+            nc.scalar.copy(windows[b][:], windows[0][:])
 
         def by_four(grouped):
             return grouped.rearrange("p (c i) t -> p c t i", i=4)
@@ -96,13 +95,13 @@ def tile_moe_bdx_mlp_relu_kernel(tc, dyT, a, w2_words, w2_scales, w1_words, w1_s
             width = grouped.shape[1]
             words = keep.tile([P, width], U32, name=f"codes_{label}", tag=tag or f"codes_{label}", align_bytes=64)
             scale_bytes = keep.tile([P, width], U8, name=f"scales_{label}", align_bytes=64)
-            nc.vector.quantize_mx(out=words[:].bitcast(FP8X4), scales=scale_bytes[:], in_=grouped[:].rearrange("p c t -> p (c t)"))
+            nc.vector.quantize_mx(out=words[:].bitcast(FP8X4), scales=scale_bytes[:], in_=grouped.rearrange("p c t -> p (c t)"))
             return words, scale_bytes
 
         def interleave(rows, label, tag=None):
             grouped = keep.tile([P, rows.shape[2], PACK], BF16, name=f"gi_{label}", tag=tag or f"gi_{label}", align_bytes=64)
             nc.scalar.copy(by_four(grouped[:]), rows_by_four(rows))
-            return grouped
+            return grouped[:]
 
         def first_product(e, h, operands):
             turned = psum_t.tile([P, 2, HALF], F32, name="turned")
@@ -120,8 +119,8 @@ def tile_moe_bdx_mlp_relu_kernel(tc, dyT, a, w2_words, w2_scales, w1_words, w1_s
                         start=(s == 0),
                         stop=(s == N_PASSES - 1),
                     )
-                if (e, h, blk) == (0, 0, 1):
-                    rounded = arena[:, 6 * C : 6 * C + H // 2].bitcast(BF16)
+                if (e, blk) == (0, 1):
+                    rounded = arena[:, 2 * C * (2 + h) : 2 * C * (2 + h) + H // 2].bitcast(BF16)
                 else:
                     rounded = keep.tile([P, H], BF16, name=f"rounded_{e}_{h}_{blk}", tag=f"rounded_{e}_{h}_{blk}", align_bytes=64)[:]
                 nc.scalar.copy(
@@ -169,30 +168,37 @@ def tile_moe_bdx_mlp_relu_kernel(tc, dyT, a, w2_words, w2_scales, w1_words, w1_s
             nc.vector.tensor_copy(windows[b][:].indirect(offs_sb[:, 32 * e : 32 * e + 32]), x_sb[(e, b)])
 
         g0 = [keep.tile([P, PACK, C], F32, name=f"g0_{e}") for e in range(E)]
+        for h in range(2):
+            gather(0, 0, HALF * h, HALF, g0[0][:, 0, HALF * h : HALF * (h + 1)])
         for t in range(PACK):
             for e in range(E):
-                gather(0, t, e * C, C, g0[e][:, t, :])
-        mask0 = make_mask(0, "signs_0")
-        q00 = quantize(interleave(g0[0][:], "0_0"), "0_0")
+                if (t, e) != (0, 0):
+                    gather(0, t, e * C, C, g0[e][:, t, :])
+        q00 = [quantize(interleave(g0[0][:, :, HALF * h : HALF * (h + 1)], f"0_0_{h}"), f"0_0_{h}") for h in range(2)]
 
-        g1 = [arena[:, 2 * C * (h + 1) : 2 * C * (h + 2)].rearrange("p (t c) -> p t c", t=PACK) for h in range(2)]
+        g1_second = keep.tile([P, PACK, HALF], F32, name="g1_second")
+        g1 = [arena[:, 2 * C : 4 * C].rearrange("p (t c) -> p t c", t=PACK), g1_second[:]]
         for t in range(PACK):
             for h in range(2):
                 gather(1, t, HALF * h, HALF, g1[h][:, t, :])
-        da0 = keep.tile([P, C, PACK], BF16, name="da0", align_bytes=64)
+        da0 = arena[:, 6 * C + HALF : 8 * C + HALF].bitcast(BF16).rearrange("p (c t) -> p c t", t=PACK)
+        mask0 = keep.tile([P, C, PACK], BF16, name="mask_0", align_bytes=64)
         turned0 = []
         for h in range(2):
             q1 = quantize(interleave(g1[h], f"1_0_{h}"), f"1_0_{h}")
-            turned0.append(first_product(0, h, [(q00[0], q00[1], HALF * h), (q1[0], q1[1], 0)]))
+            turned0.append(first_product(0, h, [(q00[h][0], q00[h][1], 0), (q1[0], q1[1], 0)]))
+        nc.vector.tensor_single_scalar(by_four(mask0[:]), rows_by_four(a_sb[0][:]), 0.0, IS_GT)
         for h in range(2):
             apply_mask(da0, mask0, h, turned0[h])
         da0_q = quantize(da0, "da0")
-        q01 = quantize(interleave(g0[1][:], "0_1", tag="rounded_0_1_1"), "0_1")
+        q01 = quantize(interleave(g0[1][:], "0_1", tag="rounded_0_1_0"), "0_1")
         second_product(0, 0, da0_q, "after_first")
         scatter(0, 0)
 
-        for t in range(PACK):
+        for t in range(PACK - 1):
             gather(1, t, C, C, late_rows[:, t, :])
+        for h in range(2):
+            gather(1, PACK - 1, C + HALF * h, HALF, late_rows[:, PACK - 1, HALF * h : HALF * (h + 1)])
         q11 = [quantize(interleave(late_rows[:, :, HALF * h : HALF * (h + 1)], f"1_1_{h}"), f"1_1_{h}") for h in range(2)]
         for b in range(1, HELD):
             second_product(0, b, da0_q, None if b == 1 else f"x_0_{b}")
@@ -202,7 +208,7 @@ def tile_moe_bdx_mlp_relu_kernel(tc, dyT, a, w2_words, w2_scales, w1_words, w1_s
         da1 = keep.tile([P, C, PACK], BF16, name="da1", align_bytes=64)
         for h in range(2):
             apply_mask(da1, mask1, h, turned1[h])
-        da1_q = quantize(da1, "da1")
+        da1_q = quantize(da1[:], "da1")
         for b in range(HELD, K_BLOCKS):
             second_product(0, b, da0_q, "after_first" if b == HELD else "mask_1")
             scatter(0, b)

@@ -11,6 +11,7 @@ N_PASSES = N // (P * PACK)
 K_BLOCKS = K // P
 HALF = C // 2
 HELD = 4
+SLOT = 3 * C
 
 FLOPS = 2 * S * H * (N + K)
 BYTES = 4 * N * T + 4 * H * S + E * (N * H + H * K) // 2 + E * (N * H + H * K) // 32 + 4 * S + 2 * P * S // 16 + 4 * K * T
@@ -38,12 +39,13 @@ def tile_moe_bdx_mlp_relu_kernel(tc, dyT, a, w2_words, w2_scales, w1_words, w1_s
         psum_x = ctx.enter_context(tc.psum_pool(name="psum_x", bufs=2))
 
         offs_sb = keep.tile([P, S // 16], U16, name="offs_sb")
-        arena = keep.tile([P, PACK * 2 * C + HALF], F32, name="arena", align_bytes=64)
+        arena = keep.tile([P, PACK * SLOT], F32, name="arena", align_bytes=64)
         gate_late = keep.tile([P, C], F32, name="gate_late")
         gate_sb = [arena[:, 0:C], gate_late[:]]
-        late_rows = arena[:, 0 : PACK * 2 * C].rearrange("p (t c) -> p t c", t=PACK)[:, :, 0:C]
+        late_rows = arena[:].rearrange("p (t c) -> p t c", t=PACK)[:, :, 0:C]
         planes = [[keep.tile([P, T], F32, name=f"dy_{s}_{t}") for t in range(PACK)] for s in range(N_PASSES)]
-        a_sb = [keep.tile([P, PACK, C], F32, name=f"a_{e}") for e in range(E)]
+        a_first = [keep.tile([P, PACK, HALF], F32, name=f"a_0_{h}") for h in range(2)]
+        a_late = keep.tile([P, PACK, C], F32, name="a_1")
         w2_sb = [keep.tile([P, N_PASSES, 2 * H], U8, name=f"w2_{e}", align_bytes=64) for e in range(E)]
         s2_sb = keep.tile([P, E * N_PASSES, H], U8, name="s2_sb", align_bytes=64)
         w1_sb = keep.tile([P, E, 2 * K], U8, name="w1_sb", align_bytes=64)
@@ -58,6 +60,12 @@ def tile_moe_bdx_mlp_relu_kernel(tc, dyT, a, w2_words, w2_scales, w1_words, w1_s
         a_view = a.rearrange("(p t) c -> p t c", t=PACK)
         nc.vector.memset(s2_sb[:].rearrange("p q i -> p (q i)").bitcast(I32), 0)
         nc.vector.memset(s1_sb[:].rearrange("p e k -> p (e k)").bitcast(I32), 0)
+
+        def load_s2(e):
+            passes = slice(N_PASSES * e, N_PASSES * (e + 1))
+            for q in range(4):
+                nc.sync.dma_start(s2_sb[32 * q : 32 * q + 4, passes, :].bitcast(I32), s2_view[4 * q : 4 * q + 4, passes].bitcast(I32))
+
         nc.sync.dma_start(offs_sb[:], offs)
         nc.sync.dma_start(gate_sb[0][:, 0:HALF], gate[0:P, 0:HALF])
         for s in range(N_PASSES):
@@ -67,19 +75,20 @@ def tile_moe_bdx_mlp_relu_kernel(tc, dyT, a, w2_words, w2_scales, w1_words, w1_s
                     nc.sync.dma_start(gate_sb[0][:, HALF:C], gate[0:P, HALF:C])
                     nc.sync.dma_start(gate_sb[1], gate[0:P, C:S])
         nc.sync.dma_start(w2_sb[0][:].bitcast(I32), w2_view[0].bitcast(I32))
-        for q in range(4):
-            nc.sync.dma_start(s2_sb[32 * q : 32 * q + 4, :, :].bitcast(I32), s2_view[4 * q : 4 * q + 4].bitcast(I32))
-        nc.sync.dma_start(a_sb[0][:], a_view[:, :, 0:C])
+        load_s2(0)
+        for h in range(2):
+            nc.sync.dma_start(a_first[h][:], a_view[:, :, HALF * h : HALF * (h + 1)])
         for q in range(4):
             nc.sync.dma_start(s1_sb[32 * q : 32 * q + 4, :, :].bitcast(I32), s1_view[4 * q : 4 * q + 4].bitcast(I32))
         nc.sync.dma_start(w1_sb[:].bitcast(I32), w1_words.rearrange("e s p b -> p (e s) b").bitcast(I32))
         nc.sync.dma_start(w2_sb[1][:].bitcast(I32), w2_view[1].bitcast(I32))
-        nc.sync.dma_start(a_sb[1][:], a_view[:, :, C : 2 * C])
+        load_s2(1)
+        nc.sync.dma_start(a_late[:], a_view[:, :, C : 2 * C])
 
         make_identity(nc, identity[:])
         nc.vector.memset(windows[0][:], 0.0)
         for b in range(1, K_BLOCKS):
-            nc.scalar.copy(windows[b][:], windows[0][:])
+            nc.scalar.activation(windows[b][:], windows[0][:], SIGN)
 
         def by_four(grouped):
             return grouped.rearrange("p (c i) t -> p c t i", i=4)
@@ -119,8 +128,8 @@ def tile_moe_bdx_mlp_relu_kernel(tc, dyT, a, w2_words, w2_scales, w1_words, w1_s
                         start=(s == 0),
                         stop=(s == N_PASSES - 1),
                     )
-                if (e, blk) == (0, 1):
-                    rounded = arena[:, 2 * C * (2 + h) : 2 * C * (2 + h) + H // 2].bitcast(BF16)
+                if (e, h, blk) == (0, 1, 1):
+                    rounded = arena[:, 3 * SLOT : 3 * SLOT + H // 2].bitcast(BF16)
                 else:
                     rounded = keep.tile([P, H], BF16, name=f"rounded_{e}_{h}_{blk}", tag=f"rounded_{e}_{h}_{blk}", align_bytes=64)[:]
                 nc.scalar.copy(
@@ -136,20 +145,18 @@ def tile_moe_bdx_mlp_relu_kernel(tc, dyT, a, w2_words, w2_scales, w1_words, w1_s
             nc.vector.tensor_tensor(
                 da[:, cols, :].rearrange("p r (u v) -> p r u v", u=2),
                 turned[:].rearrange("p u r -> p (u r)").bitcast(BF16).rearrange("p (u r v) -> p r u v", u=2, v=2),
-                mask[:, cols, :].rearrange("p r (u v) -> p r u v", u=2),
+                mask.rearrange("p r (u v) -> p r u v", u=2),
                 MULT,
             )
 
-        x_sb = {}
-
         def make_mask(e, tag):
             signs = keep.tile([P, C, PACK], BF16, name=f"signs_{e}", tag=tag, align_bytes=64)
-            nc.scalar.activation(by_four(signs[:]), rows_by_four(a_sb[e][:]), SIGN)
+            nc.scalar.activation(by_four(signs[:]), rows_by_four(a_late[:]), SIGN)
             mask = keep.tile([P, C, PACK], BF16, name=f"mask_{e}", tag=f"mask_{e}", align_bytes=64)
             nc.scalar.activation(mask[:].rearrange("p c t -> p (c t)"), signs[:].rearrange("p c t -> p (c t)"), RELU)
             return mask
 
-        def second_product(e, b, da_q, tag):
+        def second_product(e, b, da_q):
             dx = psum_x.tile([P, C], F32, name="dx")
             nc.tensor.matmul_mx(
                 out=dx[:],
@@ -160,12 +167,13 @@ def tile_moe_bdx_mlp_relu_kernel(tc, dyT, a, w2_words, w2_scales, w1_words, w1_s
                 start=True,
                 stop=True,
             )
-            x = arena[:, 0:C] if tag is None else keep.tile([P, C], F32, name=f"x_{e}_{b}", tag=tag, align_bytes=64)[:]
-            nc.scalar.copy(x, dx[:])
-            x_sb[(e, b)] = x
+            return dx
 
-        def scatter(e, b):
-            nc.vector.tensor_copy(windows[b][:].indirect(offs_sb[:, 32 * e : 32 * e + 32]), x_sb[(e, b)])
+        def copy_scatter(e, b, dx, first, count, tag):
+            x = arena[:, 0:C] if tag is None else keep.tile([P, count], F32, name=f"x_{e}_{b}_{first}", tag=tag, align_bytes=64)[:]
+            nc.scalar.copy(x, dx[:, first : first + count])
+            cols = slice((C * e + first) // 16, (C * e + first + count) // 16)
+            nc.vector.tensor_copy(windows[b][:].indirect(offs_sb[:, cols]), x)
 
         g0 = [keep.tile([P, PACK, C], F32, name=f"g0_{e}") for e in range(E)]
         for h in range(2):
@@ -176,43 +184,45 @@ def tile_moe_bdx_mlp_relu_kernel(tc, dyT, a, w2_words, w2_scales, w1_words, w1_s
                     gather(0, t, e * C, C, g0[e][:, t, :])
         q00 = [quantize(interleave(g0[0][:, :, HALF * h : HALF * (h + 1)], f"0_0_{h}"), f"0_0_{h}") for h in range(2)]
 
-        g1_second = keep.tile([P, PACK, HALF], F32, name="g1_second")
-        g1 = [arena[:, 2 * C : 4 * C].rearrange("p (t c) -> p t c", t=PACK), g1_second[:]]
+        g1 = [arena[:, first : first + 2 * C].rearrange("p (t c) -> p t c", t=PACK) for first in (SLOT, 2 * SLOT + HALF)]
         for t in range(PACK):
             for h in range(2):
                 gather(1, t, HALF * h, HALF, g1[h][:, t, :])
-        da0 = arena[:, 6 * C + HALF : 8 * C + HALF].bitcast(BF16).rearrange("p (c t) -> p c t", t=PACK)
-        mask0 = keep.tile([P, C, PACK], BF16, name="mask_0", align_bytes=64)
-        turned0 = []
-        for h in range(2):
-            q1 = quantize(interleave(g1[h], f"1_0_{h}"), f"1_0_{h}")
-            turned0.append(first_product(0, h, [(q00[h][0], q00[h][1], 0), (q1[0], q1[1], 0)]))
-        nc.vector.tensor_single_scalar(by_four(mask0[:]), rows_by_four(a_sb[0][:]), 0.0, IS_GT)
-        for h in range(2):
-            apply_mask(da0, mask0, h, turned0[h])
-        da0_q = quantize(da0, "da0")
-        q01 = quantize(interleave(g0[1][:], "0_1", tag="rounded_0_1_0"), "0_1")
-        second_product(0, 0, da0_q, "after_first")
-        scatter(0, 0)
+        da0 = arena[:, 3 * SLOT + HALF : 3 * SLOT + HALF + 2 * C].bitcast(BF16).rearrange("p (c t) -> p c t", t=PACK)
+        mask0 = arena[:, 2 * SLOT + C : 3 * SLOT].bitcast(BF16).rearrange("p (c t) -> p c t", t=PACK)
 
-        for t in range(PACK - 1):
-            gather(1, t, C, C, late_rows[:, t, :])
+        def mask_on_vector(h):
+            nc.vector.tensor_single_scalar(by_four(mask0[:, HALF * h : HALF * (h + 1), :]), rows_by_four(a_first[h][:]), 0.0, IS_GT)
+
+        gather(1, 0, C, C, late_rows[:, 0, :])
+        q10 = [quantize(interleave(g1[0], "1_0_0"), "1_0_0")]
+        gather(1, 1, C, C, late_rows[:, 1, :])
+        q10.append(quantize(interleave(g1[1], "1_0_1"), "1_0_1"))
+        mask_on_vector(0)
+        gather(1, 2, C, C, late_rows[:, 2, :])
+        mask_on_vector(1)
         for h in range(2):
-            gather(1, PACK - 1, C + HALF * h, HALF, late_rows[:, PACK - 1, HALF * h : HALF * (h + 1)])
+            turned = first_product(0, h, [(q00[h][0], q00[h][1], 0), (q10[h][0], q10[h][1], 0)])
+            apply_mask(da0, mask0[:, HALF * h : HALF * (h + 1), :], h, turned)
+        gather(1, PACK - 1, C, HALF, late_rows[:, PACK - 1, 0:HALF])
+        da0_q = quantize(da0, "da0")
+        gather(1, PACK - 1, C + HALF, HALF, late_rows[:, PACK - 1, HALF:C])
+        q01 = quantize(interleave(g0[1][:], "0_1", tag="rounded_0_1_0"), "0_1")
+        copy_scatter(0, 0, second_product(0, 0, da0_q), 0, C, "after_first")
+
         q11 = [quantize(interleave(late_rows[:, :, HALF * h : HALF * (h + 1)], f"1_1_{h}"), f"1_1_{h}") for h in range(2)]
         for b in range(1, HELD):
-            second_product(0, b, da0_q, None if b == 1 else f"x_0_{b}")
-            scatter(0, b)
+            copy_scatter(0, b, second_product(0, b, da0_q), 0, C, None if b == 1 else f"x_0_{b}")
+        dx_held = second_product(0, HELD, da0_q)
+        copy_scatter(0, HELD, dx_held, 0, HALF, "x_held")
         turned1 = [first_product(1, h, [(q01[0], q01[1], HALF * h), (q11[h][0], q11[h][1], 0)]) for h in range(2)]
         mask1 = make_mask(1, "after_first")
         da1 = keep.tile([P, C, PACK], BF16, name="da1", align_bytes=64)
         for h in range(2):
-            apply_mask(da1, mask1, h, turned1[h])
+            apply_mask(da1, mask1[:, HALF * h : HALF * (h + 1), :], h, turned1[h])
+        copy_scatter(0, HELD, dx_held, HALF, HALF, "after_first")
         da1_q = quantize(da1[:], "da1")
-        for b in range(HELD, K_BLOCKS):
-            second_product(0, b, da0_q, "after_first" if b == HELD else "mask_1")
-            scatter(0, b)
+        copy_scatter(0, HELD + 1, second_product(0, HELD + 1, da0_q), 0, C, "mask_1")
         for b in range(K_BLOCKS):
-            second_product(1, b, da1_q, f"x_1_{b}")
-            scatter(1, b)
+            copy_scatter(1, b, second_product(1, b, da1_q), 0, C, f"x_1_{b}")
             nc.sync.dma_start(out[P * b : P * (b + 1), :], windows[b][:])

@@ -40,13 +40,12 @@ def tile_moe_bdx_mlp_relu_kernel(tc, dyT, a, w2_words, w2_scales, w1_words, w1_s
 
         offs_sb = keep.tile([P, S // 16], U16, name="offs_sb")
         arena = keep.tile([P, PACK * SLOT], F32, name="arena", align_bytes=64)
-        gate_late = keep.tile([P, C], F32, name="gate_late")
-        gate_sb = [arena[:, 0:C], gate_late[:]]
+        gate_sb = arena[:, HALF : HALF + S]
         late_rows = arena[:].rearrange("p (t c) -> p t c", t=PACK)[:, :, 0:C]
         planes = [[keep.tile([P, T], F32, name=f"dy_{s}_{t}") for t in range(PACK)] for s in range(N_PASSES)]
         a_first = [keep.tile([P, PACK, HALF], F32, name=f"a_0_{h}") for h in range(2)]
         a_late = keep.tile([P, PACK, C], F32, name="a_1")
-        w2_sb = [keep.tile([P, N_PASSES, 2 * H], U8, name=f"w2_{e}", align_bytes=64) for e in range(E)]
+        w2_sb = [[keep.tile([P, 2 * H], U8, name=f"w2_{e}_{s}", align_bytes=64) for s in range(N_PASSES)] for e in range(E)]
         s2_sb = keep.tile([P, E * N_PASSES, H], U8, name="s2_sb", align_bytes=64)
         w1_sb = keep.tile([P, E, 2 * K], U8, name="w1_sb", align_bytes=64)
         s1_sb = keep.tile([P, E, K], U8, name="s1_sb", align_bytes=64)
@@ -55,9 +54,9 @@ def tile_moe_bdx_mlp_relu_kernel(tc, dyT, a, w2_words, w2_scales, w1_words, w1_s
 
         s2_view = w2_scales.rearrange("e s f i -> f (e s) i")
         s1_view = w1_scales.rearrange("e s f k -> f (e s) k")
-        w2_view = w2_words.rearrange("e s p b -> e p s b")
         dy_view = dyT.rearrange("(s p t) c -> s t p c", p=P, t=PACK)
         a_view = a.rearrange("(p t) c -> p t c", t=PACK)
+        nc.vector.memset(windows[0][:], 0.0)
         nc.vector.memset(s2_sb[:].rearrange("p q i -> p (q i)").bitcast(I32), 0)
         nc.vector.memset(s1_sb[:].rearrange("p e k -> p (e k)").bitcast(I32), 0)
 
@@ -67,26 +66,27 @@ def tile_moe_bdx_mlp_relu_kernel(tc, dyT, a, w2_words, w2_scales, w1_words, w1_s
                 nc.sync.dma_start(s2_sb[32 * q : 32 * q + 4, passes, :].bitcast(I32), s2_view[4 * q : 4 * q + 4, passes].bitcast(I32))
 
         nc.sync.dma_start(offs_sb[:], offs)
-        nc.sync.dma_start(gate_sb[0][:, 0:HALF], gate[0:P, 0:HALF])
+        nc.sync.dma_start(gate_sb[:, 0:HALF], gate[0:P, 0:HALF])
         for s in range(N_PASSES):
             for t in range(PACK):
                 nc.sync.dma_start(planes[s][t][:], dy_view[s, t])
                 if s == 0 and t == 0:
-                    nc.sync.dma_start(gate_sb[0][:, HALF:C], gate[0:P, HALF:C])
-                    nc.sync.dma_start(gate_sb[1], gate[0:P, C:S])
-        nc.sync.dma_start(w2_sb[0][:].bitcast(I32), w2_view[0].bitcast(I32))
-        load_s2(0)
-        for h in range(2):
-            nc.sync.dma_start(a_first[h][:], a_view[:, :, HALF * h : HALF * (h + 1)])
+                    nc.sync.dma_start(gate_sb[:, HALF:S], gate[0:P, HALF:S])
+                if (s, t) == (1, 2):
+                    nc.sync.dma_start(w2_sb[0][0][:].bitcast(I32), w2_words[0, 0].bitcast(I32))
+                    load_s2(0)
+                if (s, t) in ((0, 2), (1, 0)):
+                    nc.sync.dma_start(a_first[s][:], a_view[:, :, HALF * s : HALF * (s + 1)])
+        nc.sync.dma_start(w2_sb[0][1][:].bitcast(I32), w2_words[0, 1].bitcast(I32))
         for q in range(4):
             nc.sync.dma_start(s1_sb[32 * q : 32 * q + 4, :, :].bitcast(I32), s1_view[4 * q : 4 * q + 4].bitcast(I32))
         nc.sync.dma_start(w1_sb[:].bitcast(I32), w1_words.rearrange("e s p b -> p (e s) b").bitcast(I32))
-        nc.sync.dma_start(w2_sb[1][:].bitcast(I32), w2_view[1].bitcast(I32))
+        for s in range(N_PASSES):
+            nc.sync.dma_start(w2_sb[1][s][:].bitcast(I32), w2_words[1, s].bitcast(I32))
         load_s2(1)
         nc.sync.dma_start(a_late[:], a_view[:, :, C : 2 * C])
 
         make_identity(nc, identity[:])
-        nc.vector.memset(windows[0][:], 0.0)
         for b in range(1, K_BLOCKS):
             nc.scalar.activation(windows[b][:], windows[0][:], SIGN)
 
@@ -98,7 +98,7 @@ def tile_moe_bdx_mlp_relu_kernel(tc, dyT, a, w2_words, w2_scales, w1_words, w1_s
 
         def gather(s, t, first, count, rows):
             cols = slice(first // 16, (first + count) // 16)
-            nc.vector.tensor_tensor(rows, planes[s][t][:].indirect(offs_sb[:, cols]), gate_sb[first // C][:, first % C : first % C + count], MULT)
+            nc.vector.tensor_tensor(rows, planes[s][t][:].indirect(offs_sb[:, cols]), gate_sb[:, first : first + count], MULT)
 
         def quantize(grouped, label, tag=None):
             width = grouped.shape[1]
@@ -123,7 +123,7 @@ def tile_moe_bdx_mlp_relu_kernel(tc, dyT, a, w2_words, w2_scales, w1_words, w1_s
                         out=dh[:],
                         lhsT=words[:, cols].bitcast(FP8X4),
                         lhsT_scale=scale_bytes[:, cols],
-                        rhs=w2_sb[e][:, s, :].bitcast(FP4X4),
+                        rhs=w2_sb[e][s][:].bitcast(FP4X4),
                         rhs_scale=s2_sb[:, N_PASSES * e + s, :],
                         start=(s == 0),
                         stop=(s == N_PASSES - 1),
@@ -140,19 +140,19 @@ def tile_moe_bdx_mlp_relu_kernel(tc, dyT, a, w2_words, w2_scales, w1_words, w1_s
                     nc.tensor.transpose(turned[:, u, P * blk : P * (blk + 1)], rounded.bitcast(F32)[:, P * u : P * (u + 1)], identity[:])
             return turned
 
-        def apply_mask(da, mask, h, turned):
-            cols = slice(HALF * h, HALF * (h + 1))
+        def apply_mask(da, mask, turned):
             nc.vector.tensor_tensor(
-                da[:, cols, :].rearrange("p r (u v) -> p r u v", u=2),
+                da.rearrange("p r (u v) -> p r u v", u=2),
                 turned[:].rearrange("p u r -> p (u r)").bitcast(BF16).rearrange("p (u r v) -> p r u v", u=2, v=2),
                 mask.rearrange("p r (u v) -> p r u v", u=2),
                 MULT,
             )
 
-        def make_mask(e, tag):
-            signs = keep.tile([P, C, PACK], BF16, name=f"signs_{e}", tag=tag, align_bytes=64)
-            nc.scalar.activation(by_four(signs[:]), rows_by_four(a_late[:]), SIGN)
-            mask = keep.tile([P, C, PACK], BF16, name=f"mask_{e}", tag=f"mask_{e}", align_bytes=64)
+        def make_mask(rows, label, tag):
+            width = rows.shape[2]
+            signs = keep.tile([P, width, PACK], BF16, name=f"signs_{label}", tag=tag, align_bytes=64)
+            nc.scalar.activation(by_four(signs[:]), rows_by_four(rows), SIGN)
+            mask = keep.tile([P, width, PACK], BF16, name=f"mask_{label}", tag=f"mask_{label}", align_bytes=64)
             nc.scalar.activation(mask[:].rearrange("p c t -> p (c t)"), signs[:].rearrange("p c t -> p (c t)"), RELU)
             return mask
 
@@ -175,40 +175,61 @@ def tile_moe_bdx_mlp_relu_kernel(tc, dyT, a, w2_words, w2_scales, w1_words, w1_s
             cols = slice((C * e + first) // 16, (C * e + first + count) // 16)
             nc.vector.tensor_copy(windows[b][:].indirect(offs_sb[:, cols]), x)
 
-        g0 = [keep.tile([P, PACK, C], F32, name=f"g0_{e}") for e in range(E)]
+        g0 = keep.tile([P, PACK, S], F32, name="g0")
+        gather(0, 0, 0, HALF, g0[:, 0, 0:HALF])
+        gather(0, 0, HALF, S - HALF, g0[:, 0, HALF:S])
+        for t in range(1, PACK - 1):
+            gather(0, t, 0, S, g0[:, t, :])
+        for e in range(E):
+            gather(0, PACK - 1, C * e, C, g0[:, PACK - 1, C * e : C * (e + 1)])
+        mask0 = [make_mask(a_first[0][:], "0_0", "signs_0_0")]
+        q00 = [quantize(interleave(g0[:, :, HALF * h : HALF * (h + 1)], f"0_0_{h}"), f"0_0_{h}") for h in range(2)]
+        mask0.append(make_mask(a_first[1][:], "0_1", "signs_0_1"))
+
+        g1_early = keep.tile([P, 2, C], F32, name="g1_early")
+        pitch = SLOT - C
+        second = SLOT + HALF + P
+        g1 = [
+            arena[:, SLOT - HALF : SLOT + HALF].rearrange("p (t c) -> p t c", t=2),
+            arena[:, second : second + 2 * pitch].rearrange("p (t c) -> p t c", t=2)[:, :, 0:HALF],
+        ]
+        gi10 = [keep.tile([P, HALF, PACK], BF16, name=f"gi_1_0_{h}", align_bytes=64) for h in range(2)]
+        for t in range(2):
+            gather(1, t, 0, C, g1_early[:, t, :])
         for h in range(2):
-            gather(0, 0, HALF * h, HALF, g0[0][:, 0, HALF * h : HALF * (h + 1)])
-        for t in range(PACK):
-            for e in range(E):
-                if (t, e) != (0, 0):
-                    gather(0, t, e * C, C, g0[e][:, t, :])
-        q00 = [quantize(interleave(g0[0][:, :, HALF * h : HALF * (h + 1)], f"0_0_{h}"), f"0_0_{h}") for h in range(2)]
-
-        g1 = [arena[:, first : first + 2 * C].rearrange("p (t c) -> p t c", t=PACK) for first in (SLOT, 2 * SLOT + HALF)]
-        for t in range(PACK):
+            nc.scalar.copy(gi10[h][:, :, 0:2], g1_early[:, :, HALF * h : HALF * (h + 1)].rearrange("p t c -> p c t"))
+        for t in range(2):
             for h in range(2):
-                gather(1, t, HALF * h, HALF, g1[h][:, t, :])
-        da0 = arena[:, 3 * SLOT + HALF : 3 * SLOT + HALF + 2 * C].bitcast(BF16).rearrange("p (c t) -> p c t", t=PACK)
-        mask0 = arena[:, 2 * SLOT + C : 3 * SLOT].bitcast(BF16).rearrange("p (c t) -> p c t", t=PACK)
+                gather(1, 2 + t, HALF * h, HALF, g1[h][:, t, :])
 
-        def mask_on_vector(h):
-            nc.vector.tensor_single_scalar(by_four(mask0[:, HALF * h : HALF * (h + 1), :]), rows_by_four(a_first[h][:]), 0.0, IS_GT)
+        def finish(h):
+            nc.scalar.copy(gi10[h][:, :, 2:4], g1[h].rearrange("p t c -> p c t"))
+            return quantize(gi10[h][:], f"1_0_{h}")
 
-        gather(1, 0, C, C, late_rows[:, 0, :])
-        q10 = [quantize(interleave(g1[0], "1_0_0"), "1_0_0")]
-        gather(1, 1, C, C, late_rows[:, 1, :])
-        q10.append(quantize(interleave(g1[1], "1_0_1"), "1_0_1"))
-        mask_on_vector(0)
+        da0_first = keep.tile([P, HALF, PACK], BF16, name="da0_first", align_bytes=64)
+        da0 = [da0_first[:], arena[:, 3 * SLOT + HALF : 3 * SLOT + HALF + C].bitcast(BF16).rearrange("p (c t) -> p c t", t=PACK)]
+        da0_words = keep.tile([P, C], U32, name="da0_words", align_bytes=64)
+        da0_scales = keep.tile([P, C], U8, name="da0_scales", align_bytes=64)
+        for h in range(2):
+            gather(1, 0, C + HALF * h, HALF, late_rows[:, 0, HALF * h : HALF * (h + 1)])
+        q10 = [finish(0)]
+        gather(1, 1, C, HALF, late_rows[:, 1, 0:HALF])
+        q10.append(finish(1))
+        gather(1, 1, C + HALF, HALF, late_rows[:, 1, HALF:C])
         gather(1, 2, C, C, late_rows[:, 2, :])
-        mask_on_vector(1)
         for h in range(2):
             turned = first_product(0, h, [(q00[h][0], q00[h][1], 0), (q10[h][0], q10[h][1], 0)])
-            apply_mask(da0, mask0[:, HALF * h : HALF * (h + 1), :], h, turned)
-        gather(1, PACK - 1, C, HALF, late_rows[:, PACK - 1, 0:HALF])
-        da0_q = quantize(da0, "da0")
+            apply_mask(da0[h], mask0[h][:], turned)
+            if h == 1:
+                gather(1, PACK - 1, C, HALF, late_rows[:, PACK - 1, 0:HALF])
+            cols = slice(HALF * h, HALF * (h + 1))
+            nc.vector.quantize_mx(out=da0_words[:, cols].bitcast(FP8X4), scales=da0_scales[:, cols], in_=da0[h].rearrange("p c t -> p (c t)"))
+        da0_q = (da0_words, da0_scales)
         gather(1, PACK - 1, C + HALF, HALF, late_rows[:, PACK - 1, HALF:C])
-        q01 = quantize(interleave(g0[1][:], "0_1", tag="rounded_0_1_0"), "0_1")
-        copy_scatter(0, 0, second_product(0, 0, da0_q), 0, C, "after_first")
+        q01 = quantize(interleave(g0[:, :, C:S], "0_1", tag="rounded_0_1_0"), "0_1")
+        dx_first = second_product(0, 0, da0_q)
+        copy_scatter(0, 0, dx_first, 0, HALF, "x_first")
+        copy_scatter(0, 0, dx_first, HALF, HALF, "after_first")
 
         q11 = [quantize(interleave(late_rows[:, :, HALF * h : HALF * (h + 1)], f"1_1_{h}"), f"1_1_{h}") for h in range(2)]
         for b in range(1, HELD):
@@ -216,10 +237,10 @@ def tile_moe_bdx_mlp_relu_kernel(tc, dyT, a, w2_words, w2_scales, w1_words, w1_s
         dx_held = second_product(0, HELD, da0_q)
         copy_scatter(0, HELD, dx_held, 0, HALF, "x_held")
         turned1 = [first_product(1, h, [(q01[0], q01[1], HALF * h), (q11[h][0], q11[h][1], 0)]) for h in range(2)]
-        mask1 = make_mask(1, "after_first")
+        mask1 = make_mask(a_late[:], "1", "after_first")
         da1 = keep.tile([P, C, PACK], BF16, name="da1", align_bytes=64)
         for h in range(2):
-            apply_mask(da1, mask1[:, HALF * h : HALF * (h + 1), :], h, turned1[h])
+            apply_mask(da1[:, HALF * h : HALF * (h + 1), :], mask1[:, HALF * h : HALF * (h + 1), :], turned1[h])
         copy_scatter(0, HELD, dx_held, HALF, HALF, "after_first")
         da1_q = quantize(da1[:], "da1")
         copy_scatter(0, HELD + 1, second_product(0, HELD + 1, da0_q), 0, C, "mask_1")

@@ -40,7 +40,7 @@ def tile_moe_bdx_mlp_relu_kernel(tc, dyT, a, w2_words, w2_scales, w1_words, w1_s
 
         offs_sb = keep.tile([P, S // 16], U16, name="offs_sb")
         arena = keep.tile([P, PACK * SLOT], F32, name="arena", align_bytes=64)
-        gate_sb = arena[:, HALF : HALF + S]
+        gate_sb = arena[:, SLOT + HALF : SLOT + HALF + S]
         late_rows = arena[:].rearrange("p (t c) -> p t c", t=PACK)[:, :, 0:C]
         planes = [[keep.tile([P, T], F32, name=f"dy_{s}_{t}") for t in range(PACK)] for s in range(N_PASSES)]
         a_first = [keep.tile([P, PACK, HALF], F32, name=f"a_0_{h}") for h in range(2)]
@@ -75,9 +75,10 @@ def tile_moe_bdx_mlp_relu_kernel(tc, dyT, a, w2_words, w2_scales, w1_words, w1_s
                 if (s, t) == (1, 2):
                     nc.sync.dma_start(w2_sb[0][0][:].bitcast(I32), w2_words[0, 0].bitcast(I32))
                     load_s2(0)
-                if (s, t) in ((0, 2), (1, 0)):
-                    nc.sync.dma_start(a_first[s][:], a_view[:, :, HALF * s : HALF * (s + 1)])
+                if (s, t) == (0, 2):
+                    nc.sync.dma_start(a_first[0][:], a_view[:, :, 0:HALF])
         nc.sync.dma_start(w2_sb[0][1][:].bitcast(I32), w2_words[0, 1].bitcast(I32))
+        nc.sync.dma_start(a_first[1][:], a_view[:, :, HALF:C])
         for q in range(4):
             nc.sync.dma_start(s1_sb[32 * q : 32 * q + 4, :, :].bitcast(I32), s1_view[4 * q : 4 * q + 4].bitcast(I32))
         nc.sync.dma_start(w1_sb[:].bitcast(I32), w1_words.rearrange("e s p b -> p (e s) b").bitcast(I32))
@@ -182,13 +183,12 @@ def tile_moe_bdx_mlp_relu_kernel(tc, dyT, a, w2_words, w2_scales, w1_words, w1_s
             gather(0, t, 0, S, g0[:, t, :])
         for e in range(E):
             gather(0, PACK - 1, C * e, C, g0[:, PACK - 1, C * e : C * (e + 1)])
-        mask0 = [make_mask(a_first[0][:], "0_0", "signs_0_0")]
+        mask0 = [make_mask(a_first[0][:], "0_0", "signs_0_0")[:]]
         q00 = [quantize(interleave(g0[:, :, HALF * h : HALF * (h + 1)], f"0_0_{h}"), f"0_0_{h}") for h in range(2)]
-        mask0.append(make_mask(a_first[1][:], "0_1", "signs_0_1"))
 
         g1_early = keep.tile([P, 2, C], F32, name="g1_early")
-        pitch = SLOT - C
-        second = SLOT + HALF + P
+        pitch = C + P
+        second = 2 * SLOT - P
         g1 = [
             arena[:, SLOT - HALF : SLOT + HALF].rearrange("p (t c) -> p t c", t=2),
             arena[:, second : second + 2 * pitch].rearrange("p (t c) -> p t c", t=2)[:, :, 0:HALF],
@@ -210,16 +210,17 @@ def tile_moe_bdx_mlp_relu_kernel(tc, dyT, a, w2_words, w2_scales, w1_words, w1_s
         da0 = [da0_first[:], arena[:, 3 * SLOT + HALF : 3 * SLOT + HALF + C].bitcast(BF16).rearrange("p (c t) -> p c t", t=PACK)]
         da0_words = keep.tile([P, C], U32, name="da0_words", align_bytes=64)
         da0_scales = keep.tile([P, C], U8, name="da0_scales", align_bytes=64)
-        for h in range(2):
-            gather(1, 0, C + HALF * h, HALF, late_rows[:, 0, HALF * h : HALF * (h + 1)])
+        gather(1, 0, C, C, late_rows[:, 0, :])
+        gather(1, 1, C + HALF, HALF, late_rows[:, 1, HALF:C])
         q10 = [finish(0)]
         gather(1, 1, C, HALF, late_rows[:, 1, 0:HALF])
         q10.append(finish(1))
-        gather(1, 1, C + HALF, HALF, late_rows[:, 1, HALF:C])
+        mask0.append(arena[:, 2 * SLOT + C : 2 * SLOT + 2 * C].bitcast(BF16).rearrange("p (c t) -> p c t", t=PACK))
+        nc.vector.tensor_single_scalar(by_four(mask0[1]), rows_by_four(a_first[1][:]), 0.0, IS_GT)
         gather(1, 2, C, C, late_rows[:, 2, :])
         for h in range(2):
             turned = first_product(0, h, [(q00[h][0], q00[h][1], 0), (q10[h][0], q10[h][1], 0)])
-            apply_mask(da0[h], mask0[h][:], turned)
+            apply_mask(da0[h], mask0[h], turned)
             if h == 1:
                 gather(1, PACK - 1, C, HALF, late_rows[:, PACK - 1, 0:HALF])
             cols = slice(HALF * h, HALF * (h + 1))

@@ -10,7 +10,8 @@ PACK = 4
 N_PASSES = N // (P * PACK)
 K_BLOCKS = K // P
 HALF = C // 2
-HELD = 4
+BY_TOKEN = 3
+PIECES = T // C
 SLOT = 3 * C
 
 FLOPS = 2 * S * H * (N + K)
@@ -25,7 +26,6 @@ U8 = mybir.dt.uint8
 FP4X4 = mybir.dt.float4_e2m1fn_x4
 FP8X4 = mybir.dt.float8_e5m2_x4
 MULT = mybir.AluOpType.mult
-IS_GT = mybir.AluOpType.is_gt
 SIGN = mybir.ActivationFunctionType.Sign
 RELU = mybir.ActivationFunctionType.Relu
 
@@ -39,24 +39,25 @@ def tile_moe_bdx_mlp_relu_kernel(tc, dyT, a, w2_words, w2_scales, w1_words, w1_s
         psum_x = ctx.enter_context(tc.psum_pool(name="psum_x", bufs=2))
 
         offs_sb = keep.tile([P, S // 16], U16, name="offs_sb")
-        arena = keep.tile([P, PACK * SLOT], F32, name="arena", align_bytes=64)
+        arena = keep.tile([P, PACK * SLOT + P], F32, name="arena", align_bytes=64)
         gate_sb = arena[:, SLOT + HALF : SLOT + HALF + S]
-        late_rows = arena[:].rearrange("p (t c) -> p t c", t=PACK)[:, :, 0:C]
-        planes = [[keep.tile([P, T], F32, name=f"dy_{s}_{t}") for t in range(PACK)] for s in range(N_PASSES)]
+        late_rows = arena[:, 0 : PACK * SLOT].rearrange("p (t c) -> p t c", t=PACK)[:, :, 0:C]
+        planes = [[keep.tile([P, T], F32, name=f"dy_{s}_{t}", tag=f"dy_{s}_{t}", align_bytes=64) for t in range(PACK)] for s in range(N_PASSES)]
         a_first = [keep.tile([P, PACK, HALF], F32, name=f"a_0_{h}") for h in range(2)]
         a_late = keep.tile([P, PACK, C], F32, name="a_1")
         w2_sb = [[keep.tile([P, 2 * H], U8, name=f"w2_{e}_{s}", align_bytes=64) for s in range(N_PASSES)] for e in range(E)]
         s2_sb = keep.tile([P, E * N_PASSES, H], U8, name="s2_sb", align_bytes=64)
         w1_sb = keep.tile([P, E, 2 * K], U8, name="w1_sb", align_bytes=64)
         s1_sb = keep.tile([P, E, K], U8, name="s1_sb", align_bytes=64)
-        windows = [keep.tile([P, T], F32, name=f"window_{b}") for b in range(K_BLOCKS)]
+        windows = {b: keep.tile([P, T], F32, name=f"window_{b}") for b in range(BY_TOKEN, K_BLOCKS)}
+        pair_windows = [keep.tile([P, T], F32, name=f"pair_window_{u}") for u in range(2)]
         identity = keep.tile([P, P], F32, name="identity")
 
         s2_view = w2_scales.rearrange("e s f i -> f (e s) i")
         s1_view = w1_scales.rearrange("e s f k -> f (e s) k")
         dy_view = dyT.rearrange("(s p t) c -> s t p c", p=P, t=PACK)
         a_view = a.rearrange("(p t) c -> p t c", t=PACK)
-        nc.vector.memset(windows[0][:], 0.0)
+        nc.vector.memset(windows[BY_TOKEN][:], 0.0)
         nc.vector.memset(s2_sb[:].rearrange("p q i -> p (q i)").bitcast(I32), 0)
         nc.vector.memset(s1_sb[:].rearrange("p e k -> p (e k)").bitcast(I32), 0)
 
@@ -88,8 +89,8 @@ def tile_moe_bdx_mlp_relu_kernel(tc, dyT, a, w2_words, w2_scales, w1_words, w1_s
         nc.sync.dma_start(a_late[:], a_view[:, :, C : 2 * C])
 
         make_identity(nc, identity[:])
-        for b in range(1, K_BLOCKS):
-            nc.scalar.activation(windows[b][:], windows[0][:], SIGN)
+        for zeroed in pair_windows + [windows[b] for b in range(BY_TOKEN + 1, K_BLOCKS)]:
+            nc.scalar.activation(zeroed[:], windows[BY_TOKEN][:], SIGN)
 
         def by_four(grouped):
             return grouped.rearrange("p (c i) t -> p c t i", i=4)
@@ -129,8 +130,8 @@ def tile_moe_bdx_mlp_relu_kernel(tc, dyT, a, w2_words, w2_scales, w1_words, w1_s
                         start=(s == 0),
                         stop=(s == N_PASSES - 1),
                     )
-                if (e, h, blk) == (0, 1, 1):
-                    rounded = arena[:, 3 * SLOT : 3 * SLOT + H // 2].bitcast(BF16)
+                if (e, h, blk) == (0, 0, 1):
+                    rounded = arena[:, 3 * SLOT + HALF : 3 * SLOT + C].bitcast(BF16)
                 else:
                     rounded = keep.tile([P, H], BF16, name=f"rounded_{e}_{h}_{blk}", tag=f"rounded_{e}_{h}_{blk}", align_bytes=64)[:]
                 nc.scalar.copy(
@@ -170,25 +171,39 @@ def tile_moe_bdx_mlp_relu_kernel(tc, dyT, a, w2_words, w2_scales, w1_words, w1_s
             )
             return dx
 
-        def copy_scatter(e, b, dx, first, count, tag):
-            x = arena[:, 0:C] if tag is None else keep.tile([P, count], F32, name=f"x_{e}_{b}_{first}", tag=tag, align_bytes=64)[:]
-            nc.scalar.copy(x, dx[:, first : first + count])
-            cols = slice((C * e + first) // 16, (C * e + first + count) // 16)
-            nc.vector.tensor_copy(windows[b][:].indirect(offs_sb[:, cols]), x)
+        def copy_out(e, b, dx, first, count):
+            x = keep.tile([P, count], F32, name=f"x_{e}_{b}_{first}", align_bytes=64)
+            nc.scalar.copy(x[:], dx[:, first : first + count])
+            return x[:]
 
-        g0 = keep.tile([P, PACK, S], F32, name="g0")
+        def scatter(window, first, values):
+            cols = slice(first // 16, (first + values.shape[1]) // 16)
+            nc.vector.tensor_copy(window[:].indirect(offs_sb[:, cols]), values)
+
+        def copy_scatter(e, b):
+            scatter(windows[b], C * e, copy_out(e, b, second_product(e, b, da_q[e]), 0, C))
+
+        g0 = keep.tile([P, PACK, S], F32, name="g0", tag="g0")
         gather(0, 0, 0, HALF, g0[:, 0, 0:HALF])
         gather(0, 0, HALF, S - HALF, g0[:, 0, HALF:S])
         for t in range(1, PACK - 1):
             gather(0, t, 0, S, g0[:, t, :])
         for e in range(E):
             gather(0, PACK - 1, C * e, C, g0[:, PACK - 1, C * e : C * (e + 1)])
-        mask0 = [make_mask(a_first[0][:], "0_0", "signs_0_0")[:]]
+        signs_first = keep.tile([P, 2 * C], BF16, name="signs_first", align_bytes=64)
+        nc.scalar.activation(
+            signs_first[:].rearrange("p (u r v) -> p u r v", u=2, v=2),
+            a_first[0][:].rearrange("p (u v) r -> p u r v", u=2),
+            SIGN,
+        )
+        mask_first = keep.tile([P, 2 * C], BF16, name="mask_first", align_bytes=64)
+        nc.scalar.activation(mask_first[:], signs_first[:], RELU)
         q00 = [quantize(interleave(g0[:, :, HALF * h : HALF * (h + 1)], f"0_0_{h}"), f"0_0_{h}") for h in range(2)]
+        q01 = quantize(interleave(g0[:, :, C:S], "0_1"), "0_1")
 
         g1_early = keep.tile([P, 2, C], F32, name="g1_early")
-        pitch = C + P
         second = 2 * SLOT - P
+        pitch = 3 * SLOT - second
         g1 = [
             arena[:, SLOT - HALF : SLOT + HALF].rearrange("p (t c) -> p t c", t=2),
             arena[:, second : second + 2 * pitch].rearrange("p (t c) -> p t c", t=2)[:, :, 0:HALF],
@@ -206,45 +221,66 @@ def tile_moe_bdx_mlp_relu_kernel(tc, dyT, a, w2_words, w2_scales, w1_words, w1_s
             nc.scalar.copy(gi10[h][:, :, 2:4], g1[h].rearrange("p t c -> p c t"))
             return quantize(gi10[h][:], f"1_0_{h}")
 
-        da0_first = keep.tile([P, HALF, PACK], BF16, name="da0_first", align_bytes=64)
-        da0 = [da0_first[:], arena[:, 3 * SLOT + HALF : 3 * SLOT + HALF + C].bitcast(BF16).rearrange("p (c t) -> p c t", t=PACK)]
-        da0_words = keep.tile([P, C], U32, name="da0_words", align_bytes=64)
-        da0_scales = keep.tile([P, C], U8, name="da0_scales", align_bytes=64)
         gather(1, 0, C, C, late_rows[:, 0, :])
         gather(1, 1, C + HALF, HALF, late_rows[:, 1, HALF:C])
         q10 = [finish(0)]
         gather(1, 1, C, HALF, late_rows[:, 1, 0:HALF])
         q10.append(finish(1))
-        mask0.append(arena[:, 2 * SLOT + C : 2 * SLOT + 2 * C].bitcast(BF16).rearrange("p (c t) -> p c t", t=PACK))
-        nc.vector.tensor_single_scalar(by_four(mask0[1]), rows_by_four(a_first[1][:]), 0.0, IS_GT)
         gather(1, 2, C, C, late_rows[:, 2, :])
-        for h in range(2):
-            turned = first_product(0, h, [(q00[h][0], q00[h][1], 0), (q10[h][0], q10[h][1], 0)])
-            apply_mask(da0[h], mask0[h], turned)
-            if h == 1:
-                gather(1, PACK - 1, C, HALF, late_rows[:, PACK - 1, 0:HALF])
-            cols = slice(HALF * h, HALF * (h + 1))
-            nc.vector.quantize_mx(out=da0_words[:, cols].bitcast(FP8X4), scales=da0_scales[:, cols], in_=da0[h].rearrange("p c t -> p (c t)"))
-        da0_q = (da0_words, da0_scales)
-        gather(1, PACK - 1, C + HALF, HALF, late_rows[:, PACK - 1, HALF:C])
-        q01 = quantize(interleave(g0[:, :, C:S], "0_1", tag="rounded_0_1_0"), "0_1")
-        dx_first = second_product(0, 0, da0_q)
-        copy_scatter(0, 0, dx_first, 0, HALF, "x_first")
-        copy_scatter(0, 0, dx_first, HALF, HALF, "after_first")
+        gather(1, PACK - 1, C, HALF, late_rows[:, PACK - 1, 0:HALF])
 
-        q11 = [quantize(interleave(late_rows[:, :, HALF * h : HALF * (h + 1)], f"1_1_{h}"), f"1_1_{h}") for h in range(2)]
-        for b in range(1, HELD):
-            copy_scatter(0, b, second_product(0, b, da0_q), 0, C, None if b == 1 else f"x_0_{b}")
-        dx_held = second_product(0, HELD, da0_q)
-        copy_scatter(0, HELD, dx_held, 0, HALF, "x_held")
+        turned0 = [first_product(0, h, [(q00[h][0], q00[h][1], 0), (q10[h][0], q10[h][1], 0)]) for h in range(2)]
+        pairs = [keep.tile([P, C], F32, name=f"pairs_{h}", align_bytes=64) for h in range(2)]
+        nc.vector.tensor_tensor(pairs[0][:].bitcast(BF16), turned0[0][:].rearrange("p u r -> p (u r)").bitcast(BF16), mask_first[:], MULT)
+        gather(1, PACK - 1, C + HALF, HALF, late_rows[:, PACK - 1, HALF:C])
+        for u in range(2):
+            scatter(pair_windows[u], 0, pairs[0][:, HALF * u : HALF * (u + 1)])
+
+        mask_second = make_mask(a_first[1][:], "0_1", "rounded_0_1_0")
+        da0 = keep.tile([P, PACK * C], BF16, name="da0", align_bytes=64)
+        da0_words = da0[:].bitcast(U32).rearrange("p (r u) -> p r u", u=2)
+        nc.scalar.copy(da0_words[:, 0:HALF, :], pairs[0][:].bitcast(U32).rearrange("p (u r) -> p r u", u=2))
+        da0_grouped = da0[:].rearrange("p (c t) -> p c t", t=PACK)
+        apply_mask(da0_grouped[:, HALF:C, :], mask_second[:], turned0[1])
+        da_q = [quantize(da0_grouped, "da0")]
+        q11 = [quantize(interleave(late_rows[:, :, 0:HALF], "1_1_0"), "1_1_0")]
+        nc.scalar.copy(pairs[1][:].bitcast(U32).rearrange("p (u r) -> p u r", u=2), da0_words[:, HALF:C, :].rearrange("p r u -> p u r"))
+        pairs_by_token = keep.tile([P, 2 * T], U32, name="pairs_by_token", tag="g0")
+        for u in range(2):
+            scatter(pair_windows[u], HALF, pairs[1][:, HALF * u : HALF * (u + 1)])
+            nc.sync.dma_start(pairs_by_token[:, T * u : T * (u + 1)].bitcast(I32), pair_windows[u][:].bitcast(I32))
+        q11.append(quantize(interleave(late_rows[:, :, HALF:C], "1_1_1"), "1_1_1"))
+        copy_scatter(0, BY_TOKEN)
+
+        signs1 = keep.tile([P, C, PACK], BF16, name="signs1", align_bytes=64)
+        nc.scalar.activation(by_four(signs1[:]), rows_by_four(a_late[:]), SIGN)
         turned1 = [first_product(1, h, [(q01[0], q01[1], HALF * h), (q11[h][0], q11[h][1], 0)]) for h in range(2)]
-        mask1 = make_mask(a_late[:], "1", "after_first")
+        copy_scatter(0, BY_TOKEN + 1)
+        mask1 = keep.tile([P, C, PACK], BF16, name="mask1", align_bytes=64)
+        nc.scalar.activation(mask1[:].rearrange("p c t -> p (c t)"), signs1[:].rearrange("p c t -> p (c t)"), RELU)
         da1 = keep.tile([P, C, PACK], BF16, name="da1", align_bytes=64)
         for h in range(2):
             apply_mask(da1[:, HALF * h : HALF * (h + 1), :], mask1[:, HALF * h : HALF * (h + 1), :], turned1[h])
-        copy_scatter(0, HELD, dx_held, HALF, HALF, "after_first")
-        da1_q = quantize(da1[:], "da1")
-        copy_scatter(0, HELD + 1, second_product(0, HELD + 1, da0_q), 0, C, "mask_1")
-        for b in range(K_BLOCKS):
-            copy_scatter(1, b, second_product(1, b, da1_q), 0, C, f"x_1_{b}")
+        last = K_BLOCKS - 1
+        dx_last = second_product(0, last, da_q[0])
+        scatter(windows[last], 0, copy_out(0, last, dx_last, 0, HALF))
+        da_q.append(quantize(da1[:], "da1"))
+        scatter(windows[last], HALF, copy_out(0, last, dx_last, HALF, HALF))
+
+        def store(b):
             nc.sync.dma_start(out[P * b : P * (b + 1), :], windows[b][:])
+
+        both = pairs_by_token[:].rearrange("p (u c) -> p c u", u=2)
+        token_q = []
+        for j in range(PIECES):
+            grouped = keep.tile([P, C, 2], U32, name=f"by_token_{j}", tag=f"dy_1_{j}", align_bytes=64)
+            nc.scalar.copy(grouped[:], both[:, C * j : C * (j + 1), :])
+            token_q.append(quantize(grouped[:].rearrange("p c u -> p (c u)").bitcast(BF16).rearrange("p (c t) -> p c t", t=PACK), f"token_{j}", tag=("gi_0_0_0", "gi_0_0_1", "gi_0_1")[j]))
+            copy_scatter(1, BY_TOKEN + j)
+            store(BY_TOKEN + j)
+        for b in range(BY_TOKEN):
+            windows[b] = keep.tile([P, T], F32, name=f"window_{b}", tag=f"dy_0_{b}", align_bytes=64)
+            for j in range(PIECES):
+                nc.scalar.copy(windows[b][:, C * j : C * (j + 1)], second_product(0, b, token_q[j])[:])
+            copy_scatter(1, b)
+            store(b)

@@ -66,12 +66,12 @@ def tile_moe_bdx_mlp_relu_kernel(tc, dyT, a, w2_words, w2_scales, w1_words, w1_s
             for q in range(4):
                 nc.sync.dma_start(s2_sb[32 * q : 32 * q + 4, passes, :].bitcast(I32), s2_view[4 * q : 4 * q + 4, passes].bitcast(I32))
 
-        nc.sync.dma_start(offs_sb[:], offs)
-        nc.sync.dma_start(gate_sb[:, 0:HALF], gate[0:P, 0:HALF])
         for s in range(N_PASSES):
             for t in range(PACK):
                 nc.sync.dma_start(planes[s][t][:], dy_view[s, t])
                 if s == 0 and t == 0:
+                    nc.sync.dma_start(offs_sb[:], offs)
+                    nc.sync.dma_start(gate_sb[:, 0:HALF], gate[0:P, 0:HALF])
                     nc.sync.dma_start(gate_sb[:, HALF:S], gate[0:P, HALF:S])
                 if (s, t) == (1, 2):
                     nc.sync.dma_start(w2_sb[0][0][:].bitcast(I32), w2_words[0, 0].bitcast(I32))
@@ -107,6 +107,14 @@ def tile_moe_bdx_mlp_relu_kernel(tc, dyT, a, w2_words, w2_scales, w1_words, w1_s
             words = keep.tile([P, width], U32, name=f"codes_{label}", tag=tag or f"codes_{label}", align_bytes=64)
             scale_bytes = keep.tile([P, width], U8, name=f"scales_{label}", align_bytes=64)
             nc.vector.quantize_mx(out=words[:].bitcast(FP8X4), scales=scale_bytes[:], in_=grouped.rearrange("p c t -> p (c t)"))
+            return words, scale_bytes
+
+        def quantize_halves(values, label):
+            words = keep.tile([P, C], U32, name=f"codes_{label}", align_bytes=64)
+            scale_bytes = keep.tile([P, C], U8, name=f"scales_{label}", align_bytes=64)
+            for h in range(2):
+                cols = slice(HALF * h, HALF * (h + 1))
+                nc.vector.quantize_mx(out=words[:, cols].bitcast(FP8X4), scales=scale_bytes[:, cols], in_=values[:, 2 * C * h : 2 * C * (h + 1)])
             return words, scale_bytes
 
         def interleave(rows, label, tag=None):
@@ -205,7 +213,7 @@ def tile_moe_bdx_mlp_relu_kernel(tc, dyT, a, w2_words, w2_scales, w1_words, w1_s
         second = 2 * SLOT - P
         pitch = 3 * SLOT - second
         g1 = [
-            arena[:, SLOT - HALF : SLOT + HALF].rearrange("p (t c) -> p t c", t=2),
+            arena[:, HALF : HALF + 2 * (SLOT - HALF)].rearrange("p (t c) -> p t c", t=2)[:, :, 0:HALF],
             arena[:, second : second + 2 * pitch].rearrange("p (t c) -> p t c", t=2)[:, :, 0:HALF],
         ]
         gi10 = [keep.tile([P, HALF, PACK], BF16, name=f"gi_1_0_{h}", align_bytes=64) for h in range(2)]
@@ -221,11 +229,12 @@ def tile_moe_bdx_mlp_relu_kernel(tc, dyT, a, w2_words, w2_scales, w1_words, w1_s
             nc.scalar.copy(gi10[h][:, :, 2:4], g1[h].rearrange("p t c -> p c t"))
             return quantize(gi10[h][:], f"1_0_{h}")
 
-        gather(1, 0, C, C, late_rows[:, 0, :])
+        gather(1, 0, C, HALF, late_rows[:, 0, 0:HALF])
         gather(1, 1, C + HALF, HALF, late_rows[:, 1, HALF:C])
         q10 = [finish(0)]
         gather(1, 1, C, HALF, late_rows[:, 1, 0:HALF])
         q10.append(finish(1))
+        gather(1, 0, C + HALF, HALF, late_rows[:, 0, HALF:C])
         gather(1, 2, C, C, late_rows[:, 2, :])
         gather(1, PACK - 1, C, HALF, late_rows[:, PACK - 1, 0:HALF])
 
@@ -242,7 +251,7 @@ def tile_moe_bdx_mlp_relu_kernel(tc, dyT, a, w2_words, w2_scales, w1_words, w1_s
         nc.scalar.copy(da0_words[:, 0:HALF, :], pairs[0][:].bitcast(U32).rearrange("p (u r) -> p r u", u=2))
         da0_grouped = da0[:].rearrange("p (c t) -> p c t", t=PACK)
         apply_mask(da0_grouped[:, HALF:C, :], mask_second[:], turned0[1])
-        da_q = [quantize(da0_grouped, "da0")]
+        da_q = [quantize_halves(da0[:], "da0")]
         q11 = [quantize(interleave(late_rows[:, :, 0:HALF], "1_1_0"), "1_1_0")]
         nc.scalar.copy(pairs[1][:].bitcast(U32).rearrange("p (u r) -> p u r", u=2), da0_words[:, HALF:C, :].rearrange("p r u -> p u r"))
         pairs_by_token = keep.tile([P, 2 * T], U32, name="pairs_by_token", tag="g0")
@@ -251,36 +260,47 @@ def tile_moe_bdx_mlp_relu_kernel(tc, dyT, a, w2_words, w2_scales, w1_words, w1_s
             nc.sync.dma_start(pairs_by_token[:, T * u : T * (u + 1)].bitcast(I32), pair_windows[u][:].bitcast(I32))
         q11.append(quantize(interleave(late_rows[:, :, HALF:C], "1_1_1"), "1_1_1"))
         copy_scatter(0, BY_TOKEN)
+        copy_scatter(0, BY_TOKEN + 1)
 
         signs1 = keep.tile([P, C, PACK], BF16, name="signs1", align_bytes=64)
-        nc.scalar.activation(by_four(signs1[:]), rows_by_four(a_late[:]), SIGN)
+        for h in range(2):
+            cols = slice(HALF * h, HALF * (h + 1))
+            nc.scalar.activation(by_four(signs1[:, cols, :]), rows_by_four(a_late[:, :, cols]), SIGN)
         turned1 = [first_product(1, h, [(q01[0], q01[1], HALF * h), (q11[h][0], q11[h][1], 0)]) for h in range(2)]
-        copy_scatter(0, BY_TOKEN + 1)
+        last = K_BLOCKS - 1
+        dx_last = second_product(0, last, da_q[0])
+        scatter(windows[last], 0, copy_out(0, last, dx_last, 0, HALF))
         mask1 = keep.tile([P, C, PACK], BF16, name="mask1", align_bytes=64)
         nc.scalar.activation(mask1[:].rearrange("p c t -> p (c t)"), signs1[:].rearrange("p c t -> p (c t)"), RELU)
         da1 = keep.tile([P, C, PACK], BF16, name="da1", align_bytes=64)
         for h in range(2):
             apply_mask(da1[:, HALF * h : HALF * (h + 1), :], mask1[:, HALF * h : HALF * (h + 1), :], turned1[h])
-        last = K_BLOCKS - 1
-        dx_last = second_product(0, last, da_q[0])
-        scatter(windows[last], 0, copy_out(0, last, dx_last, 0, HALF))
-        da_q.append(quantize(da1[:], "da1"))
-        scatter(windows[last], HALF, copy_out(0, last, dx_last, HALF, HALF))
+        da_q.append(quantize_halves(da1[:].rearrange("p c t -> p (c t)"), "da1"))
 
         def store(b):
             nc.sync.dma_start(out[P * b : P * (b + 1), :], windows[b][:])
 
         both = pairs_by_token[:].rearrange("p (u c) -> p c u", u=2)
         token_q = []
-        for j in range(PIECES):
+
+        def quantize_tokens(j):
             grouped = keep.tile([P, C, 2], U32, name=f"by_token_{j}", tag=f"dy_1_{j}", align_bytes=64)
             nc.scalar.copy(grouped[:], both[:, C * j : C * (j + 1), :])
             token_q.append(quantize(grouped[:].rearrange("p c u -> p (c u)").bitcast(BF16).rearrange("p (c t) -> p c t", t=PACK), f"token_{j}", tag=("gi_0_0_0", "gi_0_0_1", "gi_0_1")[j]))
-            copy_scatter(1, BY_TOKEN + j)
-            store(BY_TOKEN + j)
-        for b in range(BY_TOKEN):
+
+        def fill(b):
             windows[b] = keep.tile([P, T], F32, name=f"window_{b}", tag=f"dy_0_{b}", align_bytes=64)
             for j in range(PIECES):
                 nc.scalar.copy(windows[b][:, C * j : C * (j + 1)], second_product(0, b, token_q[j])[:])
+
+        order = list(range(BY_TOKEN, K_BLOCKS)) + list(range(BY_TOKEN))
+        quantize_tokens(0)
+        scatter(windows[last], HALF, copy_out(0, last, dx_last, HALF, HALF))
+        for step, b in enumerate(order):
             copy_scatter(1, b)
             store(b)
+            if step == 0:
+                for j in range(1, PIECES):
+                    quantize_tokens(j)
+            elif step <= BY_TOKEN:
+                fill(step - 1)

@@ -76,10 +76,9 @@ def tile_moe_bdx_mlp_relu_kernel(tc, dyT, a, w2_words, w2_scales, w1_words, w1_s
                 if (s, t) == (1, 2):
                     nc.sync.dma_start(w2_sb[0][0][:].bitcast(I32), w2_words[0, 0].bitcast(I32))
                     load_s2(0)
-                if (s, t) == (0, 2):
-                    nc.sync.dma_start(a_first[0][:], a_view[:, :, 0:HALF])
         nc.sync.dma_start(w2_sb[0][1][:].bitcast(I32), w2_words[0, 1].bitcast(I32))
-        nc.sync.dma_start(a_first[1][:], a_view[:, :, HALF:C])
+        for h in range(2):
+            nc.sync.dma_start(a_first[h][:], a_view[:, :, HALF * h : HALF * (h + 1)])
         for q in range(4):
             nc.sync.dma_start(s1_sb[32 * q : 32 * q + 4, :, :].bitcast(I32), s1_view[4 * q : 4 * q + 4].bitcast(I32))
         nc.sync.dma_start(w1_sb[:].bitcast(I32), w1_words.rearrange("e s p b -> p (e s) b").bitcast(I32))
@@ -138,10 +137,7 @@ def tile_moe_bdx_mlp_relu_kernel(tc, dyT, a, w2_words, w2_scales, w1_words, w1_s
                         start=(s == 0),
                         stop=(s == N_PASSES - 1),
                     )
-                if (e, h, blk) == (0, 0, 1):
-                    rounded = arena[:, 3 * SLOT + HALF : 3 * SLOT + C].bitcast(BF16)
-                else:
-                    rounded = keep.tile([P, H], BF16, name=f"rounded_{e}_{h}_{blk}", tag=f"rounded_{e}_{h}_{blk}", align_bytes=64)[:]
+                rounded = keep.tile([P, H], BF16, name=f"rounded_{e}_{h}_{blk}", tag=f"rounded_{e}_{h}_{blk}", align_bytes=64)[:]
                 nc.scalar.copy(
                     rounded.rearrange("r (u p v) -> r u p v", u=2, v=2),
                     dh[:].rearrange("r (p u v) -> r u p v", u=2, v=2),
@@ -198,25 +194,20 @@ def tile_moe_bdx_mlp_relu_kernel(tc, dyT, a, w2_words, w2_scales, w1_words, w1_s
             gather(0, t, 0, S, g0[:, t, :])
         for e in range(E):
             gather(0, PACK - 1, C * e, C, g0[:, PACK - 1, C * e : C * (e + 1)])
-        signs_first = keep.tile([P, 2 * C], BF16, name="signs_first", align_bytes=64)
-        nc.scalar.activation(
-            signs_first[:].rearrange("p (u r v) -> p u r v", u=2, v=2),
-            a_first[0][:].rearrange("p (u v) r -> p u r v", u=2),
-            SIGN,
-        )
-        mask_first = keep.tile([P, 2 * C], BF16, name="mask_first", align_bytes=64)
-        nc.scalar.activation(mask_first[:], signs_first[:], RELU)
         q00 = [quantize(interleave(g0[:, :, HALF * h : HALF * (h + 1)], f"0_0_{h}"), f"0_0_{h}") for h in range(2)]
-        q01 = quantize(interleave(g0[:, :, C:S], "0_1"), "0_1")
+        gi01 = interleave(g0[:, :, C:S], "0_1")
 
         g1_early = keep.tile([P, 2, C], F32, name="g1_early")
         second = 2 * SLOT - P
         pitch = 3 * SLOT - second
         g1 = [
-            arena[:, HALF : HALF + 2 * (SLOT - HALF)].rearrange("p (t c) -> p t c", t=2)[:, :, 0:HALF],
+            arena[:, SLOT - HALF : SLOT + HALF].rearrange("p (t c) -> p t c", t=2),
             arena[:, second : second + 2 * pitch].rearrange("p (t c) -> p t c", t=2)[:, :, 0:HALF],
         ]
-        gi10 = [keep.tile([P, HALF, PACK], BF16, name=f"gi_1_0_{h}", align_bytes=64) for h in range(2)]
+        gi10 = [
+            keep.tile([P, HALF, PACK], BF16, name="gi_1_0_0", align_bytes=64)[:],
+            arena[:, HALF : HALF + C].bitcast(BF16).rearrange("p (c t) -> p c t", t=PACK),
+        ]
         for t in range(2):
             gather(1, t, 0, C, g1_early[:, t, :])
         for h in range(2):
@@ -227,18 +218,28 @@ def tile_moe_bdx_mlp_relu_kernel(tc, dyT, a, w2_words, w2_scales, w1_words, w1_s
 
         def finish(h):
             nc.scalar.copy(gi10[h][:, :, 2:4], g1[h].rearrange("p t c -> p c t"))
-            return quantize(gi10[h][:], f"1_0_{h}")
+            return quantize(gi10[h], f"1_0_{h}")
 
         gather(1, 0, C, HALF, late_rows[:, 0, 0:HALF])
         gather(1, 1, C + HALF, HALF, late_rows[:, 1, HALF:C])
         q10 = [finish(0)]
         gather(1, 1, C, HALF, late_rows[:, 1, 0:HALF])
         q10.append(finish(1))
-        gather(1, 0, C + HALF, HALF, late_rows[:, 0, HALF:C])
+        q01 = quantize(gi01, "0_1", tag="dy_1_1")
         gather(1, 2, C, C, late_rows[:, 2, :])
+        gather(1, 0, C + HALF, HALF, late_rows[:, 0, HALF:C])
         gather(1, PACK - 1, C, HALF, late_rows[:, PACK - 1, 0:HALF])
 
-        turned0 = [first_product(0, h, [(q00[h][0], q00[h][1], 0), (q10[h][0], q10[h][1], 0)]) for h in range(2)]
+        signs_first = arena[:, 3 * SLOT + HALF : 3 * SLOT + HALF + C].bitcast(BF16)
+        nc.scalar.activation(
+            signs_first.rearrange("p (u r v) -> p u r v", u=2, v=2),
+            a_first[0][:].rearrange("p (u v) r -> p u r v", u=2),
+            SIGN,
+        )
+        turned0 = [first_product(0, 0, [(q00[0][0], q00[0][1], 0), (q10[0][0], q10[0][1], 0)])]
+        mask_first = keep.tile([P, 2 * C], BF16, name="mask_first", align_bytes=64)
+        nc.scalar.activation(mask_first[:], signs_first, RELU)
+        turned0.append(first_product(0, 1, [(q00[1][0], q00[1][1], 0), (q10[1][0], q10[1][1], 0)]))
         pairs = [keep.tile([P, C], F32, name=f"pairs_{h}", align_bytes=64) for h in range(2)]
         nc.vector.tensor_tensor(pairs[0][:].bitcast(BF16), turned0[0][:].rearrange("p u r -> p (u r)").bitcast(BF16), mask_first[:], MULT)
         gather(1, PACK - 1, C + HALF, HALF, late_rows[:, PACK - 1, HALF:C])

@@ -39,9 +39,10 @@ def tile_moe_bdx_mlp_relu_kernel(tc, dyT, a, w2_words, w2_scales, w1_words, w1_s
         psum_x = ctx.enter_context(tc.psum_pool(name="psum_x", bufs=2))
 
         offs_sb = keep.tile([P, S // 16], U16, name="offs_sb")
-        arena = keep.tile([P, PACK * SLOT + P], F32, name="arena", align_bytes=64)
+        whole = keep.tile([P, C + PACK * SLOT], F32, name="arena", align_bytes=64)
+        arena = whole[:, C : C + PACK * SLOT]
         gate_sb = arena[:, SLOT + HALF : SLOT + HALF + S]
-        late_rows = arena[:, 0 : PACK * SLOT].rearrange("p (t c) -> p t c", t=PACK)[:, :, 0:C]
+        late_rows = arena.rearrange("p (t c) -> p t c", t=PACK)[:, :, 0:C]
         planes = [[keep.tile([P, T], F32, name=f"dy_{s}_{t}", tag=f"dy_{s}_{t}", align_bytes=64) for t in range(PACK)] for s in range(N_PASSES)]
         a_first = [keep.tile([P, PACK, HALF], F32, name=f"a_0_{h}") for h in range(2)]
         a_late = keep.tile([P, PACK, C], F32, name="a_1")
@@ -73,12 +74,13 @@ def tile_moe_bdx_mlp_relu_kernel(tc, dyT, a, w2_words, w2_scales, w1_words, w1_s
                     nc.sync.dma_start(offs_sb[:], offs)
                     nc.sync.dma_start(gate_sb[:, 0:HALF], gate[0:P, 0:HALF])
                     nc.sync.dma_start(gate_sb[:, HALF:S], gate[0:P, HALF:S])
+                if (s, t) == (0, 2):
+                    nc.sync.dma_start(a_first[0][:], a_view[:, :, 0:HALF])
                 if (s, t) == (1, 2):
                     nc.sync.dma_start(w2_sb[0][0][:].bitcast(I32), w2_words[0, 0].bitcast(I32))
                     load_s2(0)
         nc.sync.dma_start(w2_sb[0][1][:].bitcast(I32), w2_words[0, 1].bitcast(I32))
-        for h in range(2):
-            nc.sync.dma_start(a_first[h][:], a_view[:, :, HALF * h : HALF * (h + 1)])
+        nc.sync.dma_start(a_first[1][:], a_view[:, :, HALF:C])
         for q in range(4):
             nc.sync.dma_start(s1_sb[32 * q : 32 * q + 4, :, :].bitcast(I32), s1_view[4 * q : 4 * q + 4].bitcast(I32))
         nc.sync.dma_start(w1_sb[:].bitcast(I32), w1_words.rearrange("e s p b -> p (e s) b").bitcast(I32))
@@ -194,55 +196,47 @@ def tile_moe_bdx_mlp_relu_kernel(tc, dyT, a, w2_words, w2_scales, w1_words, w1_s
             gather(0, t, 0, S, g0[:, t, :])
         for e in range(E):
             gather(0, PACK - 1, C * e, C, g0[:, PACK - 1, C * e : C * (e + 1)])
-        q00 = [quantize(interleave(g0[:, :, HALF * h : HALF * (h + 1)], f"0_0_{h}"), f"0_0_{h}") for h in range(2)]
-        gi01 = interleave(g0[:, :, C:S], "0_1")
-
-        g1_early = keep.tile([P, 2, C], F32, name="g1_early")
-        second = 2 * SLOT - P
-        pitch = 3 * SLOT - second
-        g1 = [
-            arena[:, SLOT - HALF : SLOT + HALF].rearrange("p (t c) -> p t c", t=2),
-            arena[:, second : second + 2 * pitch].rearrange("p (t c) -> p t c", t=2)[:, :, 0:HALF],
-        ]
-        gi10 = [
-            keep.tile([P, HALF, PACK], BF16, name="gi_1_0_0", align_bytes=64)[:],
-            arena[:, HALF : HALF + C].bitcast(BF16).rearrange("p (c t) -> p c t", t=PACK),
-        ]
-        for t in range(2):
-            gather(1, t, 0, C, g1_early[:, t, :])
-        for h in range(2):
-            nc.scalar.copy(gi10[h][:, :, 0:2], g1_early[:, :, HALF * h : HALF * (h + 1)].rearrange("p t c -> p c t"))
-        for t in range(2):
-            for h in range(2):
-                gather(1, 2 + t, HALF * h, HALF, g1[h][:, t, :])
-
-        def finish(h):
-            nc.scalar.copy(gi10[h][:, :, 2:4], g1[h].rearrange("p t c -> p c t"))
-            return quantize(gi10[h], f"1_0_{h}")
-
-        gather(1, 0, C, HALF, late_rows[:, 0, 0:HALF])
-        gather(1, 1, C + HALF, HALF, late_rows[:, 1, HALF:C])
-        q10 = [finish(0)]
-        gather(1, 1, C, HALF, late_rows[:, 1, 0:HALF])
-        q10.append(finish(1))
-        q01 = quantize(gi01, "0_1", tag="dy_1_1")
-        gather(1, 2, C, C, late_rows[:, 2, :])
-        gather(1, 0, C + HALF, HALF, late_rows[:, 0, HALF:C])
-        gather(1, PACK - 1, C, HALF, late_rows[:, PACK - 1, 0:HALF])
-
-        signs_first = arena[:, 3 * SLOT + HALF : 3 * SLOT + HALF + C].bitcast(BF16)
+        signs_first = keep.tile([P, 2 * C], BF16, name="signs_first", tag="signs_first", align_bytes=64)[:]
         nc.scalar.activation(
             signs_first.rearrange("p (u r v) -> p u r v", u=2, v=2),
             a_first[0][:].rearrange("p (u v) r -> p u r v", u=2),
             SIGN,
         )
-        turned0 = [first_product(0, 0, [(q00[0][0], q00[0][1], 0), (q10[0][0], q10[0][1], 0)])]
         mask_first = keep.tile([P, 2 * C], BF16, name="mask_first", align_bytes=64)
         nc.scalar.activation(mask_first[:], signs_first, RELU)
+        q00 = [quantize(interleave(g0[:, :, HALF * h : HALF * (h + 1)], f"0_0_{h}"), f"0_0_{h}") for h in range(2)]
+        gi01 = interleave(g0[:, :, C:S], "0_1")
+
+        g1_early = whole[:, 0 : 2 * S].rearrange("p (t c) -> p t c", t=2)[:, :, 0:C]
+        third = 2 * SLOT - HALF
+        g1 = [
+            arena[:, third : third + SLOT].rearrange("p (t c) -> p t c", t=2)[:, :, 0:HALF],
+            arena[:, 2 * SLOT : 4 * SLOT].rearrange("p (t c) -> p t c", t=2)[:, :, 0:HALF],
+        ]
+        gi10 = [keep.tile([P, HALF, PACK], BF16, name=f"gi_1_0_{h}", align_bytes=64)[:] for h in range(2)]
+        gather(1, 0, 0, S, whole[:, 0:S])
+        gather(1, 1, 0, C, g1_early[:, 1, :])
+        for h in range(2):
+            nc.scalar.copy(gi10[h][:, :, 0:2], g1_early[:, :, HALF * h : HALF * (h + 1)].rearrange("p t c -> p c t"))
+        gather(1, 2, 0, C, arena[:, third : third + C])
+        for h in range(2):
+            gather(1, PACK - 1, HALF * h, HALF, g1[h][:, 1, :])
+
+        def finish(h):
+            nc.scalar.copy(gi10[h][:, :, 2:4], g1[h].rearrange("p t c -> p c t"))
+            return quantize(gi10[h], f"1_0_{h}")
+
+        gather(1, 1, C, C, late_rows[:, 1, :])
+        q10 = [finish(0)]
+        q10.append(finish(1))
+        gather(1, 2, C, C, late_rows[:, 2, :])
+        gather(1, PACK - 1, C, C, late_rows[:, PACK - 1, :])
+
+        turned0 = [first_product(0, 0, [(q00[0][0], q00[0][1], 0), (q10[0][0], q10[0][1], 0)])]
         turned0.append(first_product(0, 1, [(q00[1][0], q00[1][1], 0), (q10[1][0], q10[1][1], 0)]))
         pairs = [keep.tile([P, C], F32, name=f"pairs_{h}", align_bytes=64) for h in range(2)]
         nc.vector.tensor_tensor(pairs[0][:].bitcast(BF16), turned0[0][:].rearrange("p u r -> p (u r)").bitcast(BF16), mask_first[:], MULT)
-        gather(1, PACK - 1, C + HALF, HALF, late_rows[:, PACK - 1, HALF:C])
+        q01 = quantize(gi01, "0_1", tag="rounded_0_0_1")
         for u in range(2):
             scatter(pair_windows[u], 0, pairs[0][:, HALF * u : HALF * (u + 1)])
 
@@ -253,13 +247,15 @@ def tile_moe_bdx_mlp_relu_kernel(tc, dyT, a, w2_words, w2_scales, w1_words, w1_s
         da0_grouped = da0[:].rearrange("p (c t) -> p c t", t=PACK)
         apply_mask(da0_grouped[:, HALF:C, :], mask_second[:], turned0[1])
         da_q = [quantize_halves(da0[:], "da0")]
-        q11 = [quantize(interleave(late_rows[:, :, 0:HALF], "1_1_0"), "1_1_0")]
+        gi11 = keep.tile([P, C, PACK], BF16, name="gi_1_1", align_bytes=64)
+        nc.scalar.copy(by_four(gi11[:, 0:HALF, :]), rows_by_four(late_rows[:, :, 0:HALF]))
         nc.scalar.copy(pairs[1][:].bitcast(U32).rearrange("p (u r) -> p u r", u=2), da0_words[:, HALF:C, :].rearrange("p r u -> p u r"))
         pairs_by_token = keep.tile([P, 2 * T], U32, name="pairs_by_token", tag="g0")
         for u in range(2):
             scatter(pair_windows[u], HALF, pairs[1][:, HALF * u : HALF * (u + 1)])
             nc.sync.dma_start(pairs_by_token[:, T * u : T * (u + 1)].bitcast(I32), pair_windows[u][:].bitcast(I32))
-        q11.append(quantize(interleave(late_rows[:, :, HALF:C], "1_1_1"), "1_1_1"))
+        nc.scalar.copy(by_four(gi11[:, HALF:C, :]), rows_by_four(late_rows[:, :, HALF:C]))
+        q11 = quantize(gi11[:], "1_1")
         copy_scatter(0, BY_TOKEN)
         copy_scatter(0, BY_TOKEN + 1)
 
@@ -267,16 +263,14 @@ def tile_moe_bdx_mlp_relu_kernel(tc, dyT, a, w2_words, w2_scales, w1_words, w1_s
         for h in range(2):
             cols = slice(HALF * h, HALF * (h + 1))
             nc.scalar.activation(by_four(signs1[:, cols, :]), rows_by_four(a_late[:, :, cols]), SIGN)
-        turned1 = [first_product(1, h, [(q01[0], q01[1], HALF * h), (q11[h][0], q11[h][1], 0)]) for h in range(2)]
-        last = K_BLOCKS - 1
-        dx_last = second_product(0, last, da_q[0])
-        scatter(windows[last], 0, copy_out(0, last, dx_last, 0, HALF))
+        turned1 = [first_product(1, h, [(q01[0], q01[1], HALF * h), (q11[0], q11[1], HALF * h)]) for h in range(2)]
         mask1 = keep.tile([P, C, PACK], BF16, name="mask1", align_bytes=64)
         nc.scalar.activation(mask1[:].rearrange("p c t -> p (c t)"), signs1[:].rearrange("p c t -> p (c t)"), RELU)
         da1 = keep.tile([P, C, PACK], BF16, name="da1", align_bytes=64)
         for h in range(2):
             apply_mask(da1[:, HALF * h : HALF * (h + 1), :], mask1[:, HALF * h : HALF * (h + 1), :], turned1[h])
         da_q.append(quantize_halves(da1[:].rearrange("p c t -> p (c t)"), "da1"))
+        copy_scatter(0, K_BLOCKS - 1)
 
         def store(b):
             nc.sync.dma_start(out[P * b : P * (b + 1), :], windows[b][:])
@@ -296,7 +290,6 @@ def tile_moe_bdx_mlp_relu_kernel(tc, dyT, a, w2_words, w2_scales, w1_words, w1_s
 
         order = list(range(BY_TOKEN, K_BLOCKS)) + list(range(BY_TOKEN))
         quantize_tokens(0)
-        scatter(windows[last], HALF, copy_out(0, last, dx_last, HALF, HALF))
         for step, b in enumerate(order):
             copy_scatter(1, b)
             store(b)

@@ -76,9 +76,8 @@ def tile_moe_bdx_mlp_relu_kernel(tc, dyT, a, w2_words, w2_scales, w1_words, w1_s
                     nc.sync.dma_start(gate_sb[:, HALF:S], gate[0:P, HALF:S])
                 if (s, t) == (0, 2):
                     nc.sync.dma_start(a_first[0][:], a_view[:, :, 0:HALF])
-                if (s, t) == (1, 2):
-                    nc.sync.dma_start(w2_sb[0][0][:].bitcast(I32), w2_words[0, 0].bitcast(I32))
-                    load_s2(0)
+        nc.sync.dma_start(w2_sb[0][0][:].bitcast(I32), w2_words[0, 0].bitcast(I32))
+        load_s2(0)
         nc.sync.dma_start(w2_sb[0][1][:].bitcast(I32), w2_words[0, 1].bitcast(I32))
         nc.sync.dma_start(a_first[1][:], a_view[:, :, HALF:C])
         for q in range(4):
@@ -123,22 +122,30 @@ def tile_moe_bdx_mlp_relu_kernel(tc, dyT, a, w2_words, w2_scales, w1_words, w1_s
             nc.scalar.copy(by_four(grouped[:]), rows_by_four(rows))
             return grouped[:]
 
-        def first_product(e, h, operands):
-            turned = psum_t.tile([P, 2, HALF], F32, name="turned")
+        def dh_pass(dh, e, s, operand, first):
+            words, scale_bytes = operand
+            nc.tensor.matmul_mx(
+                out=dh[:],
+                lhsT=words[:, first : first + P].bitcast(FP8X4),
+                lhsT_scale=scale_bytes[:, first : first + P],
+                rhs=w2_sb[e][s][:].bitcast(FP4X4),
+                rhs_scale=s2_sb[:, N_PASSES * e + s, :],
+                start=(s == 0),
+                stop=(s == N_PASSES - 1),
+            )
+
+        def open_product(e, operand, first):
+            banks = []
             for blk in range(2):
                 dh = psum_h.tile([P, H], F32, name="dh")
-                for s in range(N_PASSES):
-                    words, scale_bytes, first = operands[s]
-                    cols = slice(first + P * blk, first + P * (blk + 1))
-                    nc.tensor.matmul_mx(
-                        out=dh[:],
-                        lhsT=words[:, cols].bitcast(FP8X4),
-                        lhsT_scale=scale_bytes[:, cols],
-                        rhs=w2_sb[e][s][:].bitcast(FP4X4),
-                        rhs_scale=s2_sb[:, N_PASSES * e + s, :],
-                        start=(s == 0),
-                        stop=(s == N_PASSES - 1),
-                    )
+                dh_pass(dh, e, 0, operand, first + P * blk)
+                banks.append(dh)
+            return banks
+
+        def close_product(e, h, banks, operand, first):
+            turned = psum_t.tile([P, 2, HALF], F32, name="turned")
+            for blk, dh in enumerate(banks):
+                dh_pass(dh, e, 1, operand, first + P * blk)
                 rounded = keep.tile([P, H], BF16, name=f"rounded_{e}_{h}_{blk}", tag=f"rounded_{e}_{h}_{blk}", align_bytes=64)[:]
                 nc.scalar.copy(
                     rounded.rearrange("r (u p v) -> r u p v", u=2, v=2),
@@ -202,7 +209,7 @@ def tile_moe_bdx_mlp_relu_kernel(tc, dyT, a, w2_words, w2_scales, w1_words, w1_s
             a_first[0][:].rearrange("p (u v) r -> p u r v", u=2),
             SIGN,
         )
-        mask_first = keep.tile([P, 2 * C], BF16, name="mask_first", align_bytes=64)
+        mask_first = keep.tile([P, 2 * C], BF16, name="mask_first", tag="mask_first", align_bytes=64)
         nc.scalar.activation(mask_first[:], signs_first, RELU)
         q00 = [quantize(interleave(g0[:, :, HALF * h : HALF * (h + 1)], f"0_0_{h}"), f"0_0_{h}") for h in range(2)]
         gi01 = interleave(g0[:, :, C:S], "0_1")
@@ -232,8 +239,8 @@ def tile_moe_bdx_mlp_relu_kernel(tc, dyT, a, w2_words, w2_scales, w1_words, w1_s
         gather(1, 2, C, C, late_rows[:, 2, :])
         gather(1, PACK - 1, C, C, late_rows[:, PACK - 1, :])
 
-        turned0 = [first_product(0, 0, [(q00[0][0], q00[0][1], 0), (q10[0][0], q10[0][1], 0)])]
-        turned0.append(first_product(0, 1, [(q00[1][0], q00[1][1], 0), (q10[1][0], q10[1][1], 0)]))
+        banks0 = [open_product(0, q00[h], 0) for h in range(2)]
+        turned0 = [close_product(0, h, banks0[h], q10[h], 0) for h in range(2)]
         pairs = [keep.tile([P, C], F32, name=f"pairs_{h}", align_bytes=64) for h in range(2)]
         nc.vector.tensor_tensor(pairs[0][:].bitcast(BF16), turned0[0][:].rearrange("p u r -> p (u r)").bitcast(BF16), mask_first[:], MULT)
         q01 = quantize(gi01, "0_1", tag="rounded_0_0_1")
@@ -241,13 +248,13 @@ def tile_moe_bdx_mlp_relu_kernel(tc, dyT, a, w2_words, w2_scales, w1_words, w1_s
             scatter(pair_windows[u], 0, pairs[0][:, HALF * u : HALF * (u + 1)])
 
         mask_second = make_mask(a_first[1][:], "0_1", "rounded_0_1_0")
-        da0 = keep.tile([P, PACK * C], BF16, name="da0", align_bytes=64)
+        da0 = keep.tile([P, PACK * C], BF16, name="da0", tag="da0", align_bytes=64)
         da0_words = da0[:].bitcast(U32).rearrange("p (r u) -> p r u", u=2)
         nc.scalar.copy(da0_words[:, 0:HALF, :], pairs[0][:].bitcast(U32).rearrange("p (u r) -> p r u", u=2))
         da0_grouped = da0[:].rearrange("p (c t) -> p c t", t=PACK)
         apply_mask(da0_grouped[:, HALF:C, :], mask_second[:], turned0[1])
         da_q = [quantize_halves(da0[:], "da0")]
-        gi11 = keep.tile([P, C, PACK], BF16, name="gi_1_1", align_bytes=64)
+        gi11 = keep.tile([P, C, PACK], BF16, name="gi_1_1", tag="rounded_0_0_0", align_bytes=64)
         nc.scalar.copy(by_four(gi11[:, 0:HALF, :]), rows_by_four(late_rows[:, :, 0:HALF]))
         nc.scalar.copy(pairs[1][:].bitcast(U32).rearrange("p (u r) -> p u r", u=2), da0_words[:, HALF:C, :].rearrange("p r u -> p u r"))
         pairs_by_token = keep.tile([P, 2 * T], U32, name="pairs_by_token", tag="g0")
@@ -259,18 +266,20 @@ def tile_moe_bdx_mlp_relu_kernel(tc, dyT, a, w2_words, w2_scales, w1_words, w1_s
         copy_scatter(0, BY_TOKEN)
         copy_scatter(0, BY_TOKEN + 1)
 
-        signs1 = keep.tile([P, C, PACK], BF16, name="signs1", align_bytes=64)
+        signs1 = keep.tile([P, C, PACK], BF16, name="signs1", tag="da0", align_bytes=64)
         for h in range(2):
             cols = slice(HALF * h, HALF * (h + 1))
             nc.scalar.activation(by_four(signs1[:, cols, :]), rows_by_four(a_late[:, :, cols]), SIGN)
-        turned1 = [first_product(1, h, [(q01[0], q01[1], HALF * h), (q11[0], q11[1], HALF * h)]) for h in range(2)]
+        turned1 = [close_product(1, h, open_product(1, q01, HALF * h), q11, HALF * h) for h in range(2)]
+        last = K_BLOCKS - 1
+        dx_last = second_product(0, last, da_q[0])
+        scatter(windows[last], 0, copy_out(0, last, dx_last, 0, HALF))
         mask1 = keep.tile([P, C, PACK], BF16, name="mask1", align_bytes=64)
         nc.scalar.activation(mask1[:].rearrange("p c t -> p (c t)"), signs1[:].rearrange("p c t -> p (c t)"), RELU)
         da1 = keep.tile([P, C, PACK], BF16, name="da1", align_bytes=64)
         for h in range(2):
             apply_mask(da1[:, HALF * h : HALF * (h + 1), :], mask1[:, HALF * h : HALF * (h + 1), :], turned1[h])
         da_q.append(quantize_halves(da1[:].rearrange("p c t -> p (c t)"), "da1"))
-        copy_scatter(0, K_BLOCKS - 1)
 
         def store(b):
             nc.sync.dma_start(out[P * b : P * (b + 1), :], windows[b][:])
@@ -290,6 +299,7 @@ def tile_moe_bdx_mlp_relu_kernel(tc, dyT, a, w2_words, w2_scales, w1_words, w1_s
 
         order = list(range(BY_TOKEN, K_BLOCKS)) + list(range(BY_TOKEN))
         quantize_tokens(0)
+        scatter(windows[last], HALF, copy_out(0, last, dx_last, HALF, HALF))
         for step, b in enumerate(order):
             copy_scatter(1, b)
             store(b)

@@ -142,11 +142,13 @@ def tile_moe_bdx_mlp_relu_kernel(tc, dyT, a, w2_words, w2_scales, w1_words, w1_s
                 banks.append(dh)
             return banks
 
+        rounded_tags = {(1, 1, 1): "dy_1_2"}
+
         def close_product(e, h, banks, operand, first):
             turned = psum_t.tile([P, 2, HALF], F32, name="turned")
             for blk, dh in enumerate(banks):
                 dh_pass(dh, e, 1, operand, first + P * blk)
-                rounded = keep.tile([P, H], BF16, name=f"rounded_{e}_{h}_{blk}", tag=f"rounded_{e}_{h}_{blk}", align_bytes=64)[:]
+                rounded = keep.tile([P, H], BF16, name=f"rounded_{e}_{h}_{blk}", tag=rounded_tags.get((e, h, blk), f"rounded_{e}_{h}_{blk}"), align_bytes=64)[:]
                 nc.scalar.copy(
                     rounded.rearrange("r (u p v) -> r u p v", u=2, v=2),
                     dh[:].rearrange("r (p u v) -> r u p v", u=2, v=2),
@@ -266,31 +268,39 @@ def tile_moe_bdx_mlp_relu_kernel(tc, dyT, a, w2_words, w2_scales, w1_words, w1_s
         copy_scatter(0, BY_TOKEN)
         copy_scatter(0, BY_TOKEN + 1)
 
+        last = K_BLOCKS - 1
         signs1 = keep.tile([P, C, PACK], BF16, name="signs1", tag="da0", align_bytes=64)
+        da1 = keep.tile([P, C, PACK], BF16, name="da1", align_bytes=64)
         for h in range(2):
             cols = slice(HALF * h, HALF * (h + 1))
             nc.scalar.activation(by_four(signs1[:, cols, :]), rows_by_four(a_late[:, :, cols]), SIGN)
-        turned1 = [close_product(1, h, open_product(1, q01, HALF * h), q11, HALF * h) for h in range(2)]
-        last = K_BLOCKS - 1
-        dx_last = second_product(0, last, da_q[0])
-        scatter(windows[last], 0, copy_out(0, last, dx_last, 0, HALF))
-        mask1 = keep.tile([P, C, PACK], BF16, name="mask1", align_bytes=64)
-        nc.scalar.activation(mask1[:].rearrange("p c t -> p (c t)"), signs1[:].rearrange("p c t -> p (c t)"), RELU)
-        da1 = keep.tile([P, C, PACK], BF16, name="da1", align_bytes=64)
-        for h in range(2):
-            apply_mask(da1[:, HALF * h : HALF * (h + 1), :], mask1[:, HALF * h : HALF * (h + 1), :], turned1[h])
-        da_q.append(quantize_halves(da1[:].rearrange("p c t -> p (c t)"), "da1"))
+            mask1 = keep.tile([P, HALF, PACK], BF16, name=f"mask1_{h}", tag=("dy_1_1", "mask1_1")[h], align_bytes=64)
+            nc.scalar.activation(mask1[:].rearrange("p c t -> p (c t)"), signs1[:, cols, :].rearrange("p c t -> p (c t)"), RELU)
+            turned = close_product(1, h, open_product(1, q01, HALF * h), q11, HALF * h)
+            woven = keep.tile([P, HALF, 2], F32, name=f"woven_{h}", tag=("dy_1_0", "token_codes")[h], align_bytes=64)
+            nc.scalar.copy(woven[:], turned[:].rearrange("p u r -> p r u"))
+            nc.gpsimd.tensor_tensor(
+                da1[:, cols, :].rearrange("p c t -> p (c t)"),
+                woven[:].rearrange("p r u -> p (r u)").bitcast(BF16),
+                mask1[:].rearrange("p c t -> p (c t)"),
+                MULT,
+            )
+            if h == 0:
+                copy_scatter(0, last)
+        da_q.append(quantize(da1[:], "da1"))
 
         def store(b):
             nc.sync.dma_start(out[P * b : P * (b + 1), :], windows[b][:])
 
         both = pairs_by_token[:].rearrange("p (u c) -> p c u", u=2)
         token_q = []
-
-        def quantize_tokens(j):
+        token_codes = keep.tile([P, PIECES, C], U32, name="token_codes", tag="token_codes", align_bytes=64)
+        token_scales = keep.tile([P, PIECES, C], U8, name="token_scales", align_bytes=64)
+        for j in range(PIECES):
             grouped = keep.tile([P, C, 2], U32, name=f"by_token_{j}", tag=f"dy_1_{j}", align_bytes=64)
             nc.scalar.copy(grouped[:], both[:, C * j : C * (j + 1), :])
-            token_q.append(quantize(grouped[:].rearrange("p c u -> p (c u)").bitcast(BF16).rearrange("p (c t) -> p c t", t=PACK), f"token_{j}", tag=("gi_0_0_0", "gi_0_0_1", "gi_0_1")[j]))
+            nc.vector.quantize_mx(out=token_codes[:, j, :].bitcast(FP8X4), scales=token_scales[:, j, :], in_=grouped[:].rearrange("p c u -> p (c u)").bitcast(BF16))
+            token_q.append((token_codes[:, j, :], token_scales[:, j, :]))
 
         def fill(b):
             windows[b] = keep.tile([P, T], F32, name=f"window_{b}", tag=f"dy_0_{b}", align_bytes=64)
@@ -298,13 +308,8 @@ def tile_moe_bdx_mlp_relu_kernel(tc, dyT, a, w2_words, w2_scales, w1_words, w1_s
                 nc.scalar.copy(windows[b][:, C * j : C * (j + 1)], second_product(0, b, token_q[j])[:])
 
         order = list(range(BY_TOKEN, K_BLOCKS)) + list(range(BY_TOKEN))
-        quantize_tokens(0)
-        scatter(windows[last], HALF, copy_out(0, last, dx_last, HALF, HALF))
         for step, b in enumerate(order):
             copy_scatter(1, b)
             store(b)
-            if step == 0:
-                for j in range(1, PIECES):
-                    quantize_tokens(j)
-            elif step <= BY_TOKEN:
-                fill(step - 1)
+            if step < BY_TOKEN:
+                fill(step)

@@ -26,6 +26,7 @@ U8 = mybir.dt.uint8
 FP4X4 = mybir.dt.float4_e2m1fn_x4
 FP8X4 = mybir.dt.float8_e5m2_x4
 MULT = mybir.AluOpType.mult
+ADD = mybir.AluOpType.add
 SIGN = mybir.ActivationFunctionType.Sign
 RELU = mybir.ActivationFunctionType.Relu
 
@@ -34,6 +35,7 @@ def tile_moe_bdx_mlp_relu_kernel(tc, dyT, a, w2_words, w2_scales, w1_words, w1_s
     nc = tc.nc
     with ExitStack() as ctx:
         keep = ctx.enter_context(tc.tile_pool(name="keep", bufs=1))
+        relay = ctx.enter_context(tc.tile_pool(name="relay", bufs=1))
         psum_h = ctx.enter_context(tc.psum_pool(name="psum_h", bufs=4))
         psum_t = ctx.enter_context(tc.psum_pool(name="psum_t", bufs=2))
         psum_x = ctx.enter_context(tc.psum_pool(name="psum_x", bufs=2))
@@ -43,9 +45,14 @@ def tile_moe_bdx_mlp_relu_kernel(tc, dyT, a, w2_words, w2_scales, w1_words, w1_s
         arena = whole[:, C : C + PACK * SLOT]
         gate_sb = arena[:, SLOT + HALF : SLOT + HALF + S]
         late_rows = arena.rearrange("p (t c) -> p t c", t=PACK)[:, :, 0:C]
-        planes = [[keep.tile([P, T], F32, name=f"dy_{s}_{t}", tag=f"dy_{s}_{t}", align_bytes=64) for t in range(PACK)] for s in range(N_PASSES)]
+        token_offset = 2 * C * PACK
+        planes = [[keep.tile([P, T], F32, name=f"dy_0_{t}", tag=f"dy_0_{t}", align_bytes=64) for t in range(PACK)]]
+        planes.append(
+            [relay.tile([P, T], F32, name=f"dy_1_{t}", align_bytes=64, offset=token_offset + 4 * T * t) for t in range(2)]
+            + [keep.tile([P, T], F32, name=f"dy_1_{t}", align_bytes=64) for t in range(2, PACK)]
+        )
         a_first = [keep.tile([P, PACK, HALF], F32, name=f"a_0_{h}") for h in range(2)]
-        a_late = keep.tile([P, PACK, C], F32, name="a_1")
+        a_late = [keep.tile([P, PACK, HALF], F32, name=f"a_1_{h}") for h in range(2)]
         w2_sb = [[keep.tile([P, 2 * H], U8, name=f"w2_{e}_{s}", align_bytes=64) for s in range(N_PASSES)] for e in range(E)]
         s2_sb = keep.tile([P, E * N_PASSES, H], U8, name="s2_sb", align_bytes=64)
         w1_sb = keep.tile([P, E, 2 * K], U8, name="w1_sb", align_bytes=64)
@@ -62,11 +69,6 @@ def tile_moe_bdx_mlp_relu_kernel(tc, dyT, a, w2_words, w2_scales, w1_words, w1_s
         nc.vector.memset(s2_sb[:].rearrange("p q i -> p (q i)").bitcast(I32), 0)
         nc.vector.memset(s1_sb[:].rearrange("p e k -> p (e k)").bitcast(I32), 0)
 
-        def load_s2(e):
-            passes = slice(N_PASSES * e, N_PASSES * (e + 1))
-            for q in range(4):
-                nc.sync.dma_start(s2_sb[32 * q : 32 * q + 4, passes, :].bitcast(I32), s2_view[4 * q : 4 * q + 4, passes].bitcast(I32))
-
         for s in range(N_PASSES):
             for t in range(PACK):
                 nc.sync.dma_start(planes[s][t][:], dy_view[s, t])
@@ -77,16 +79,17 @@ def tile_moe_bdx_mlp_relu_kernel(tc, dyT, a, w2_words, w2_scales, w1_words, w1_s
                 if (s, t) == (0, 2):
                     nc.sync.dma_start(a_first[0][:], a_view[:, :, 0:HALF])
         nc.sync.dma_start(w2_sb[0][0][:].bitcast(I32), w2_words[0, 0].bitcast(I32))
-        load_s2(0)
+        for q in range(4):
+            nc.sync.dma_start(s2_sb[32 * q : 32 * q + 4, :, :].bitcast(I32), s2_view[4 * q : 4 * q + 4].bitcast(I32))
         nc.sync.dma_start(w2_sb[0][1][:].bitcast(I32), w2_words[0, 1].bitcast(I32))
         nc.sync.dma_start(a_first[1][:], a_view[:, :, HALF:C])
+        for s in range(N_PASSES):
+            nc.sync.dma_start(w2_sb[1][s][:].bitcast(I32), w2_words[1, s].bitcast(I32))
+        nc.sync.dma_start(a_late[0][:], a_view[:, :, C : C + HALF])
         for q in range(4):
             nc.sync.dma_start(s1_sb[32 * q : 32 * q + 4, :, :].bitcast(I32), s1_view[4 * q : 4 * q + 4].bitcast(I32))
         nc.sync.dma_start(w1_sb[:].bitcast(I32), w1_words.rearrange("e s p b -> p (e s) b").bitcast(I32))
-        for s in range(N_PASSES):
-            nc.sync.dma_start(w2_sb[1][s][:].bitcast(I32), w2_words[1, s].bitcast(I32))
-        load_s2(1)
-        nc.sync.dma_start(a_late[:], a_view[:, :, C : 2 * C])
+        nc.sync.dma_start(a_late[1][:], a_view[:, :, C + HALF : 2 * C])
 
         make_identity(nc, identity[:])
         for zeroed in pair_windows + [windows[b] for b in range(BY_TOKEN + 1, K_BLOCKS)]:
@@ -107,14 +110,6 @@ def tile_moe_bdx_mlp_relu_kernel(tc, dyT, a, w2_words, w2_scales, w1_words, w1_s
             words = keep.tile([P, width], U32, name=f"codes_{label}", tag=tag or f"codes_{label}", align_bytes=64)
             scale_bytes = keep.tile([P, width], U8, name=f"scales_{label}", align_bytes=64)
             nc.vector.quantize_mx(out=words[:].bitcast(FP8X4), scales=scale_bytes[:], in_=grouped.rearrange("p c t -> p (c t)"))
-            return words, scale_bytes
-
-        def quantize_halves(values, label):
-            words = keep.tile([P, C], U32, name=f"codes_{label}", align_bytes=64)
-            scale_bytes = keep.tile([P, C], U8, name=f"scales_{label}", align_bytes=64)
-            for h in range(2):
-                cols = slice(HALF * h, HALF * (h + 1))
-                nc.vector.quantize_mx(out=words[:, cols].bitcast(FP8X4), scales=scale_bytes[:, cols], in_=values[:, 2 * C * h : 2 * C * (h + 1)])
             return words, scale_bytes
 
         def interleave(rows, label, tag=None):
@@ -142,13 +137,11 @@ def tile_moe_bdx_mlp_relu_kernel(tc, dyT, a, w2_words, w2_scales, w1_words, w1_s
                 banks.append(dh)
             return banks
 
-        rounded_tags = {(1, 1, 1): "dy_1_2"}
-
         def close_product(e, h, banks, operand, first):
             turned = psum_t.tile([P, 2, HALF], F32, name="turned")
             for blk, dh in enumerate(banks):
                 dh_pass(dh, e, 1, operand, first + P * blk)
-                rounded = keep.tile([P, H], BF16, name=f"rounded_{e}_{h}_{blk}", tag=rounded_tags.get((e, h, blk), f"rounded_{e}_{h}_{blk}"), align_bytes=64)[:]
+                rounded = keep.tile([P, H], BF16, name=f"rounded_{e}_{h}_{blk}", tag=f"rounded_{e}_{h}_{blk}", align_bytes=64)[:]
                 nc.scalar.copy(
                     rounded.rearrange("r (u p v) -> r u p v", u=2, v=2),
                     dh[:].rearrange("r (p u v) -> r u p v", u=2, v=2),
@@ -165,11 +158,11 @@ def tile_moe_bdx_mlp_relu_kernel(tc, dyT, a, w2_words, w2_scales, w1_words, w1_s
                 MULT,
             )
 
-        def make_mask(rows, label, tag):
+        def make_mask(rows, label, tag, mask_tag=None):
             width = rows.shape[2]
             signs = keep.tile([P, width, PACK], BF16, name=f"signs_{label}", tag=tag, align_bytes=64)
             nc.scalar.activation(by_four(signs[:]), rows_by_four(rows), SIGN)
-            mask = keep.tile([P, width, PACK], BF16, name=f"mask_{label}", tag=f"mask_{label}", align_bytes=64)
+            mask = keep.tile([P, width, PACK], BF16, name=f"mask_{label}", tag=mask_tag or f"mask_{label}", align_bytes=64)
             nc.scalar.activation(mask[:].rearrange("p c t -> p (c t)"), signs[:].rearrange("p c t -> p (c t)"), RELU)
             return mask
 
@@ -214,7 +207,12 @@ def tile_moe_bdx_mlp_relu_kernel(tc, dyT, a, w2_words, w2_scales, w1_words, w1_s
         mask_first = keep.tile([P, 2 * C], BF16, name="mask_first", tag="mask_first", align_bytes=64)
         nc.scalar.activation(mask_first[:], signs_first, RELU)
         q00 = [quantize(interleave(g0[:, :, HALF * h : HALF * (h + 1)], f"0_0_{h}"), f"0_0_{h}") for h in range(2)]
-        gi01 = interleave(g0[:, :, C:S], "0_1")
+        gi01 = [
+            relay.tile([P, HALF, PACK], BF16, name="gi_0_1_0", align_bytes=64, offset=0)[:],
+            keep.tile([P, HALF, PACK], BF16, name="gi_0_1_1", align_bytes=64)[:],
+        ]
+        for h in range(2):
+            nc.scalar.copy(by_four(gi01[h]), rows_by_four(g0[:, :, C + HALF * h : C + HALF * (h + 1)]))
 
         g1_early = whole[:, 0 : 2 * S].rearrange("p (t c) -> p t c", t=2)[:, :, 0:C]
         third = 2 * SLOT - HALF
@@ -245,46 +243,58 @@ def tile_moe_bdx_mlp_relu_kernel(tc, dyT, a, w2_words, w2_scales, w1_words, w1_s
         turned0 = [close_product(0, h, banks0[h], q10[h], 0) for h in range(2)]
         pairs = [keep.tile([P, C], F32, name=f"pairs_{h}", align_bytes=64) for h in range(2)]
         nc.vector.tensor_tensor(pairs[0][:].bitcast(BF16), turned0[0][:].rearrange("p u r -> p (u r)").bitcast(BF16), mask_first[:], MULT)
-        q01 = quantize(gi01, "0_1", tag="rounded_0_0_1")
+        q01 = [quantize(gi01[0], "0_1_0", tag="rounded_0_0_1")]
         for u in range(2):
             scatter(pair_windows[u], 0, pairs[0][:, HALF * u : HALF * (u + 1)])
 
         mask_second = make_mask(a_first[1][:], "0_1", "rounded_0_1_0")
-        da0 = keep.tile([P, PACK * C], BF16, name="da0", tag="da0", align_bytes=64)
-        da0_words = da0[:].bitcast(U32).rearrange("p (r u) -> p r u", u=2)
-        nc.scalar.copy(da0_words[:, 0:HALF, :], pairs[0][:].bitcast(U32).rearrange("p (u r) -> p r u", u=2))
-        da0_grouped = da0[:].rearrange("p (c t) -> p c t", t=PACK)
-        apply_mask(da0_grouped[:, HALF:C, :], mask_second[:], turned0[1])
-        da_q = [quantize_halves(da0[:], "da0")]
-        gi11 = keep.tile([P, C, PACK], BF16, name="gi_1_1", tag="rounded_0_0_0", align_bytes=64)
-        nc.scalar.copy(by_four(gi11[:, 0:HALF, :]), rows_by_four(late_rows[:, :, 0:HALF]))
-        nc.scalar.copy(pairs[1][:].bitcast(U32).rearrange("p (u r) -> p u r", u=2), da0_words[:, HALF:C, :].rearrange("p r u -> p u r"))
+        gi11 = relay.tile([P, C, PACK], BF16, name="gi_1_1", align_bytes=64, offset=0)
+        nc.gpsimd.tensor_scalar(gi11[:], late_rows.rearrange("p t c -> p c t"), 1.0, 0.0, MULT, ADD)
+        q11 = quantize(gi11[:], "1_1")
+        da0 = [
+            keep.tile([P, HALF, PACK], BF16, name="da0_0", tag="da0_0", align_bytes=64),
+            relay.tile([P, HALF, PACK], BF16, name="da0_1", align_bytes=64, offset=0),
+        ]
+        da0_words = [half[:].rearrange("p r t -> p (r t)").bitcast(U32).rearrange("p (r u) -> p r u", u=2) for half in da0]
+        nc.scalar.copy(da0_words[0], pairs[0][:].bitcast(U32).rearrange("p (u r) -> p r u", u=2))
+        apply_mask(da0[1][:], mask_second[:], turned0[1])
+        da0_codes = relay.tile([P, C], U32, name="codes_da0", align_bytes=64, offset=2 * HALF * PACK)
+        da0_scales = keep.tile([P, C], U8, name="scales_da0", align_bytes=64)
+        for h in range(2):
+            cols = slice(HALF * h, HALF * (h + 1))
+            nc.vector.quantize_mx(out=da0_codes[:, cols].bitcast(FP8X4), scales=da0_scales[:, cols], in_=da0[h][:].rearrange("p r t -> p (r t)"))
+        da_q = [(da0_codes, da0_scales)]
+        q01.append(quantize(gi01[1], "0_1_1", tag="da0_0"))
+        for u in range(2):
+            nc.scalar.copy(pairs[1][:, HALF * u : HALF * (u + 1)].bitcast(U32), da0_words[1][:, :, u])
         pairs_by_token = keep.tile([P, 2 * T], U32, name="pairs_by_token", tag="g0")
         for u in range(2):
             scatter(pair_windows[u], HALF, pairs[1][:, HALF * u : HALF * (u + 1)])
             nc.sync.dma_start(pairs_by_token[:, T * u : T * (u + 1)].bitcast(I32), pair_windows[u][:].bitcast(I32))
-        nc.scalar.copy(by_four(gi11[:, HALF:C, :]), rows_by_four(late_rows[:, :, HALF:C]))
-        q11 = quantize(gi11[:], "1_1")
         copy_scatter(0, BY_TOKEN)
         copy_scatter(0, BY_TOKEN + 1)
 
         last = K_BLOCKS - 1
-        signs1 = keep.tile([P, C, PACK], BF16, name="signs1", tag="da0", align_bytes=64)
         da1 = keep.tile([P, C, PACK], BF16, name="da1", align_bytes=64)
+        masks1 = []
         for h in range(2):
-            cols = slice(HALF * h, HALF * (h + 1))
-            nc.scalar.activation(by_four(signs1[:, cols, :]), rows_by_four(a_late[:, :, cols]), SIGN)
-            mask1 = keep.tile([P, HALF, PACK], BF16, name=f"mask1_{h}", tag=("dy_1_1", "mask1_1")[h], align_bytes=64)
-            nc.scalar.activation(mask1[:].rearrange("p c t -> p (c t)"), signs1[:, cols, :].rearrange("p c t -> p (c t)"), RELU)
-            turned = close_product(1, h, open_product(1, q01, HALF * h), q11, HALF * h)
-            woven = keep.tile([P, HALF, 2], F32, name=f"woven_{h}", tag=("dy_1_0", "token_codes")[h], align_bytes=64)
-            nc.scalar.copy(woven[:], turned[:].rearrange("p u r -> p r u"))
-            nc.gpsimd.tensor_tensor(
-                da1[:, cols, :].rearrange("p c t -> p (c t)"),
-                woven[:].rearrange("p r u -> p (r u)").bitcast(BF16),
-                mask1[:].rearrange("p c t -> p (c t)"),
-                MULT,
-            )
+            turned = close_product(1, h, open_product(1, q01[h], 0), q11, HALF * h)
+            masks1.append(make_mask(a_late[h][:], f"1_{h}", ("signs_first", "da0_0")[h], ("mask_0_1", None)[h]))
+            if h == 0:
+                pieces = [(0, HALF, keep.tile([P, HALF, 2], F32, name="woven_0", tag="mask_first", align_bytes=64))]
+            else:
+                pieces = [
+                    (0, P, relay.tile([P, P, 2], F32, name="woven_1_0", align_bytes=64, offset=token_offset)),
+                    (P, P, keep.tile([P, P, 2], F32, name="woven_1_1", tag="token_codes", align_bytes=64)),
+                ]
+            for first, count, woven in pieces:
+                nc.scalar.copy(woven[:], turned[:, :, first : first + count].rearrange("p u r -> p r u"))
+                nc.gpsimd.tensor_tensor(
+                    da1[:, HALF * h + first : HALF * h + first + count, :].rearrange("p c t -> p (c t)"),
+                    woven[:].rearrange("p r u -> p (r u)").bitcast(BF16),
+                    masks1[h][:, first : first + count, :].rearrange("p c t -> p (c t)"),
+                    MULT,
+                )
             if h == 0:
                 copy_scatter(0, last)
         da_q.append(quantize(da1[:], "da1"))
@@ -296,10 +306,11 @@ def tile_moe_bdx_mlp_relu_kernel(tc, dyT, a, w2_words, w2_scales, w1_words, w1_s
         token_q = []
         token_codes = keep.tile([P, PIECES, C], U32, name="token_codes", tag="token_codes", align_bytes=64)
         token_scales = keep.tile([P, PIECES, C], U8, name="token_scales", align_bytes=64)
+        by_token = relay.tile([P, PIECES, C, 2], U32, name="by_token", align_bytes=64, offset=token_offset)
         for j in range(PIECES):
-            grouped = keep.tile([P, C, 2], U32, name=f"by_token_{j}", tag=f"dy_1_{j}", align_bytes=64)
-            nc.scalar.copy(grouped[:], both[:, C * j : C * (j + 1), :])
-            nc.vector.quantize_mx(out=token_codes[:, j, :].bitcast(FP8X4), scales=token_scales[:, j, :], in_=grouped[:].rearrange("p c u -> p (c u)").bitcast(BF16))
+            grouped = by_token[:, j]
+            nc.scalar.copy(grouped, both[:, C * j : C * (j + 1), :])
+            nc.vector.quantize_mx(out=token_codes[:, j, :].bitcast(FP8X4), scales=token_scales[:, j, :], in_=grouped.rearrange("p c u -> p (c u)").bitcast(BF16))
             token_q.append((token_codes[:, j, :], token_scales[:, j, :]))
 
         def fill(b):

@@ -27,6 +27,8 @@ FP4X4 = mybir.dt.float4_e2m1fn_x4
 FP8X4 = mybir.dt.float8_e5m2_x4
 MULT = mybir.AluOpType.mult
 ADD = mybir.AluOpType.add
+MIN = mybir.AluOpType.min
+MAX = mybir.AluOpType.max
 SIGN = mybir.ActivationFunctionType.Sign
 RELU = mybir.ActivationFunctionType.Relu
 
@@ -158,11 +160,11 @@ def tile_moe_bdx_mlp_relu_kernel(tc, dyT, a, w2_words, w2_scales, w1_words, w1_s
                 MULT,
             )
 
-        def make_mask(rows, label, tag, mask_tag=None):
+        def make_mask(rows, label, tag):
             width = rows.shape[2]
             signs = keep.tile([P, width, PACK], BF16, name=f"signs_{label}", tag=tag, align_bytes=64)
             nc.scalar.activation(by_four(signs[:]), rows_by_four(rows), SIGN)
-            mask = keep.tile([P, width, PACK], BF16, name=f"mask_{label}", tag=mask_tag or f"mask_{label}", align_bytes=64)
+            mask = keep.tile([P, width, PACK], BF16, name=f"mask_{label}", tag=f"mask_{label}", align_bytes=64)
             nc.scalar.activation(mask[:].rearrange("p c t -> p (c t)"), signs[:].rearrange("p c t -> p (c t)"), RELU)
             return mask
 
@@ -207,12 +209,8 @@ def tile_moe_bdx_mlp_relu_kernel(tc, dyT, a, w2_words, w2_scales, w1_words, w1_s
         mask_first = keep.tile([P, 2 * C], BF16, name="mask_first", tag="mask_first", align_bytes=64)
         nc.scalar.activation(mask_first[:], signs_first, RELU)
         q00 = [quantize(interleave(g0[:, :, HALF * h : HALF * (h + 1)], f"0_0_{h}"), f"0_0_{h}") for h in range(2)]
-        gi01 = [
-            relay.tile([P, HALF, PACK], BF16, name="gi_0_1_0", align_bytes=64, offset=0)[:],
-            keep.tile([P, HALF, PACK], BF16, name="gi_0_1_1", align_bytes=64)[:],
-        ]
-        for h in range(2):
-            nc.scalar.copy(by_four(gi01[h]), rows_by_four(g0[:, :, C + HALF * h : C + HALF * (h + 1)]))
+        gi01 = relay.tile([P, C, PACK], BF16, name="gi_0_1", align_bytes=64, offset=0)[:]
+        nc.scalar.copy(by_four(gi01), rows_by_four(g0[:, :, C:S]))
 
         g1_early = whole[:, 0 : 2 * S].rearrange("p (t c) -> p t c", t=2)[:, :, 0:C]
         third = 2 * SLOT - HALF
@@ -243,14 +241,14 @@ def tile_moe_bdx_mlp_relu_kernel(tc, dyT, a, w2_words, w2_scales, w1_words, w1_s
         turned0 = [close_product(0, h, banks0[h], q10[h], 0) for h in range(2)]
         pairs = [keep.tile([P, C], F32, name=f"pairs_{h}", align_bytes=64) for h in range(2)]
         nc.vector.tensor_tensor(pairs[0][:].bitcast(BF16), turned0[0][:].rearrange("p u r -> p (u r)").bitcast(BF16), mask_first[:], MULT)
-        q01 = [quantize(gi01[0], "0_1_0", tag="rounded_0_0_1")]
+        q01 = quantize(gi01, "0_1", tag="rounded_0_0_1")
         for u in range(2):
             scatter(pair_windows[u], 0, pairs[0][:, HALF * u : HALF * (u + 1)])
 
         mask_second = make_mask(a_first[1][:], "0_1", "rounded_0_1_0")
-        gi11 = relay.tile([P, C, PACK], BF16, name="gi_1_1", align_bytes=64, offset=0)
-        nc.gpsimd.tensor_scalar(gi11[:], late_rows.rearrange("p t c -> p c t"), 1.0, 0.0, MULT, ADD)
-        q11 = quantize(gi11[:], "1_1")
+        gi11 = relay.tile([P, HALF, PACK], BF16, name="gi_1_1_0", align_bytes=64, offset=HALF * PACK)
+        nc.gpsimd.tensor_scalar(gi11[:], late_rows[:, :, 0:HALF].rearrange("p t c -> p c t"), 1.0, 0.0, MULT, ADD)
+        q11 = [quantize(gi11[:], "1_1_0")]
         da0 = [
             keep.tile([P, HALF, PACK], BF16, name="da0_0", tag="da0_0", align_bytes=64),
             relay.tile([P, HALF, PACK], BF16, name="da0_1", align_bytes=64, offset=0),
@@ -264,22 +262,32 @@ def tile_moe_bdx_mlp_relu_kernel(tc, dyT, a, w2_words, w2_scales, w1_words, w1_s
             cols = slice(HALF * h, HALF * (h + 1))
             nc.vector.quantize_mx(out=da0_codes[:, cols].bitcast(FP8X4), scales=da0_scales[:, cols], in_=da0[h][:].rearrange("p r t -> p (r t)"))
         da_q = [(da0_codes, da0_scales)]
-        q01.append(quantize(gi01[1], "0_1_1", tag="da0_0"))
+        q11.append(quantize(interleave(late_rows[:, :, HALF:C], "1_1_1", tag="rounded_0_1_1"), "1_1_1", tag="da0_0"))
         for u in range(2):
             nc.scalar.copy(pairs[1][:, HALF * u : HALF * (u + 1)].bitcast(U32), da0_words[1][:, :, u])
+        masks1 = []
+
+        def make_late_mask(h):
+            if h == 0:
+                signs = keep.tile([P, HALF, PACK], BF16, name="signs_1_0", tag="mask_0_1", align_bytes=64)
+            else:
+                signs = relay.tile([P, HALF, PACK], BF16, name="signs_1_1", align_bytes=64, offset=0)
+            nc.scalar.activation(by_four(signs[:]), rows_by_four(a_late[h][:]), SIGN)
+            masks1.append(keep.tile([P, HALF, PACK], BF16, name=f"mask_1_{h}", tag=("rounded_0_1_1", "signs_first")[h], align_bytes=64))
+            nc.gpsimd.tensor_scalar(masks1[h][:].rearrange("p c t -> p (c t)"), signs[:].rearrange("p c t -> p (c t)"), 1.0, 0.0, MIN, MAX)
+
+        make_late_mask(0)
+        make_late_mask(1)
         pairs_by_token = keep.tile([P, 2 * T], U32, name="pairs_by_token", tag="g0")
         for u in range(2):
             scatter(pair_windows[u], HALF, pairs[1][:, HALF * u : HALF * (u + 1)])
             nc.sync.dma_start(pairs_by_token[:, T * u : T * (u + 1)].bitcast(I32), pair_windows[u][:].bitcast(I32))
         copy_scatter(0, BY_TOKEN)
-        copy_scatter(0, BY_TOKEN + 1)
 
         last = K_BLOCKS - 1
         da1 = keep.tile([P, C, PACK], BF16, name="da1", align_bytes=64)
-        masks1 = []
         for h in range(2):
-            turned = close_product(1, h, open_product(1, q01[h], 0), q11, HALF * h)
-            masks1.append(make_mask(a_late[h][:], f"1_{h}", ("signs_first", "da0_0")[h], ("mask_0_1", None)[h]))
+            turned = close_product(1, h, open_product(1, q01, HALF * h), q11[h], 0)
             if h == 0:
                 pieces = [(0, HALF, keep.tile([P, HALF, 2], F32, name="woven_0", tag="mask_first", align_bytes=64))]
             else:
@@ -296,7 +304,8 @@ def tile_moe_bdx_mlp_relu_kernel(tc, dyT, a, w2_words, w2_scales, w1_words, w1_s
                     MULT,
                 )
             if h == 0:
-                copy_scatter(0, last)
+                copy_scatter(0, BY_TOKEN + 1)
+        copy_scatter(0, last)
         da_q.append(quantize(da1[:], "da1"))
 
         def store(b):

@@ -12,7 +12,9 @@ K_BLOCKS = K // P
 HALF = C // 2
 BY_TOKEN = 3
 PIECES = T // C
-SLOT = 3 * C
+EARLY_STEP = 2 * C
+LATE_STEP = 2 * C + 3 * P
+JOINT = 2
 
 FLOPS = 2 * S * H * (N + K)
 BYTES = 4 * N * T + 4 * H * S + E * (N * H + H * K) // 2 + E * (N * H + H * K) // 32 + 4 * S + 2 * P * S // 16 + 4 * K * T
@@ -43,10 +45,11 @@ def tile_moe_bdx_mlp_relu_kernel(tc, dyT, a, w2_words, w2_scales, w1_words, w1_s
         psum_x = ctx.enter_context(tc.psum_pool(name="psum_x", bufs=2))
 
         offs_sb = keep.tile([P, S // 16], U16, name="offs_sb")
-        whole = keep.tile([P, C + PACK * SLOT], F32, name="arena", align_bytes=64)
-        arena = whole[:, C : C + PACK * SLOT]
-        gate_sb = arena[:, SLOT + HALF : SLOT + HALF + S]
-        late_rows = arena.rearrange("p (t c) -> p t c", t=PACK)[:, :, 0:C]
+        gate_first = (PACK - 1) * LATE_STEP + HALF
+        arena = keep.tile([P, PACK * LATE_STEP + P], F32, name="arena", align_bytes=64)
+        gate_sb = arena[:, gate_first : gate_first + S]
+        early_rows = arena[:, HALF : HALF + PACK * EARLY_STEP].rearrange("p (t c) -> p t c", t=PACK)[:, :, 0:C]
+        late_rows = arena[:, 0 : PACK * LATE_STEP].rearrange("p (t c) -> p t c", t=PACK)[:, :, 0:C]
         token_offset = 2 * C * PACK
         planes = [[keep.tile([P, T], F32, name=f"dy_0_{t}", tag=f"dy_0_{t}", align_bytes=64) for t in range(PACK)]]
         planes.append(
@@ -72,7 +75,7 @@ def tile_moe_bdx_mlp_relu_kernel(tc, dyT, a, w2_words, w2_scales, w1_words, w1_s
         nc.vector.memset(s1_sb[:].rearrange("p e k -> p (e k)").bitcast(I32), 0)
 
         for s in range(N_PASSES):
-            for t in range(PACK):
+            for t in ((0, 1, 2, 3), (JOINT, 0, 1, 3))[s]:
                 nc.sync.dma_start(planes[s][t][:], dy_view[s, t])
                 if s == 0 and t == 0:
                     nc.sync.dma_start(offs_sb[:], offs)
@@ -212,30 +215,17 @@ def tile_moe_bdx_mlp_relu_kernel(tc, dyT, a, w2_words, w2_scales, w1_words, w1_s
         gi01 = relay.tile([P, C, PACK], BF16, name="gi_0_1", align_bytes=64, offset=0)[:]
         nc.scalar.copy(by_four(gi01), rows_by_four(g0[:, :, C:S]))
 
-        g1_early = whole[:, 0 : 2 * S].rearrange("p (t c) -> p t c", t=2)[:, :, 0:C]
-        third = 2 * SLOT - HALF
-        g1 = [
-            arena[:, third : third + SLOT].rearrange("p (t c) -> p t c", t=2)[:, :, 0:HALF],
-            arena[:, 2 * SLOT : 4 * SLOT].rearrange("p (t c) -> p t c", t=2)[:, :, 0:HALF],
-        ]
-        gi10 = [keep.tile([P, HALF, PACK], BF16, name=f"gi_1_0_{h}", align_bytes=64)[:] for h in range(2)]
-        gather(1, 0, 0, S, whole[:, 0:S])
-        gather(1, 1, 0, C, g1_early[:, 1, :])
+        gather(1, JOINT, 0, S, arena[:, HALF + JOINT * EARLY_STEP : HALF + JOINT * EARLY_STEP + S])
+        for t in range(JOINT):
+            gather(1, t, 0, C, early_rows[:, t, :])
         for h in range(2):
-            nc.scalar.copy(gi10[h][:, :, 0:2], g1_early[:, :, HALF * h : HALF * (h + 1)].rearrange("p t c -> p c t"))
-        gather(1, 2, 0, C, arena[:, third : third + C])
-        for h in range(2):
-            gather(1, PACK - 1, HALF * h, HALF, g1[h][:, 1, :])
-
-        def finish(h):
-            nc.scalar.copy(gi10[h][:, :, 2:4], g1[h].rearrange("p t c -> p c t"))
-            return quantize(gi10[h], f"1_0_{h}")
-
-        gather(1, 1, C, C, late_rows[:, 1, :])
-        q10 = [finish(0)]
-        q10.append(finish(1))
-        gather(1, 2, C, C, late_rows[:, 2, :])
+            gather(1, PACK - 1, HALF * h, HALF, early_rows[:, PACK - 1, HALF * h : HALF * (h + 1)])
         gather(1, PACK - 1, C, C, late_rows[:, PACK - 1, :])
+        gi10 = [interleave(early_rows[:, :, HALF * h : HALF * (h + 1)], f"1_0_{h}") for h in range(2)]
+        q10 = []
+        for h in range(2):
+            q10.append(quantize(gi10[h], f"1_0_{h}"))
+            gather(1, h, C, C, late_rows[:, h, :])
 
         banks0 = [open_product(0, q00[h], 0) for h in range(2)]
         turned0 = [close_product(0, h, banks0[h], q10[h], 0) for h in range(2)]

@@ -163,14 +163,6 @@ def tile_moe_bdx_mlp_relu_kernel(tc, dyT, a, w2_words, w2_scales, w1_words, w1_s
                 MULT,
             )
 
-        def make_mask(rows, label, tag):
-            width = rows.shape[2]
-            signs = keep.tile([P, width, PACK], BF16, name=f"signs_{label}", tag=tag, align_bytes=64)
-            nc.scalar.activation(by_four(signs[:]), rows_by_four(rows), SIGN)
-            mask = keep.tile([P, width, PACK], BF16, name=f"mask_{label}", tag=f"mask_{label}", align_bytes=64)
-            nc.scalar.activation(mask[:].rearrange("p c t -> p (c t)"), signs[:].rearrange("p c t -> p (c t)"), RELU)
-            return mask
-
         def second_product(e, b, da_q):
             dx = psum_x.tile([P, C], F32, name="dx")
             nc.tensor.matmul_mx(
@@ -184,8 +176,8 @@ def tile_moe_bdx_mlp_relu_kernel(tc, dyT, a, w2_words, w2_scales, w1_words, w1_s
             )
             return dx
 
-        def copy_out(e, b, dx, first, count):
-            x = keep.tile([P, count], F32, name=f"x_{e}_{b}_{first}", align_bytes=64)
+        def copy_out(e, b, dx, first, count, tag=None):
+            x = keep.tile([P, count], F32, name=f"x_{e}_{b}_{first}", tag=tag or f"x_{e}_{b}_{first}", align_bytes=64)
             nc.scalar.copy(x[:], dx[:, first : first + count])
             return x[:]
 
@@ -215,7 +207,7 @@ def tile_moe_bdx_mlp_relu_kernel(tc, dyT, a, w2_words, w2_scales, w1_words, w1_s
         gi01 = relay.tile([P, C, PACK], BF16, name="gi_0_1", align_bytes=64, offset=0)[:]
         nc.scalar.copy(by_four(gi01), rows_by_four(g0[:, :, C:S]))
 
-        gather(1, JOINT, 0, S, arena[:, HALF + JOINT * EARLY_STEP : HALF + JOINT * EARLY_STEP + S])
+        gather(1, JOINT, 0, C + HALF, arena[:, HALF + JOINT * EARLY_STEP : HALF + JOINT * EARLY_STEP + C + HALF])
         for t in range(JOINT):
             gather(1, t, 0, C, early_rows[:, t, :])
         for h in range(2):
@@ -226,6 +218,7 @@ def tile_moe_bdx_mlp_relu_kernel(tc, dyT, a, w2_words, w2_scales, w1_words, w1_s
         for h in range(2):
             q10.append(quantize(gi10[h], f"1_0_{h}"))
             gather(1, h, C, C, late_rows[:, h, :])
+        gather(1, JOINT, C + HALF, HALF, late_rows[:, JOINT, HALF:C])
 
         banks0 = [open_product(0, q00[h], 0) for h in range(2)]
         turned0 = [close_product(0, h, banks0[h], q10[h], 0) for h in range(2)]
@@ -235,7 +228,10 @@ def tile_moe_bdx_mlp_relu_kernel(tc, dyT, a, w2_words, w2_scales, w1_words, w1_s
         for u in range(2):
             scatter(pair_windows[u], 0, pairs[0][:, HALF * u : HALF * (u + 1)])
 
-        mask_second = make_mask(a_first[1][:], "0_1", "rounded_0_1_0")
+        signs_second = keep.tile([P, HALF, PACK], BF16, name="signs_second", tag="rounded_0_1_0", align_bytes=64)
+        nc.scalar.activation(by_four(signs_second[:]), rows_by_four(a_first[1][:]), SIGN)
+        mask_second = keep.tile([P, HALF, PACK], BF16, name="mask_second", tag="mask_second", align_bytes=64)
+        nc.scalar.activation(mask_second[:].rearrange("p c t -> p (c t)"), signs_second[:].rearrange("p c t -> p (c t)"), RELU)
         gi11 = relay.tile([P, HALF, PACK], BF16, name="gi_1_1_0", align_bytes=64, offset=HALF * PACK)
         nc.gpsimd.tensor_scalar(gi11[:], late_rows[:, :, 0:HALF].rearrange("p t c -> p c t"), 1.0, 0.0, MULT, ADD)
         q11 = [quantize(gi11[:], "1_1_0")]
@@ -253,13 +249,11 @@ def tile_moe_bdx_mlp_relu_kernel(tc, dyT, a, w2_words, w2_scales, w1_words, w1_s
             nc.vector.quantize_mx(out=da0_codes[:, cols].bitcast(FP8X4), scales=da0_scales[:, cols], in_=da0[h][:].rearrange("p r t -> p (r t)"))
         da_q = [(da0_codes, da0_scales)]
         q11.append(quantize(interleave(late_rows[:, :, HALF:C], "1_1_1", tag="rounded_0_1_1"), "1_1_1", tag="da0_0"))
-        for u in range(2):
-            nc.scalar.copy(pairs[1][:, HALF * u : HALF * (u + 1)].bitcast(U32), da0_words[1][:, :, u])
         masks1 = []
 
         def make_late_mask(h):
             if h == 0:
-                signs = keep.tile([P, HALF, PACK], BF16, name="signs_1_0", tag="mask_0_1", align_bytes=64)
+                signs = keep.tile([P, HALF, PACK], BF16, name="signs_1_0", tag="mask_first", align_bytes=64)
             else:
                 signs = relay.tile([P, HALF, PACK], BF16, name="signs_1_1", align_bytes=64, offset=0)
             nc.scalar.activation(by_four(signs[:]), rows_by_four(a_late[h][:]), SIGN)
@@ -267,19 +261,20 @@ def tile_moe_bdx_mlp_relu_kernel(tc, dyT, a, w2_words, w2_scales, w1_words, w1_s
             nc.gpsimd.tensor_scalar(masks1[h][:].rearrange("p c t -> p (c t)"), signs[:].rearrange("p c t -> p (c t)"), 1.0, 0.0, MIN, MAX)
 
         make_late_mask(0)
-        make_late_mask(1)
+        for u in range(2):
+            nc.scalar.copy(pairs[1][:, HALF * u : HALF * (u + 1)].bitcast(U32), da0_words[1][:, :, u])
         pairs_by_token = keep.tile([P, 2 * T], U32, name="pairs_by_token", tag="g0")
         for u in range(2):
             scatter(pair_windows[u], HALF, pairs[1][:, HALF * u : HALF * (u + 1)])
             nc.sync.dma_start(pairs_by_token[:, T * u : T * (u + 1)].bitcast(I32), pair_windows[u][:].bitcast(I32))
-        copy_scatter(0, BY_TOKEN)
 
         last = K_BLOCKS - 1
-        da1 = keep.tile([P, C, PACK], BF16, name="da1", align_bytes=64)
+        da1 = keep.tile([P, C, PACK], BF16, name="da1", tag="da1", align_bytes=64)
         for h in range(2):
             turned = close_product(1, h, open_product(1, q01, HALF * h), q11[h], 0)
+            copy_scatter(0, BY_TOKEN + h)
             if h == 0:
-                pieces = [(0, HALF, keep.tile([P, HALF, 2], F32, name="woven_0", tag="mask_first", align_bytes=64))]
+                pieces = [(0, HALF, keep.tile([P, HALF, 2], F32, name="woven_0", tag="mask_second", align_bytes=64))]
             else:
                 pieces = [
                     (0, P, relay.tile([P, P, 2], F32, name="woven_1_0", align_bytes=64, offset=token_offset)),
@@ -294,9 +289,11 @@ def tile_moe_bdx_mlp_relu_kernel(tc, dyT, a, w2_words, w2_scales, w1_words, w1_s
                     MULT,
                 )
             if h == 0:
-                copy_scatter(0, BY_TOKEN + 1)
-        copy_scatter(0, last)
+                make_late_mask(1)
+        dx_last = second_product(0, last, da_q[0])
+        scatter(windows[last], 0, copy_out(0, last, dx_last, 0, HALF))
         da_q.append(quantize(da1[:], "da1"))
+        scatter(windows[last], HALF, copy_out(0, last, dx_last, HALF, HALF, tag="da1"))
 
         def store(b):
             nc.sync.dma_start(out[P * b : P * (b + 1), :], windows[b][:])

@@ -15,6 +15,7 @@ PIECES = T // C
 EARLY_STEP = 2 * C
 LATE_STEP = 2 * C + 3 * P
 JOINT = 2
+SQUARE = 32
 
 FLOPS = 2 * S * H * (N + K)
 BYTES = 4 * N * T + 4 * H * S + E * (N * H + H * K) // 2 + E * (N * H + H * K) // 32 + 4 * S + 2 * P * S // 16 + 4 * K * T
@@ -70,7 +71,10 @@ def tile_moe_bdx_mlp_relu_kernel(tc, dyT, a, w2_words, w2_scales, w1_words, w1_s
         s1_view = w1_scales.rearrange("e s f k -> f (e s) k")
         dy_view = dyT.rearrange("(s p t) c -> s t p c", p=P, t=PACK)
         a_view = a.rearrange("(p t) c -> p t c", t=PACK)
-        nc.vector.memset(windows[BY_TOKEN][:], 0.0)
+        gate_runs = keep.tile([P, SQUARE], F32, name="gate_runs", align_bytes=64)
+        nc.sync.dma_start(gate_runs[:], gate[0 : P * SQUARE // S, :].rearrange("r (b c) -> (r b) c", c=SQUARE))
+        zero = keep.tile([P, 1], F32, name="zero")
+        nc.vector.memset(zero[:], 0.0)
         nc.vector.memset(s2_sb[:].rearrange("p q i -> p (q i)").bitcast(I32), 0)
         nc.vector.memset(s1_sb[:].rearrange("p e k -> p (e k)").bitcast(I32), 0)
 
@@ -80,7 +84,7 @@ def tile_moe_bdx_mlp_relu_kernel(tc, dyT, a, w2_words, w2_scales, w1_words, w1_s
                 if s == 0 and t == 0:
                     nc.sync.dma_start(offs_sb[:], offs)
                     nc.sync.dma_start(gate_sb[:, 0:HALF], gate[0:P, 0:HALF])
-                    nc.sync.dma_start(gate_sb[:, HALF:S], gate[0:P, HALF:S])
+                    nc.sync.dma_start(gate_sb[:, HALF:C], gate[0:P, HALF:C])
                 if (s, t) == (0, 2):
                     nc.sync.dma_start(a_first[0][:], a_view[:, :, 0:HALF])
         nc.sync.dma_start(w2_sb[0][0][:].bitcast(I32), w2_words[0, 0].bitcast(I32))
@@ -96,9 +100,16 @@ def tile_moe_bdx_mlp_relu_kernel(tc, dyT, a, w2_words, w2_scales, w1_words, w1_s
         nc.sync.dma_start(w1_sb[:].bitcast(I32), w1_words.rearrange("e s p b -> p (e s) b").bitcast(I32))
         nc.sync.dma_start(a_late[1][:], a_view[:, :, C + HALF : 2 * C])
 
+        gate_turned = keep.tile([P, SQUARE], F32, name="gate_turned", align_bytes=64)
+        nc.vector.transpose(gate_turned[:], gate_runs[:])
+        gate_spread = keep.tile([P, C // SQUARE, SQUARE], F32, name="gate_spread", align_bytes=64)
+        nc.vector.tensor_copy(gate_spread[:], gate_turned[:, C // SQUARE : S // SQUARE].unsqueeze(2).to_broadcast([P, C // SQUARE, SQUARE]))
+        nc.vector.transpose(gate_sb[:, C:S], gate_spread[:].rearrange("p b c -> p (b c)"))
         make_identity(nc, identity[:])
-        for zeroed in pair_windows + [windows[b] for b in range(BY_TOKEN + 1, K_BLOCKS)]:
-            nc.scalar.activation(zeroed[:], windows[BY_TOKEN][:], SIGN)
+        for zeroed in pair_windows + [windows[b] for b in range(BY_TOKEN, K_BLOCKS - 1)]:
+            nc.scalar.activation(zeroed[:], zero[:].to_broadcast([P, T]), SIGN)
+        nc.vector.memset(windows[K_BLOCKS - 1][:, 0 : T // 2], 0.0)
+        nc.scalar.activation(windows[K_BLOCKS - 1][:, T // 2 : T], zero[:].to_broadcast([P, T // 2]), SIGN)
 
         def by_four(grouped):
             return grouped.rearrange("p (c i) t -> p c t i", i=4)
@@ -142,10 +153,10 @@ def tile_moe_bdx_mlp_relu_kernel(tc, dyT, a, w2_words, w2_scales, w1_words, w1_s
                 banks.append(dh)
             return banks
 
-        def close_product(e, h, banks, operand, first):
+        def close_product(e, h, banks, operands):
             turned = psum_t.tile([P, 2, HALF], F32, name="turned")
             for blk, dh in enumerate(banks):
-                dh_pass(dh, e, 1, operand, first + P * blk)
+                dh_pass(dh, e, 1, *operands[blk])
                 rounded = keep.tile([P, H], BF16, name=f"rounded_{e}_{h}_{blk}", tag=f"rounded_{e}_{h}_{blk}", align_bytes=64)[:]
                 nc.scalar.copy(
                     rounded.rearrange("r (u p v) -> r u p v", u=2, v=2),
@@ -207,21 +218,23 @@ def tile_moe_bdx_mlp_relu_kernel(tc, dyT, a, w2_words, w2_scales, w1_words, w1_s
         gi01 = relay.tile([P, C, PACK], BF16, name="gi_0_1", align_bytes=64, offset=0)[:]
         nc.scalar.copy(by_four(gi01), rows_by_four(g0[:, :, C:S]))
 
-        gather(1, JOINT, 0, C + HALF, arena[:, HALF + JOINT * EARLY_STEP : HALF + JOINT * EARLY_STEP + C + HALF])
+        gather(1, JOINT, 0, C + P, arena[:, HALF + JOINT * EARLY_STEP : HALF + JOINT * EARLY_STEP + C + P])
         for t in range(JOINT):
             gather(1, t, 0, C, early_rows[:, t, :])
         for h in range(2):
             gather(1, PACK - 1, HALF * h, HALF, early_rows[:, PACK - 1, HALF * h : HALF * (h + 1)])
         gather(1, PACK - 1, C, C, late_rows[:, PACK - 1, :])
-        gi10 = [interleave(early_rows[:, :, HALF * h : HALF * (h + 1)], f"1_0_{h}") for h in range(2)]
-        q10 = []
-        for h in range(2):
-            q10.append(quantize(gi10[h], f"1_0_{h}"))
-            gather(1, h, C, C, late_rows[:, h, :])
-        gather(1, JOINT, C + HALF, HALF, late_rows[:, JOINT, HALF:C])
+        gi10 = [interleave(early_rows[:, :, P * blk : P * (blk + 1)], f"1_0_0_{blk}") for blk in range(2)]
+        gi10.append(interleave(early_rows[:, :, HALF:C], "1_0_1"))
+        q10 = [[(quantize(gi10[blk], f"1_0_0_{blk}"), 0) for blk in range(2)]]
+        gather(1, 0, C, C, late_rows[:, 0, :])
+        second_half = quantize(gi10[2], "1_0_1")
+        q10.append([(second_half, 0), (second_half, P)])
+        gather(1, 1, C, C, late_rows[:, 1, :])
+        gather(1, JOINT, C + P, C - P, late_rows[:, JOINT, P:C])
 
         banks0 = [open_product(0, q00[h], 0) for h in range(2)]
-        turned0 = [close_product(0, h, banks0[h], q10[h], 0) for h in range(2)]
+        turned0 = [close_product(0, h, banks0[h], q10[h]) for h in range(2)]
         pairs = [keep.tile([P, C], F32, name=f"pairs_{h}", align_bytes=64) for h in range(2)]
         nc.vector.tensor_tensor(pairs[0][:].bitcast(BF16), turned0[0][:].rearrange("p u r -> p (u r)").bitcast(BF16), mask_first[:], MULT)
         q01 = quantize(gi01, "0_1", tag="rounded_0_0_1")
@@ -271,7 +284,7 @@ def tile_moe_bdx_mlp_relu_kernel(tc, dyT, a, w2_words, w2_scales, w1_words, w1_s
         last = K_BLOCKS - 1
         da1 = keep.tile([P, C, PACK], BF16, name="da1", tag="da1", align_bytes=64)
         for h in range(2):
-            turned = close_product(1, h, open_product(1, q01, HALF * h), q11[h], 0)
+            turned = close_product(1, h, open_product(1, q01, HALF * h), [(q11[h], 0), (q11[h], P)])
             copy_scatter(0, BY_TOKEN + h)
             if h == 0:
                 pieces = [(0, HALF, keep.tile([P, HALF, 2], F32, name="woven_0", tag="mask_second", align_bytes=64))]
@@ -293,7 +306,7 @@ def tile_moe_bdx_mlp_relu_kernel(tc, dyT, a, w2_words, w2_scales, w1_words, w1_s
         dx_last = second_product(0, last, da_q[0])
         scatter(windows[last], 0, copy_out(0, last, dx_last, 0, HALF))
         da_q.append(quantize(da1[:], "da1"))
-        scatter(windows[last], HALF, copy_out(0, last, dx_last, HALF, HALF, tag="da1"))
+        last_half = copy_out(0, last, dx_last, HALF, HALF, tag="da1")
 
         def store(b):
             nc.sync.dma_start(out[P * b : P * (b + 1), :], windows[b][:])
@@ -308,6 +321,8 @@ def tile_moe_bdx_mlp_relu_kernel(tc, dyT, a, w2_words, w2_scales, w1_words, w1_s
             nc.scalar.copy(grouped, both[:, C * j : C * (j + 1), :])
             nc.vector.quantize_mx(out=token_codes[:, j, :].bitcast(FP8X4), scales=token_scales[:, j, :], in_=grouped.rearrange("p c u -> p (c u)").bitcast(BF16))
             token_q.append((token_codes[:, j, :], token_scales[:, j, :]))
+
+        scatter(windows[last], HALF, last_half)
 
         def fill(b):
             windows[b] = keep.tile([P, T], F32, name=f"window_{b}", tag=f"dy_0_{b}", align_bytes=64)

@@ -12,10 +12,13 @@ K_BLOCKS = K // P
 HALF = C // 2
 BY_TOKEN = 3
 PIECES = T // C
+SQUARE = 32
+OFFSETS_PER_COLUMN = 16
 EARLY_STEP = 2 * C
 LATE_STEP = 2 * C + 3 * P
 JOINT = 2
-SQUARE = 32
+JOINT_EXTRA = P
+HELD = 192
 
 FLOPS = 2 * S * H * (N + K)
 BYTES = 4 * N * T + 4 * H * S + E * (N * H + H * K) // 2 + E * (N * H + H * K) // 32 + 4 * S + 2 * P * S // 16 + 4 * K * T
@@ -29,7 +32,6 @@ U8 = mybir.dt.uint8
 FP4X4 = mybir.dt.float4_e2m1fn_x4
 FP8X4 = mybir.dt.float8_e5m2_x4
 MULT = mybir.AluOpType.mult
-ADD = mybir.AluOpType.add
 MIN = mybir.AluOpType.min
 MAX = mybir.AluOpType.max
 SIGN = mybir.ActivationFunctionType.Sign
@@ -45,7 +47,7 @@ def tile_moe_bdx_mlp_relu_kernel(tc, dyT, a, w2_words, w2_scales, w1_words, w1_s
         psum_t = ctx.enter_context(tc.psum_pool(name="psum_t", bufs=2))
         psum_x = ctx.enter_context(tc.psum_pool(name="psum_x", bufs=2))
 
-        offs_sb = keep.tile([P, S // 16], U16, name="offs_sb")
+        offs_sb = keep.tile([P, S // OFFSETS_PER_COLUMN], U16, name="offs_sb")
         gate_first = (PACK - 1) * LATE_STEP + HALF
         arena = keep.tile([P, PACK * LATE_STEP + P], F32, name="arena", align_bytes=64)
         gate_sb = arena[:, gate_first : gate_first + S]
@@ -57,8 +59,7 @@ def tile_moe_bdx_mlp_relu_kernel(tc, dyT, a, w2_words, w2_scales, w1_words, w1_s
             [relay.tile([P, T], F32, name=f"dy_1_{t}", align_bytes=64, offset=token_offset + 4 * T * t) for t in range(2)]
             + [keep.tile([P, T], F32, name=f"dy_1_{t}", align_bytes=64) for t in range(2, PACK)]
         )
-        a_first = [keep.tile([P, PACK, HALF], F32, name=f"a_0_{h}") for h in range(2)]
-        a_late = [keep.tile([P, PACK, HALF], F32, name=f"a_1_{h}") for h in range(2)]
+        a_sb = [[keep.tile([P, PACK, HALF], F32, name=f"a_{e}_{h}") for h in range(2)] for e in range(E)]
         w2_sb = [[keep.tile([P, 2 * H], U8, name=f"w2_{e}_{s}", align_bytes=64) for s in range(N_PASSES)] for e in range(E)]
         s2_sb = keep.tile([P, E * N_PASSES, H], U8, name="s2_sb", align_bytes=64)
         w1_sb = keep.tile([P, E, 2 * K], U8, name="w1_sb", align_bytes=64)
@@ -71,6 +72,17 @@ def tile_moe_bdx_mlp_relu_kernel(tc, dyT, a, w2_words, w2_scales, w1_words, w1_s
         s1_view = w1_scales.rearrange("e s f k -> f (e s) k")
         dy_view = dyT.rearrange("(s p t) c -> s t p c", p=P, t=PACK)
         a_view = a.rearrange("(p t) c -> p t c", t=PACK)
+
+        def load_a(e, h):
+            nc.sync.dma_start(a_sb[e][h][:], a_view[:, :, C * e + HALF * h : C * e + HALF * (h + 1)])
+
+        def load_w2(e, s):
+            nc.sync.dma_start(w2_sb[e][s][:].bitcast(I32), w2_words[e, s].bitcast(I32))
+
+        def load_scales(scale_tile, view):
+            for q in range(4):
+                nc.sync.dma_start(scale_tile[32 * q : 32 * q + 4, :, :].bitcast(I32), view[4 * q : 4 * q + 4].bitcast(I32))
+
         gate_runs = keep.tile([P, SQUARE], F32, name="gate_runs", align_bytes=64)
         nc.sync.dma_start(gate_runs[:], gate[0 : P * SQUARE // S, :].rearrange("r (b c) -> (r b) c", c=SQUARE))
         zero = keep.tile([P, 1], F32, name="zero")
@@ -78,27 +90,29 @@ def tile_moe_bdx_mlp_relu_kernel(tc, dyT, a, w2_words, w2_scales, w1_words, w1_s
         nc.vector.memset(s2_sb[:].rearrange("p q i -> p (q i)").bitcast(I32), 0)
         nc.vector.memset(s1_sb[:].rearrange("p e k -> p (e k)").bitcast(I32), 0)
 
+        def load_plane(s, t):
+            nc.sync.dma_start(planes[s][t][:], dy_view[s, t])
+
+        load_plane(0, 0)
+        nc.sync.dma_start(offs_sb[:], offs)
+        for h in range(2):
+            nc.sync.dma_start(gate_sb[:, HALF * h : HALF * (h + 1)], gate[0:P, HALF * h : HALF * (h + 1)])
+        load_plane(0, 1)
+        load_plane(0, 2)
+        load_a(0, 0)
+        load_plane(0, 3)
+        for t in (JOINT, 0, 1, PACK - 1):
+            load_plane(1, t)
+        load_w2(0, 0)
+        load_scales(s2_sb, s2_view)
+        load_w2(0, 1)
+        load_a(0, 1)
         for s in range(N_PASSES):
-            for t in ((0, 1, 2, 3), (JOINT, 0, 1, 3))[s]:
-                nc.sync.dma_start(planes[s][t][:], dy_view[s, t])
-                if s == 0 and t == 0:
-                    nc.sync.dma_start(offs_sb[:], offs)
-                    nc.sync.dma_start(gate_sb[:, 0:HALF], gate[0:P, 0:HALF])
-                    nc.sync.dma_start(gate_sb[:, HALF:C], gate[0:P, HALF:C])
-                if (s, t) == (0, 2):
-                    nc.sync.dma_start(a_first[0][:], a_view[:, :, 0:HALF])
-        nc.sync.dma_start(w2_sb[0][0][:].bitcast(I32), w2_words[0, 0].bitcast(I32))
-        for q in range(4):
-            nc.sync.dma_start(s2_sb[32 * q : 32 * q + 4, :, :].bitcast(I32), s2_view[4 * q : 4 * q + 4].bitcast(I32))
-        nc.sync.dma_start(w2_sb[0][1][:].bitcast(I32), w2_words[0, 1].bitcast(I32))
-        nc.sync.dma_start(a_first[1][:], a_view[:, :, HALF:C])
-        for s in range(N_PASSES):
-            nc.sync.dma_start(w2_sb[1][s][:].bitcast(I32), w2_words[1, s].bitcast(I32))
-        nc.sync.dma_start(a_late[0][:], a_view[:, :, C : C + HALF])
-        for q in range(4):
-            nc.sync.dma_start(s1_sb[32 * q : 32 * q + 4, :, :].bitcast(I32), s1_view[4 * q : 4 * q + 4].bitcast(I32))
+            load_w2(1, s)
+        load_a(1, 0)
+        load_scales(s1_sb, s1_view)
         nc.sync.dma_start(w1_sb[:].bitcast(I32), w1_words.rearrange("e s p b -> p (e s) b").bitcast(I32))
-        nc.sync.dma_start(a_late[1][:], a_view[:, :, C + HALF : 2 * C])
+        load_a(1, 1)
 
         gate_turned = keep.tile([P, SQUARE], F32, name="gate_turned", align_bytes=64)
         nc.vector.transpose(gate_turned[:], gate_runs[:])
@@ -106,10 +120,11 @@ def tile_moe_bdx_mlp_relu_kernel(tc, dyT, a, w2_words, w2_scales, w1_words, w1_s
         nc.vector.tensor_copy(gate_spread[:], gate_turned[:, C // SQUARE : S // SQUARE].unsqueeze(2).to_broadcast([P, C // SQUARE, SQUARE]))
         nc.vector.transpose(gate_sb[:, C:S], gate_spread[:].rearrange("p b c -> p (b c)"))
         make_identity(nc, identity[:])
-        for zeroed in pair_windows + [windows[b] for b in range(BY_TOKEN, K_BLOCKS - 1)]:
+        last = K_BLOCKS - 1
+        for zeroed in pair_windows + [windows[b] for b in range(BY_TOKEN, last)]:
             nc.scalar.activation(zeroed[:], zero[:].to_broadcast([P, T]), SIGN)
-        nc.vector.memset(windows[K_BLOCKS - 1][:, 0 : T // 2], 0.0)
-        nc.scalar.activation(windows[K_BLOCKS - 1][:, T // 2 : T], zero[:].to_broadcast([P, T // 2]), SIGN)
+        nc.vector.memset(windows[last][:, 0 : T // 2], 0.0)
+        nc.scalar.activation(windows[last][:, T // 2 : T], zero[:].to_broadcast([P, T // 2]), SIGN)
 
         def by_four(grouped):
             return grouped.rearrange("p (c i) t -> p c t i", i=4)
@@ -117,21 +132,29 @@ def tile_moe_bdx_mlp_relu_kernel(tc, dyT, a, w2_words, w2_scales, w1_words, w1_s
         def rows_by_four(rows):
             return rows.rearrange("p t (c i) -> p c t i", i=4)
 
-        def gather(s, t, first, count, rows):
-            cols = slice(first // 16, (first + count) // 16)
-            nc.vector.tensor_tensor(rows, planes[s][t][:].indirect(offs_sb[:, cols]), gate_sb[:, first : first + count], MULT)
+        def flat(grouped):
+            return grouped.rearrange("p c t -> p (c t)")
 
-        def quantize(grouped, label, tag=None):
-            width = grouped.shape[1]
-            words = keep.tile([P, width], U32, name=f"codes_{label}", tag=tag or f"codes_{label}", align_bytes=64)
-            scale_bytes = keep.tile([P, width], U8, name=f"scales_{label}", align_bytes=64)
-            nc.vector.quantize_mx(out=words[:].bitcast(FP8X4), scales=scale_bytes[:], in_=grouped.rearrange("p c t -> p (c t)"))
-            return words, scale_bytes
+        def offsets(first, count):
+            return offs_sb[:, first // OFFSETS_PER_COLUMN : (first + count) // OFFSETS_PER_COLUMN]
+
+        def gather(s, t, first, count, rows):
+            nc.vector.tensor_tensor(rows, planes[s][t][:].indirect(offsets(first, count)), gate_sb[:, first : first + count], MULT)
+
+        def scatter(window, first, values):
+            nc.vector.tensor_copy(window[:].indirect(offsets(first, values.shape[1])), values)
 
         def interleave(rows, label, tag=None):
             grouped = keep.tile([P, rows.shape[2], PACK], BF16, name=f"gi_{label}", tag=tag or f"gi_{label}", align_bytes=64)
             nc.scalar.copy(by_four(grouped[:]), rows_by_four(rows))
             return grouped[:]
+
+        def quantize(grouped, label, tag=None):
+            width = grouped.shape[1]
+            words = keep.tile([P, width], U32, name=f"codes_{label}", tag=tag or f"codes_{label}", align_bytes=64)
+            scale_bytes = keep.tile([P, width], U8, name=f"scales_{label}", align_bytes=64)
+            nc.vector.quantize_mx(out=words[:].bitcast(FP8X4), scales=scale_bytes[:], in_=flat(grouped))
+            return words, scale_bytes
 
         def dh_pass(dh, e, s, operand, first):
             words, scale_bytes = operand
@@ -166,22 +189,19 @@ def tile_moe_bdx_mlp_relu_kernel(tc, dyT, a, w2_words, w2_scales, w1_words, w1_s
                     nc.tensor.transpose(turned[:, u, P * blk : P * (blk + 1)], rounded.bitcast(F32)[:, P * u : P * (u + 1)], identity[:])
             return turned
 
-        def apply_mask(da, mask, turned):
-            nc.vector.tensor_tensor(
-                da.rearrange("p r (u v) -> p r u v", u=2),
-                turned[:].rearrange("p u r -> p (u r)").bitcast(BF16).rearrange("p (u r v) -> p r u v", u=2, v=2),
-                mask.rearrange("p r (u v) -> p r u v", u=2),
-                MULT,
-            )
+        def mask_on_gpsimd(da, woven, turned, mask):
+            nc.scalar.copy(woven, turned.rearrange("p u r -> p r u"))
+            nc.gpsimd.tensor_tensor(flat(da), flat(woven).bitcast(BF16), flat(mask), MULT)
 
-        def second_product(e, b, da_q):
+        def second_product(e, b, operand):
+            words, scale_bytes = operand
             dx = psum_x.tile([P, C], F32, name="dx")
             nc.tensor.matmul_mx(
                 out=dx[:],
-                lhsT=w1_sb[:, e, 256 * b : 256 * (b + 1)].bitcast(FP4X4),
+                lhsT=w1_sb[:, e, 2 * P * b : 2 * P * (b + 1)].bitcast(FP4X4),
                 lhsT_scale=s1_sb[:, e, P * b : P * (b + 1)],
-                rhs=da_q[0][:].bitcast(FP8X4),
-                rhs_scale=da_q[1][:],
+                rhs=words[:].bitcast(FP8X4),
+                rhs_scale=scale_bytes[:],
                 start=True,
                 stop=True,
             )
@@ -191,10 +211,6 @@ def tile_moe_bdx_mlp_relu_kernel(tc, dyT, a, w2_words, w2_scales, w1_words, w1_s
             x = keep.tile([P, count], F32, name=f"x_{e}_{b}_{first}", tag=tag or f"x_{e}_{b}_{first}", align_bytes=64)
             nc.scalar.copy(x[:], dx[:, first : first + count])
             return x[:]
-
-        def scatter(window, first, values):
-            cols = slice(first // 16, (first + values.shape[1]) // 16)
-            nc.vector.tensor_copy(window[:].indirect(offs_sb[:, cols]), values)
 
         def copy_scatter(e, b):
             scatter(windows[b], C * e, copy_out(e, b, second_product(e, b, da_q[e]), 0, C))
@@ -209,7 +225,7 @@ def tile_moe_bdx_mlp_relu_kernel(tc, dyT, a, w2_words, w2_scales, w1_words, w1_s
         signs_first = keep.tile([P, 2 * C], BF16, name="signs_first", tag="signs_first", align_bytes=64)[:]
         nc.scalar.activation(
             signs_first.rearrange("p (u r v) -> p u r v", u=2, v=2),
-            a_first[0][:].rearrange("p (u v) r -> p u r v", u=2),
+            a_sb[0][0][:].rearrange("p (u v) r -> p u r v", u=2),
             SIGN,
         )
         mask_first = keep.tile([P, 2 * C], BF16, name="mask_first", tag="mask_first", align_bytes=64)
@@ -218,20 +234,21 @@ def tile_moe_bdx_mlp_relu_kernel(tc, dyT, a, w2_words, w2_scales, w1_words, w1_s
         gi01 = relay.tile([P, C, PACK], BF16, name="gi_0_1", align_bytes=64, offset=0)[:]
         nc.scalar.copy(by_four(gi01), rows_by_four(g0[:, :, C:S]))
 
-        gather(1, JOINT, 0, C + P, arena[:, HALF + JOINT * EARLY_STEP : HALF + JOINT * EARLY_STEP + C + P])
+        joint_first = HALF + JOINT * EARLY_STEP
+        gather(1, JOINT, 0, C + JOINT_EXTRA, arena[:, joint_first : joint_first + C + JOINT_EXTRA])
         for t in range(JOINT):
             gather(1, t, 0, C, early_rows[:, t, :])
         for h in range(2):
             gather(1, PACK - 1, HALF * h, HALF, early_rows[:, PACK - 1, HALF * h : HALF * (h + 1)])
         gather(1, PACK - 1, C, C, late_rows[:, PACK - 1, :])
         gi10 = [interleave(early_rows[:, :, P * blk : P * (blk + 1)], f"1_0_0_{blk}") for blk in range(2)]
-        gi10.append(interleave(early_rows[:, :, HALF:C], "1_0_1"))
+        gi10_second = interleave(early_rows[:, :, HALF:C], "1_0_1")
         q10 = [[(quantize(gi10[blk], f"1_0_0_{blk}"), 0) for blk in range(2)]]
         gather(1, 0, C, C, late_rows[:, 0, :])
-        second_half = quantize(gi10[2], "1_0_1")
-        q10.append([(second_half, 0), (second_half, P)])
+        q10_second = quantize(gi10_second, "1_0_1")
+        q10.append([(q10_second, P * blk) for blk in range(2)])
         gather(1, 1, C, C, late_rows[:, 1, :])
-        gather(1, JOINT, C + P, C - P, late_rows[:, JOINT, P:C])
+        gather(1, JOINT, C + JOINT_EXTRA, C - JOINT_EXTRA, late_rows[:, JOINT, JOINT_EXTRA:C])
 
         banks0 = [open_product(0, q00[h], 0) for h in range(2)]
         turned0 = [close_product(0, h, banks0[h], q10[h]) for h in range(2)]
@@ -242,96 +259,79 @@ def tile_moe_bdx_mlp_relu_kernel(tc, dyT, a, w2_words, w2_scales, w1_words, w1_s
             scatter(pair_windows[u], 0, pairs[0][:, HALF * u : HALF * (u + 1)])
 
         signs_second = keep.tile([P, HALF, PACK], BF16, name="signs_second", tag="rounded_0_1_0", align_bytes=64)
-        nc.scalar.activation(by_four(signs_second[:]), rows_by_four(a_first[1][:]), SIGN)
         mask_second = keep.tile([P, HALF, PACK], BF16, name="mask_second", tag="mask_second", align_bytes=64)
-        nc.scalar.activation(mask_second[:].rearrange("p c t -> p (c t)"), signs_second[:].rearrange("p c t -> p (c t)"), RELU)
-        gi11 = relay.tile([P, HALF, PACK], BF16, name="gi_1_1_0", align_bytes=64, offset=HALF * PACK)
-        nc.gpsimd.tensor_scalar(gi11[:], late_rows[:, :, 0:HALF].rearrange("p t c -> p c t"), 1.0, 0.0, MULT, ADD)
-        q11 = [quantize(gi11[:], "1_1_0")]
         da0 = [
-            keep.tile([P, HALF, PACK], BF16, name="da0_0", tag="da0_0", align_bytes=64),
+            keep.tile([P, HALF, PACK], BF16, name="da0_0", align_bytes=64),
             relay.tile([P, HALF, PACK], BF16, name="da0_1", align_bytes=64, offset=0),
         ]
-        da0_words = [half[:].rearrange("p r t -> p (r t)").bitcast(U32).rearrange("p (r u) -> p r u", u=2) for half in da0]
+        da0_words = [flat(half[:]).bitcast(U32).rearrange("p (r u) -> p r u", u=2) for half in da0]
+        woven_second = keep.tile([P, HALF, 2], F32, name="woven_second", tag="mask_first", align_bytes=64)
+        for blk in range(2):
+            cols = slice(P * blk, P * (blk + 1))
+            nc.scalar.activation(by_four(signs_second[:, cols, :]), rows_by_four(a_sb[0][1][:, :, cols]), SIGN)
+            nc.scalar.activation(flat(mask_second[:, cols, :]), flat(signs_second[:, cols, :]), RELU)
+            mask_on_gpsimd(da0[1][:, cols, :], woven_second[:, cols, :], turned0[1][:, :, cols], mask_second[:, cols, :])
         nc.scalar.copy(da0_words[0], pairs[0][:].bitcast(U32).rearrange("p (u r) -> p r u", u=2))
-        apply_mask(da0[1][:], mask_second[:], turned0[1])
         da0_codes = relay.tile([P, C], U32, name="codes_da0", align_bytes=64, offset=2 * HALF * PACK)
         da0_scales = keep.tile([P, C], U8, name="scales_da0", align_bytes=64)
         for h in range(2):
             cols = slice(HALF * h, HALF * (h + 1))
-            nc.vector.quantize_mx(out=da0_codes[:, cols].bitcast(FP8X4), scales=da0_scales[:, cols], in_=da0[h][:].rearrange("p r t -> p (r t)"))
+            nc.vector.quantize_mx(out=da0_codes[:, cols].bitcast(FP8X4), scales=da0_scales[:, cols], in_=flat(da0[h][:]))
         da_q = [(da0_codes, da0_scales)]
-        q11.append(quantize(interleave(late_rows[:, :, HALF:C], "1_1_1", tag="rounded_0_1_1"), "1_1_1", tag="da0_0"))
-        masks1 = []
-
-        def make_late_mask(h):
-            if h == 0:
-                signs = keep.tile([P, HALF, PACK], BF16, name="signs_1_0", tag="mask_first", align_bytes=64)
-            else:
-                signs = relay.tile([P, HALF, PACK], BF16, name="signs_1_1", align_bytes=64, offset=0)
-            nc.scalar.activation(by_four(signs[:]), rows_by_four(a_late[h][:]), SIGN)
-            masks1.append(keep.tile([P, HALF, PACK], BF16, name=f"mask_1_{h}", tag=("rounded_0_1_1", "signs_first")[h], align_bytes=64))
-            nc.gpsimd.tensor_scalar(masks1[h][:].rearrange("p c t -> p (c t)"), signs[:].rearrange("p c t -> p (c t)"), 1.0, 0.0, MIN, MAX)
-
-        make_late_mask(0)
+        q11 = [quantize(interleave(late_rows[:, :, HALF * h : HALF * (h + 1)], f"1_1_{h}", tag=f"rounded_0_1_{h}"), f"1_1_{h}") for h in range(2)]
         for u in range(2):
             nc.scalar.copy(pairs[1][:, HALF * u : HALF * (u + 1)].bitcast(U32), da0_words[1][:, :, u])
+
+        def late_mask(h, signs, mask_tag):
+            nc.scalar.activation(by_four(signs[:]), rows_by_four(a_sb[1][h][:]), SIGN)
+            mask = keep.tile([P, HALF, PACK], BF16, name=f"mask_1_{h}", tag=mask_tag, align_bytes=64)
+            nc.gpsimd.tensor_scalar(flat(mask[:]), flat(signs[:]), 1.0, 0.0, MIN, MAX)
+            return mask
+
+        mask_10 = late_mask(0, keep.tile([P, HALF, PACK], BF16, name="signs_1_0", tag="mask_second", align_bytes=64), "rounded_0_1_1")
         pairs_by_token = keep.tile([P, 2 * T], U32, name="pairs_by_token", tag="g0")
         for u in range(2):
             scatter(pair_windows[u], HALF, pairs[1][:, HALF * u : HALF * (u + 1)])
             nc.sync.dma_start(pairs_by_token[:, T * u : T * (u + 1)].bitcast(I32), pair_windows[u][:].bitcast(I32))
 
-        last = K_BLOCKS - 1
         da1 = keep.tile([P, C, PACK], BF16, name="da1", tag="da1", align_bytes=64)
-        for h in range(2):
-            turned = close_product(1, h, open_product(1, q01, HALF * h), [(q11[h], 0), (q11[h], P)])
-            copy_scatter(0, BY_TOKEN + h)
-            if h == 0:
-                pieces = [(0, HALF, keep.tile([P, HALF, 2], F32, name="woven_0", tag="mask_second", align_bytes=64))]
-            else:
-                pieces = [
-                    (0, P, relay.tile([P, P, 2], F32, name="woven_1_0", align_bytes=64, offset=token_offset)),
-                    (P, P, keep.tile([P, P, 2], F32, name="woven_1_1", tag="token_codes", align_bytes=64)),
-                ]
-            for first, count, woven in pieces:
-                nc.scalar.copy(woven[:], turned[:, :, first : first + count].rearrange("p u r -> p r u"))
-                nc.gpsimd.tensor_tensor(
-                    da1[:, HALF * h + first : HALF * h + first + count, :].rearrange("p c t -> p (c t)"),
-                    woven[:].rearrange("p r u -> p (r u)").bitcast(BF16),
-                    masks1[h][:, first : first + count, :].rearrange("p c t -> p (c t)"),
-                    MULT,
-                )
-            if h == 0:
-                make_late_mask(1)
+        turned_10 = close_product(1, 0, open_product(1, q01, 0), [(q11[0], P * blk) for blk in range(2)])
+        copy_scatter(0, BY_TOKEN)
+        woven_10 = keep.tile([P, HALF, 2], F32, name="woven_1_0", tag="mask_first", align_bytes=64)
+        mask_on_gpsimd(da1[:, 0:HALF, :], woven_10[:], turned_10[:], mask_10[:])
+        mask_11 = late_mask(1, relay.tile([P, HALF, PACK], BF16, name="signs_1_1", align_bytes=64, offset=0), "signs_first")
+        turned_11 = close_product(1, 1, open_product(1, q01, HALF), [(q11[1], P * blk) for blk in range(2)])
+        copy_scatter(0, BY_TOKEN + 1)
+        woven_11 = [
+            relay.tile([P, P, 2], F32, name="woven_1_1_0", align_bytes=64, offset=token_offset),
+            keep.tile([P, P, 2], F32, name="woven_1_1_1", tag="token_codes", align_bytes=64),
+        ]
+        for blk in range(2):
+            cols = slice(P * blk, P * (blk + 1))
+            mask_on_gpsimd(da1[:, HALF + P * blk : HALF + P * (blk + 1), :], woven_11[blk][:], turned_11[:, :, cols], mask_11[:, cols, :])
         dx_last = second_product(0, last, da_q[0])
-        scatter(windows[last], 0, copy_out(0, last, dx_last, 0, HALF))
+        scatter(windows[last], 0, copy_out(0, last, dx_last, 0, C - HELD))
         da_q.append(quantize(da1[:], "da1"))
-        last_half = copy_out(0, last, dx_last, HALF, HALF, tag="da1")
-
-        def store(b):
-            nc.sync.dma_start(out[P * b : P * (b + 1), :], windows[b][:])
+        held_values = copy_out(0, last, dx_last, C - HELD, HELD, tag="da1")
 
         both = pairs_by_token[:].rearrange("p (u c) -> p c u", u=2)
-        token_q = []
         token_codes = keep.tile([P, PIECES, C], U32, name="token_codes", tag="token_codes", align_bytes=64)
         token_scales = keep.tile([P, PIECES, C], U8, name="token_scales", align_bytes=64)
         by_token = relay.tile([P, PIECES, C, 2], U32, name="by_token", align_bytes=64, offset=token_offset)
         for j in range(PIECES):
-            grouped = by_token[:, j]
-            nc.scalar.copy(grouped, both[:, C * j : C * (j + 1), :])
-            nc.vector.quantize_mx(out=token_codes[:, j, :].bitcast(FP8X4), scales=token_scales[:, j, :], in_=grouped.rearrange("p c u -> p (c u)").bitcast(BF16))
-            token_q.append((token_codes[:, j, :], token_scales[:, j, :]))
-
-        scatter(windows[last], HALF, last_half)
+            nc.scalar.copy(by_token[:, j], both[:, C * j : C * (j + 1), :])
+            nc.vector.quantize_mx(out=token_codes[:, j, :].bitcast(FP8X4), scales=token_scales[:, j, :], in_=flat(by_token[:, j]).bitcast(BF16))
+        scatter(windows[last], C - HELD, held_values)
 
         def fill(b):
             windows[b] = keep.tile([P, T], F32, name=f"window_{b}", tag=f"dy_0_{b}", align_bytes=64)
             for j in range(PIECES):
-                nc.scalar.copy(windows[b][:, C * j : C * (j + 1)], second_product(0, b, token_q[j])[:])
+                dx = second_product(0, b, (token_codes[:, j, :], token_scales[:, j, :]))
+                nc.scalar.copy(windows[b][:, C * j : C * (j + 1)], dx[:])
 
         order = list(range(BY_TOKEN, K_BLOCKS)) + list(range(BY_TOKEN))
         for step, b in enumerate(order):
             copy_scatter(1, b)
-            store(b)
+            nc.sync.dma_start(out[P * b : P * (b + 1), :], windows[b][:])
             if step < BY_TOKEN:
                 fill(step)

@@ -1,7 +1,6 @@
 from contextlib import ExitStack
 
 import concourse.mybir as mybir
-from concourse.masks import make_identity
 
 K, T, E, C, H, N = 768, 1536, 2, 512, 512, 1024
 S = E * C
@@ -9,16 +8,12 @@ P = 128
 PACK = 4
 N_PASSES = N // (P * PACK)
 K_BLOCKS = K // P
-HALF = C // 2
-BY_TOKEN = 3
-PIECES = T // C
+QUARTER = C // 2
 SQUARE = 32
 OFFSETS_PER_COLUMN = 16
-EARLY_STEP = 2 * C
-LATE_STEP = 2 * C + 3 * P
-JOINT = 2
-JOINT_EXTRA = P
-HELD = 192
+VECTOR_BLOCKS = (0, 1)
+SHARED_BLOCK = 2
+SCALAR_BLOCKS = (3, 4, 5)
 
 FLOPS = 2 * S * H * (N + K)
 BYTES = 4 * N * T + 4 * H * S + E * (N * H + H * K) // 2 + E * (N * H + H * K) // 32 + 4 * S + 2 * P * S // 16 + 4 * K * T
@@ -32,10 +27,8 @@ U8 = mybir.dt.uint8
 FP4X4 = mybir.dt.float4_e2m1fn_x4
 FP8X4 = mybir.dt.float8_e5m2_x4
 MULT = mybir.AluOpType.mult
-MIN = mybir.AluOpType.min
-MAX = mybir.AluOpType.max
-SIGN = mybir.ActivationFunctionType.Sign
-RELU = mybir.ActivationFunctionType.Relu
+IS_GT = mybir.AluOpType.is_gt
+COPY = mybir.ActivationFunctionType.Copy
 
 
 def tile_moe_bdx_mlp_relu_kernel(tc, dyT, a, w2_words, w2_scales, w1_words, w1_scales, gate, offs, out):
@@ -44,93 +37,80 @@ def tile_moe_bdx_mlp_relu_kernel(tc, dyT, a, w2_words, w2_scales, w1_words, w1_s
         keep = ctx.enter_context(tc.tile_pool(name="keep", bufs=1))
         relay = ctx.enter_context(tc.tile_pool(name="relay", bufs=1))
         psum_h = ctx.enter_context(tc.psum_pool(name="psum_h", bufs=4))
-        psum_t = ctx.enter_context(tc.psum_pool(name="psum_t", bufs=2))
-        psum_x = ctx.enter_context(tc.psum_pool(name="psum_x", bufs=2))
+        psum_s = ctx.enter_context(tc.psum_pool(name="psum_s", bufs=2))
+        psum_v = ctx.enter_context(tc.psum_pool(name="psum_v", bufs=2))
 
         offs_sb = keep.tile([P, S // OFFSETS_PER_COLUMN], U16, name="offs_sb")
-        gate_first = (PACK - 1) * LATE_STEP + HALF
-        arena = keep.tile([P, PACK * LATE_STEP + P], F32, name="arena", align_bytes=64)
-        gate_sb = arena[:, gate_first : gate_first + S]
-        early_rows = arena[:, HALF : HALF + PACK * EARLY_STEP].rearrange("p (t c) -> p t c", t=PACK)[:, :, 0:C]
-        late_rows = arena[:, 0 : PACK * LATE_STEP].rearrange("p (t c) -> p t c", t=PACK)[:, :, 0:C]
-        token_offset = 2 * C * PACK
-        planes = [[keep.tile([P, T], F32, name=f"dy_0_{t}", tag=f"dy_0_{t}", align_bytes=64) for t in range(PACK)]]
-        planes.append(
-            [relay.tile([P, T], F32, name=f"dy_1_{t}", align_bytes=64, offset=token_offset + 4 * T * t) for t in range(2)]
-            + [keep.tile([P, T], F32, name=f"dy_1_{t}", align_bytes=64) for t in range(2, PACK)]
-        )
-        a_sb = [[keep.tile([P, PACK, HALF], F32, name=f"a_{e}_{h}") for h in range(2)] for e in range(E)]
-        w2_sb = [[keep.tile([P, 2 * H], U8, name=f"w2_{e}_{s}", align_bytes=64) for s in range(N_PASSES)] for e in range(E)]
-        s2_sb = keep.tile([P, E * N_PASSES, H], U8, name="s2_sb", align_bytes=64)
+        gate_sb = keep.tile([P, S], F32, name="gate_sb", align_bytes=64)
+        planes = [[keep.tile([P, T], F32, name=f"dy_{s}_{t}", align_bytes=64) for t in range(PACK)] for s in range(N_PASSES)]
+        rows = [[keep.tile([P, PACK, C], F32, name=f"rows_{s}_{e}", align_bytes=64) for e in range(E)] for s in range(N_PASSES)]
+        a_sb = [keep.tile([P, PACK, QUARTER], F32, name=f"a_{q}") for q in range(S // QUARTER)]
+        w2_raw = [keep.tile([P, N_PASSES, 2 * H], U8, name=f"w2_raw_{e}", align_bytes=64) for e in range(E)]
+        w2_sb = [keep.tile([P, N_PASSES, 2 * H], U8, name=f"w2_{e}", align_bytes=64) for e in range(E)]
+        s2_raw = keep.tile([P, E, N_PASSES * H], U8, name="s2_raw", align_bytes=64)
+        s2_sb = [keep.tile([P, N_PASSES, H], U8, name=f"s2_{e}", align_bytes=64) for e in range(E)]
         w1_sb = keep.tile([P, E, 2 * K], U8, name="w1_sb", align_bytes=64)
         s1_sb = keep.tile([P, E, K], U8, name="s1_sb", align_bytes=64)
-        windows = {b: keep.tile([P, T], F32, name=f"window_{b}") for b in range(BY_TOKEN, K_BLOCKS)}
-        pair_windows = [keep.tile([P, T], F32, name=f"pair_window_{u}") for u in range(2)]
-        identity = keep.tile([P, P], F32, name="identity")
 
-        s2_view = w2_scales.rearrange("e s f i -> f (e s) i")
-        s1_view = w1_scales.rearrange("e s f k -> f (e s) k")
         dy_view = dyT.rearrange("(s p t) c -> s t p c", p=P, t=PACK)
         a_view = a.rearrange("(p t) c -> p t c", t=PACK)
 
-        def load_a(e, h):
-            nc.sync.dma_start(a_sb[e][h][:], a_view[:, :, C * e + HALF * h : C * e + HALF * (h + 1)])
+        def load_plane(s, t):
+            nc.sync.dma_start(planes[s][t][:], dy_view[s, t])
 
-        def load_w2(e, s):
-            nc.sync.dma_start(w2_sb[e][s][:].bitcast(I32), w2_words[e, s].bitcast(I32))
+        def load_a(q):
+            nc.sync.dma_start(a_sb[q][:], a_view[:, :, QUARTER * q : QUARTER * (q + 1)])
 
-        def load_scales(scale_tile, view):
+        def load_scales(rows_sb, view):
             for q in range(4):
-                nc.sync.dma_start(scale_tile[32 * q : 32 * q + 4, :, :].bitcast(I32), view[4 * q : 4 * q + 4].bitcast(I32))
+                nc.sync.dma_start(rows_sb[32 * q : 32 * q + 4].bitcast(I32), view[4 * q : 4 * q + 4].bitcast(I32))
+
+        def load_w2(e):
+            nc.sync.dma_start(w2_raw[e][:].bitcast(I32), w2_words[e].rearrange("s p b -> p s b").bitcast(I32))
+            load_scales(s2_raw[:, e, :].rearrange("p (s i) -> p s i", s=N_PASSES), w2_scales[e].rearrange("s f i -> f s i"))
 
         gate_runs = keep.tile([P, SQUARE], F32, name="gate_runs", align_bytes=64)
         nc.sync.dma_start(gate_runs[:], gate[0 : P * SQUARE // S, :].rearrange("r (b c) -> (r b) c", c=SQUARE))
         zero = keep.tile([P, 1], F32, name="zero")
         nc.vector.memset(zero[:], 0.0)
-        nc.vector.memset(s2_sb[:].rearrange("p q i -> p (q i)").bitcast(I32), 0)
+        nc.vector.memset(s2_raw[:].rearrange("p e i -> p (e i)").bitcast(I32), 0)
         nc.vector.memset(s1_sb[:].rearrange("p e k -> p (e k)").bitcast(I32), 0)
-
-        def load_plane(s, t):
-            nc.sync.dma_start(planes[s][t][:], dy_view[s, t])
 
         load_plane(0, 0)
         nc.sync.dma_start(offs_sb[:], offs)
-        for h in range(2):
-            nc.sync.dma_start(gate_sb[:, HALF * h : HALF * (h + 1)], gate[0:P, HALF * h : HALF * (h + 1)])
-        load_plane(0, 1)
-        load_plane(0, 2)
-        load_a(0, 0)
-        load_plane(0, 3)
-        for t in (JOINT, 0, 1, PACK - 1):
+        for t in range(1, PACK):
+            load_plane(0, t)
+        load_w2(0)
+        for t in range(PACK):
             load_plane(1, t)
-        load_w2(0, 0)
-        load_scales(s2_sb, s2_view)
-        load_w2(0, 1)
-        load_a(0, 1)
-        for s in range(N_PASSES):
-            load_w2(1, s)
-        load_a(1, 0)
-        load_scales(s1_sb, s1_view)
+        load_a(0)
+        load_w2(1)
+        load_a(1)
+        load_scales(s1_sb[:], w1_scales.rearrange("e s f k -> f (e s) k"))
         nc.sync.dma_start(w1_sb[:].bitcast(I32), w1_words.rearrange("e s p b -> p (e s) b").bitcast(I32))
-        load_a(1, 1)
+        load_a(2)
+        load_a(3)
 
+        windows = {b: keep.tile([P, T], F32, name=f"window_{b}") for b in VECTOR_BLOCKS + (SHARED_BLOCK,)}
+        for b in VECTOR_BLOCKS:
+            nc.vector.memset(windows[b][:], 0.0)
+        nc.scalar.activation(windows[SHARED_BLOCK][:], zero[:].to_broadcast([P, T]), COPY)
         gate_turned = keep.tile([P, SQUARE], F32, name="gate_turned", align_bytes=64)
         nc.vector.transpose(gate_turned[:], gate_runs[:])
-        gate_spread = keep.tile([P, C // SQUARE, SQUARE], F32, name="gate_spread", align_bytes=64)
-        nc.vector.tensor_copy(gate_spread[:], gate_turned[:, C // SQUARE : S // SQUARE].unsqueeze(2).to_broadcast([P, C // SQUARE, SQUARE]))
-        nc.vector.transpose(gate_sb[:, C:S], gate_spread[:].rearrange("p b c -> p (b c)"))
-        make_identity(nc, identity[:])
-        last = K_BLOCKS - 1
-        for zeroed in pair_windows + [windows[b] for b in range(BY_TOKEN, last)]:
-            nc.scalar.activation(zeroed[:], zero[:].to_broadcast([P, T]), SIGN)
-        nc.vector.memset(windows[last][:, 0 : T // 2], 0.0)
-        nc.scalar.activation(windows[last][:, T // 2 : T], zero[:].to_broadcast([P, T // 2]), SIGN)
+        per_expert = C // SQUARE
+        for e in range(E):
+            spread = relay.tile([P, per_expert, SQUARE], F32, name=f"spread_{e}", align_bytes=64, offset=4 * T * (e + 1) - 2 * C)
+            nc.vector.tensor_copy(spread[:], gate_turned[:, per_expert * e : per_expert * (e + 1)].unsqueeze(2).to_broadcast([P, per_expert, SQUARE]))
+            nc.vector.transpose(gate_sb[:, C * e : C * (e + 1)], spread[:].rearrange("p b c -> p (b c)"))
+        for j, b in enumerate(SCALAR_BLOCKS):
+            windows[b] = relay.tile([P, T], F32, name=f"window_{b}", align_bytes=64, offset=4 * T * j)
+            nc.gpsimd.memset(windows[b][:], 0.0)
 
         def by_four(grouped):
             return grouped.rearrange("p (c i) t -> p c t i", i=4)
 
-        def rows_by_four(rows):
-            return rows.rearrange("p t (c i) -> p c t i", i=4)
+        def rows_by_four(some_rows):
+            return some_rows.rearrange("p t (c i) -> p c t i", i=4)
 
         def flat(grouped):
             return grouped.rearrange("p c t -> p (c t)")
@@ -138,200 +118,153 @@ def tile_moe_bdx_mlp_relu_kernel(tc, dyT, a, w2_words, w2_scales, w1_words, w1_s
         def offsets(first, count):
             return offs_sb[:, first // OFFSETS_PER_COLUMN : (first + count) // OFFSETS_PER_COLUMN]
 
-        def gather(s, t, first, count, rows):
-            nc.vector.tensor_tensor(rows, planes[s][t][:].indirect(offsets(first, count)), gate_sb[:, first : first + count], MULT)
+        def gather_gated(s, t, first, count):
+            nc.vector.tensor_tensor(
+                rows[s][0][:, t, first : first + count], planes[s][t][:].indirect(offsets(first, count)), gate_sb[:, first : first + count], MULT
+            )
 
-        def scatter(window, first, values):
-            nc.vector.tensor_copy(window[:].indirect(offsets(first, values.shape[1])), values)
+        def gather_plain(s, t):
+            nc.scalar.activation(rows[s][1][:, t, :], planes[s][t][:].indirect(offsets(C, C)), COPY)
 
-        def interleave(rows, label, tag=None):
-            grouped = keep.tile([P, rows.shape[2], PACK], BF16, name=f"gi_{label}", tag=tag or f"gi_{label}", align_bytes=64)
-            nc.scalar.copy(by_four(grouped[:]), rows_by_four(rows))
-            return grouped[:]
+        def quantize(grouped, words, scale_bytes):
+            nc.vector.quantize_mx(out=words.bitcast(FP8X4), scales=scale_bytes, in_=flat(grouped))
 
-        def quantize(grouped, label, tag=None):
-            width = grouped.shape[1]
-            words = keep.tile([P, width], U32, name=f"codes_{label}", tag=tag or f"codes_{label}", align_bytes=64)
-            scale_bytes = keep.tile([P, width], U8, name=f"scales_{label}", align_bytes=64)
-            nc.vector.quantize_mx(out=words[:].bitcast(FP8X4), scales=scale_bytes[:], in_=flat(grouped))
+        def g_codes(s, q):
+            e, h = divmod(q, 2)
+            grouped = keep.tile([P, QUARTER, PACK], BF16, name=f"gi_{s}_{q}", align_bytes=64)
+            some_rows = rows[s][e][:, :, QUARTER * h : QUARTER * (h + 1)]
+            if e == 0:
+                nc.scalar.copy(by_four(grouped[:]), rows_by_four(some_rows))
+            else:
+                gates = gate_sb[:, QUARTER * q : QUARTER * (q + 1)].rearrange("p (c i) -> p c i", i=4)
+                nc.vector.tensor_tensor(
+                    by_four(grouped[:]), rows_by_four(some_rows), gates.unsqueeze(2).to_broadcast([P, QUARTER // 4, PACK, 4]), MULT
+                )
+            words = keep.tile([P, QUARTER], U32, name=f"codes_{s}_{q}", align_bytes=64)
+            scale_bytes = keep.tile([P, QUARTER], U8, name=f"scales_{s}_{q}", align_bytes=64)
+            quantize(grouped[:], words[:], scale_bytes[:])
             return words, scale_bytes
+
+        def permute_w2(e):
+            nc.scalar.copy(
+                w2_sb[e][:].bitcast(U16).rearrange("p s (t c i) -> p s c t i", t=PACK, i=8),
+                w2_raw[e][:].bitcast(U16).rearrange("p s (c i t) -> p s c t i", t=PACK, i=8),
+            )
+            nc.vector.tensor_copy(
+                s2_sb[e][:].rearrange("p s (t c i) -> p s c t i", t=PACK, i=16),
+                s2_raw[:, e, :].rearrange("p (s c i t) -> p s c t i", s=N_PASSES, t=PACK, i=16),
+            )
 
         def dh_pass(dh, e, s, operand, first):
             words, scale_bytes = operand
-            nc.tensor.matmul_mx(
-                out=dh[:],
-                lhsT=words[:, first : first + P].bitcast(FP8X4),
-                lhsT_scale=scale_bytes[:, first : first + P],
-                rhs=w2_sb[e][s][:].bitcast(FP4X4),
-                rhs_scale=s2_sb[:, N_PASSES * e + s, :],
-                start=(s == 0),
-                stop=(s == N_PASSES - 1),
+            for t in range(PACK):
+                nc.tensor.matmul_mx(
+                    out=dh[:, t, :],
+                    lhsT=w2_sb[e][:, s, 2 * P * t : 2 * P * (t + 1)].bitcast(FP4X4),
+                    lhsT_scale=s2_sb[e][:, s, P * t : P * (t + 1)],
+                    rhs=words[:, first : first + P].bitcast(FP8X4),
+                    rhs_scale=scale_bytes[:, first : first + P],
+                    start=(s == 0 and t == 0),
+                    stop=(s == N_PASSES - 1 and t == PACK - 1),
+                )
+
+        def mask(da, dh, q, first):
+            nc.vector.scalar_tensor_tensor(
+                da[:, first : first + P, :],
+                a_sb[q][:, :, first : first + P].rearrange("p t c -> p c t"),
+                0.0,
+                dh[:].rearrange("p t c -> p c t"),
+                IS_GT,
+                MULT,
             )
 
-        def open_product(e, operand, first):
-            banks = []
-            for blk in range(2):
-                dh = psum_h.tile([P, H], F32, name="dh")
-                dh_pass(dh, e, 0, operand, first + P * blk)
-                banks.append(dh)
-            return banks
-
-        def close_product(e, h, banks, operands):
-            turned = psum_t.tile([P, 2, HALF], F32, name="turned")
-            for blk, dh in enumerate(banks):
-                dh_pass(dh, e, 1, *operands[blk])
-                rounded = keep.tile([P, H], BF16, name=f"rounded_{e}_{h}_{blk}", tag=f"rounded_{e}_{h}_{blk}", align_bytes=64)[:]
-                nc.scalar.copy(
-                    rounded.rearrange("r (u p v) -> r u p v", u=2, v=2),
-                    dh[:].rearrange("r (p u v) -> r u p v", u=2, v=2),
-                )
-                for u in range(2):
-                    nc.tensor.transpose(turned[:, u, P * blk : P * (blk + 1)], rounded.bitcast(F32)[:, P * u : P * (u + 1)], identity[:])
-            return turned
-
-        def mask_on_gpsimd(da, woven, turned, mask):
-            nc.scalar.copy(woven, turned.rearrange("p u r -> p r u"))
-            nc.gpsimd.tensor_tensor(flat(da), flat(woven).bitcast(BF16), flat(mask), MULT)
-
-        def second_product(e, b, operand):
-            words, scale_bytes = operand
-            dx = psum_x.tile([P, C], F32, name="dx")
+        def second_product(dx, e, b, first, count):
             nc.tensor.matmul_mx(
-                out=dx[:],
+                out=dx,
                 lhsT=w1_sb[:, e, 2 * P * b : 2 * P * (b + 1)].bitcast(FP4X4),
                 lhsT_scale=s1_sb[:, e, P * b : P * (b + 1)],
-                rhs=words[:].bitcast(FP8X4),
-                rhs_scale=scale_bytes[:],
+                rhs=da_codes[e][:, first : first + count].bitcast(FP8X4),
+                rhs_scale=da_scales[e][:, first : first + count],
                 start=True,
                 stop=True,
             )
-            return dx
 
-        def copy_out(e, b, dx, first, count, tag=None):
-            x = keep.tile([P, count], F32, name=f"x_{e}_{b}_{first}", tag=tag or f"x_{e}_{b}_{first}", align_bytes=64)
-            nc.scalar.copy(x[:], dx[:, first : first + count])
-            return x[:]
+        def scatter_scalar(b, first, values):
+            nc.scalar.activation(windows[b][:].indirect(offsets(first, values.shape[1])), values, COPY)
 
-        def copy_scatter(e, b):
-            scatter(windows[b], C * e, copy_out(e, b, second_product(e, b, da_q[e]), 0, C))
-
-        g0 = keep.tile([P, PACK, S], F32, name="g0", tag="g0")
-        gather(0, 0, 0, HALF, g0[:, 0, 0:HALF])
-        gather(0, 0, HALF, S - HALF, g0[:, 0, HALF:S])
-        for t in range(1, PACK - 1):
-            gather(0, t, 0, S, g0[:, t, :])
-        for e in range(E):
-            gather(0, PACK - 1, C * e, C, g0[:, PACK - 1, C * e : C * (e + 1)])
-        signs_first = keep.tile([P, 2 * C], BF16, name="signs_first", tag="signs_first", align_bytes=64)[:]
-        nc.scalar.activation(
-            signs_first.rearrange("p (u r v) -> p u r v", u=2, v=2),
-            a_sb[0][0][:].rearrange("p (u v) r -> p u r v", u=2),
-            SIGN,
-        )
-        mask_first = keep.tile([P, 2 * C], BF16, name="mask_first", tag="mask_first", align_bytes=64)
-        nc.scalar.activation(mask_first[:], signs_first, RELU)
-        q00 = [quantize(interleave(g0[:, :, HALF * h : HALF * (h + 1)], f"0_0_{h}"), f"0_0_{h}") for h in range(2)]
-        gi01 = relay.tile([P, C, PACK], BF16, name="gi_0_1", align_bytes=64, offset=0)[:]
-        nc.scalar.copy(by_four(gi01), rows_by_four(g0[:, :, C:S]))
-
-        joint_first = HALF + JOINT * EARLY_STEP
-        gather(1, JOINT, 0, C + JOINT_EXTRA, arena[:, joint_first : joint_first + C + JOINT_EXTRA])
-        for t in range(JOINT):
-            gather(1, t, 0, C, early_rows[:, t, :])
-        for h in range(2):
-            gather(1, PACK - 1, HALF * h, HALF, early_rows[:, PACK - 1, HALF * h : HALF * (h + 1)])
-        gather(1, PACK - 1, C, C, late_rows[:, PACK - 1, :])
-        gi10 = [interleave(early_rows[:, :, P * blk : P * (blk + 1)], f"1_0_0_{blk}") for blk in range(2)]
-        gi10_second = interleave(early_rows[:, :, HALF:C], "1_0_1")
-        q10 = [[(quantize(gi10[blk], f"1_0_0_{blk}"), 0) for blk in range(2)]]
-        gather(1, 0, C, C, late_rows[:, 0, :])
-        q10_second = quantize(gi10_second, "1_0_1")
-        q10.append([(q10_second, P * blk) for blk in range(2)])
-        gather(1, 1, C, C, late_rows[:, 1, :])
-        gather(1, JOINT, C + JOINT_EXTRA, C - JOINT_EXTRA, late_rows[:, JOINT, JOINT_EXTRA:C])
-
-        banks0 = [open_product(0, q00[h], 0) for h in range(2)]
-        turned0 = [close_product(0, h, banks0[h], q10[h]) for h in range(2)]
-        pairs = [keep.tile([P, C], F32, name=f"pairs_{h}", align_bytes=64) for h in range(2)]
-        nc.vector.tensor_tensor(pairs[0][:].bitcast(BF16), turned0[0][:].rearrange("p u r -> p (u r)").bitcast(BF16), mask_first[:], MULT)
-        q01 = quantize(gi01, "0_1", tag="rounded_0_0_1")
-        for u in range(2):
-            scatter(pair_windows[u], 0, pairs[0][:, HALF * u : HALF * (u + 1)])
-
-        signs_second = keep.tile([P, HALF, PACK], BF16, name="signs_second", tag="rounded_0_1_0", align_bytes=64)
-        mask_second = keep.tile([P, HALF, PACK], BF16, name="mask_second", tag="mask_second", align_bytes=64)
-        da0 = [
-            keep.tile([P, HALF, PACK], BF16, name="da0_0", align_bytes=64),
-            relay.tile([P, HALF, PACK], BF16, name="da0_1", align_bytes=64, offset=0),
-        ]
-        da0_words = [flat(half[:]).bitcast(U32).rearrange("p (r u) -> p r u", u=2) for half in da0]
-        woven_second = keep.tile([P, HALF, 2], F32, name="woven_second", tag="mask_first", align_bytes=64)
-        for blk in range(2):
-            cols = slice(P * blk, P * (blk + 1))
-            nc.scalar.activation(by_four(signs_second[:, cols, :]), rows_by_four(a_sb[0][1][:, :, cols]), SIGN)
-            nc.scalar.activation(flat(mask_second[:, cols, :]), flat(signs_second[:, cols, :]), RELU)
-            mask_on_gpsimd(da0[1][:, cols, :], woven_second[:, cols, :], turned0[1][:, :, cols], mask_second[:, cols, :])
-        nc.scalar.copy(da0_words[0], pairs[0][:].bitcast(U32).rearrange("p (u r) -> p r u", u=2))
-        da0_codes = relay.tile([P, C], U32, name="codes_da0", align_bytes=64, offset=2 * HALF * PACK)
-        da0_scales = keep.tile([P, C], U8, name="scales_da0", align_bytes=64)
-        for h in range(2):
-            cols = slice(HALF * h, HALF * (h + 1))
-            nc.vector.quantize_mx(out=da0_codes[:, cols].bitcast(FP8X4), scales=da0_scales[:, cols], in_=flat(da0[h][:]))
-        da_q = [(da0_codes, da0_scales)]
-        q11 = [quantize(interleave(late_rows[:, :, HALF * h : HALF * (h + 1)], f"1_1_{h}", tag=f"rounded_0_1_{h}"), f"1_1_{h}") for h in range(2)]
-        for u in range(2):
-            nc.scalar.copy(pairs[1][:, HALF * u : HALF * (u + 1)].bitcast(U32), da0_words[1][:, :, u])
-
-        def late_mask(h, signs, mask_tag):
-            nc.scalar.activation(by_four(signs[:]), rows_by_four(a_sb[1][h][:]), SIGN)
-            mask = keep.tile([P, HALF, PACK], BF16, name=f"mask_1_{h}", tag=mask_tag, align_bytes=64)
-            nc.gpsimd.tensor_scalar(flat(mask[:]), flat(signs[:]), 1.0, 0.0, MIN, MAX)
-            return mask
-
-        mask_10 = late_mask(0, keep.tile([P, HALF, PACK], BF16, name="signs_1_0", tag="mask_second", align_bytes=64), "rounded_0_1_1")
-        pairs_by_token = keep.tile([P, 2 * T], U32, name="pairs_by_token", tag="g0")
-        for u in range(2):
-            scatter(pair_windows[u], HALF, pairs[1][:, HALF * u : HALF * (u + 1)])
-            nc.sync.dma_start(pairs_by_token[:, T * u : T * (u + 1)].bitcast(I32), pair_windows[u][:].bitcast(I32))
-
-        da1 = keep.tile([P, C, PACK], BF16, name="da1", tag="da1", align_bytes=64)
-        turned_10 = close_product(1, 0, open_product(1, q01, 0), [(q11[0], P * blk) for blk in range(2)])
-        copy_scatter(0, BY_TOKEN)
-        woven_10 = keep.tile([P, HALF, 2], F32, name="woven_1_0", tag="mask_first", align_bytes=64)
-        mask_on_gpsimd(da1[:, 0:HALF, :], woven_10[:], turned_10[:], mask_10[:])
-        mask_11 = late_mask(1, relay.tile([P, HALF, PACK], BF16, name="signs_1_1", align_bytes=64, offset=0), "signs_first")
-        turned_11 = close_product(1, 1, open_product(1, q01, HALF), [(q11[1], P * blk) for blk in range(2)])
-        copy_scatter(0, BY_TOKEN + 1)
-        woven_11 = [
-            relay.tile([P, P, 2], F32, name="woven_1_1_0", align_bytes=64, offset=token_offset),
-            keep.tile([P, P, 2], F32, name="woven_1_1_1", tag="token_codes", align_bytes=64),
-        ]
-        for blk in range(2):
-            cols = slice(P * blk, P * (blk + 1))
-            mask_on_gpsimd(da1[:, HALF + P * blk : HALF + P * (blk + 1), :], woven_11[blk][:], turned_11[:, :, cols], mask_11[:, cols, :])
-        dx_last = second_product(0, last, da_q[0])
-        scatter(windows[last], 0, copy_out(0, last, dx_last, 0, C - HELD))
-        da_q.append(quantize(da1[:], "da1"))
-        held_values = copy_out(0, last, dx_last, C - HELD, HELD, tag="da1")
-
-        both = pairs_by_token[:].rearrange("p (u c) -> p c u", u=2)
-        token_codes = keep.tile([P, PIECES, C], U32, name="token_codes", tag="token_codes", align_bytes=64)
-        token_scales = keep.tile([P, PIECES, C], U8, name="token_scales", align_bytes=64)
-        by_token = relay.tile([P, PIECES, C, 2], U32, name="by_token", align_bytes=64, offset=token_offset)
-        for j in range(PIECES):
-            nc.scalar.copy(by_token[:, j], both[:, C * j : C * (j + 1), :])
-            nc.vector.quantize_mx(out=token_codes[:, j, :].bitcast(FP8X4), scales=token_scales[:, j, :], in_=flat(by_token[:, j]).bitcast(BF16))
-        scatter(windows[last], C - HELD, held_values)
-
-        def fill(b):
-            windows[b] = keep.tile([P, T], F32, name=f"window_{b}", tag=f"dy_0_{b}", align_bytes=64)
-            for j in range(PIECES):
-                dx = second_product(0, b, (token_codes[:, j, :], token_scales[:, j, :]))
-                nc.scalar.copy(windows[b][:, C * j : C * (j + 1)], dx[:])
-
-        order = list(range(BY_TOKEN, K_BLOCKS)) + list(range(BY_TOKEN))
-        for step, b in enumerate(order):
-            copy_scatter(1, b)
+        def store(b):
             nc.sync.dma_start(out[P * b : P * (b + 1), :], windows[b][:])
-            if step < BY_TOKEN:
-                fill(step)
+
+        codes = []
+        for s in range(N_PASSES):
+            for t in range(PACK - 1):
+                gather_gated(s, t, 0, C)
+                gather_plain(s, t)
+            for h in range(2):
+                gather_gated(s, PACK - 1, QUARTER * h, QUARTER)
+            first_codes = [g_codes(s, q) for q in range(2)]
+            gather_plain(s, PACK - 1)
+            if s == 0:
+                codes.append(first_codes + [g_codes(s, q) for q in range(2, 4)])
+                permute_w2(0)
+                banks = [psum_h.tile([P, PACK, P], F32, name="dh") for blk in range(4)]
+                for blk, dh in enumerate(banks):
+                    dh_pass(dh, 0, 0, first_codes[blk // 2], P * (blk % 2))
+            else:
+                codes.append(first_codes)
+
+        permute_w2(1)
+        da_codes = [keep.tile([P, C], U32, name=f"codes_da_{e}", align_bytes=64) for e in range(E)]
+        da_scales = [keep.tile([P, C], U8, name=f"scales_da_{e}", align_bytes=64) for e in range(E)]
+
+        early_blocks = (SHARED_BLOCK,) + SCALAR_BLOCKS
+        for h in range(2):
+            da = keep.tile([P, QUARTER, PACK], BF16, name=f"da_0_{h}", align_bytes=64)
+            for j in range(2):
+                dh_pass(banks[2 * h + j], 0, 1, codes[1][h], P * j)
+                mask(da, banks[2 * h + j], h, P * j)
+            cols = slice(QUARTER * h, QUARTER * (h + 1))
+            quantize(da[:], da_codes[0][:, cols], da_scales[0][:, cols])
+            staged = []
+            for pair in range(2):
+                dx = psum_s.tile([P, 2, QUARTER], F32, name="dx_s")
+                for j in range(2):
+                    second_product(dx[:, j, :], 0, early_blocks[2 * pair + j], QUARTER * h, QUARTER)
+                x = keep.tile([P, 2, QUARTER], F32, name=f"x_early_{h}_{pair}", align_bytes=64)
+                nc.scalar.copy(x[:], dx[:])
+                staged.append(x)
+            for j, b in enumerate(early_blocks):
+                scatter_scalar(b, QUARTER * h, staged[j // 2][:, j % 2, :])
+
+        da = keep.tile([P, C, PACK], BF16, name="da_1", align_bytes=64)
+        for h in range(2):
+            late_codes = g_codes(1, 2 + h)
+            for j in range(2):
+                dh = psum_h.tile([P, PACK, P], F32, name="dh")
+                dh_pass(dh, 1, 0, codes[0][2 + h], P * j)
+                dh_pass(dh, 1, 1, late_codes, P * j)
+                mask(da[:, QUARTER * h : QUARTER * (h + 1), :], dh, 2 + h, P * j)
+        quantize(da[:], da_codes[1][:], da_scales[1][:])
+
+        def on_vector(e, b):
+            dx = psum_v.tile([P, C], F32, name="dx_v")
+            second_product(dx[:], e, b, 0, C)
+            x = keep.tile([P, C], F32, name=f"x_{e}_{b}", align_bytes=64)
+            nc.vector.tensor_copy(x[:], dx[:])
+            nc.vector.tensor_copy(windows[b][:].indirect(offsets(C * e, C)), x[:])
+
+        def on_scalar(b):
+            dx = psum_s.tile([P, C], F32, name="dx_s")
+            second_product(dx[:], 1, b, 0, C)
+            x = keep.tile([P, C], F32, name=f"x_1_{b}", align_bytes=64)
+            nc.scalar.copy(x[:], dx[:])
+            for h in range(2):
+                scatter_scalar(b, C + QUARTER * h, x[:, QUARTER * h : QUARTER * (h + 1)])
+
+        for b in VECTOR_BLOCKS:
+            on_vector(0, b)
+        for vector_block, scalar_block in zip((SHARED_BLOCK,) + VECTOR_BLOCKS, SCALAR_BLOCKS):
+            on_vector(1, vector_block)
+            store(vector_block)
+            on_scalar(scalar_block)
+            store(scalar_block)

@@ -1,6 +1,7 @@
 from contextlib import ExitStack
 
 import concourse.mybir as mybir
+from concourse.masks import make_identity
 
 K, T, E, C, H, N = 768, 1536, 2, 512, 512, 1024
 S = E * C
@@ -9,11 +10,11 @@ PACK = 4
 N_PASSES = N // (P * PACK)
 K_BLOCKS = K // P
 QUARTER = C // 2
-SQUARE = 32
 OFFSETS_PER_COLUMN = 16
 VECTOR_BLOCKS = (0, 1)
 SHARED_BLOCK = 2
 SCALAR_BLOCKS = (3, 4, 5)
+FREE_ROWS = 1
 
 FLOPS = 2 * S * H * (N + K)
 BYTES = 4 * N * T + 4 * H * S + E * (N * H + H * K) // 2 + E * (N * H + H * K) // 32 + 4 * S + 2 * P * S // 16 + 4 * K * T
@@ -43,12 +44,23 @@ def tile_moe_bdx_mlp_relu_kernel(tc, dyT, a, w2_words, w2_scales, w1_words, w1_s
         offs_sb = keep.tile([P, S // OFFSETS_PER_COLUMN], U16, name="offs_sb")
         gate_sb = keep.tile([P, S], F32, name="gate_sb", align_bytes=64)
         planes = [[keep.tile([P, T], F32, name=f"dy_{s}_{t}", align_bytes=64) for t in range(PACK)] for s in range(N_PASSES)]
-        rows = [[keep.tile([P, PACK, C], F32, name=f"rows_{s}_{e}", align_bytes=64) for e in range(E)] for s in range(N_PASSES)]
+        rows_offset = len(SCALAR_BLOCKS) * 4 * T
+        rows = [[relay.tile([P, PACK, C], F32, name=f"rows_0_{e}", align_bytes=64, offset=rows_offset + 4 * PACK * C * e)[:] for e in range(E)]]
+        arena = relay.tile([P, PACK + FREE_ROWS, C], F32, name="arena", align_bytes=64, offset=rows_offset + 2 * PACK * C)
+        rows.append([arena[:, FREE_ROWS : FREE_ROWS + PACK, :], arena[:, 0:PACK, :]])
+        g_codes = {}
         a_sb = [keep.tile([P, PACK, QUARTER], F32, name=f"a_{q}") for q in range(S // QUARTER)]
-        w2_raw = [keep.tile([P, N_PASSES, 2 * H], U8, name=f"w2_raw_{e}", align_bytes=64) for e in range(E)]
-        w2_sb = [keep.tile([P, N_PASSES, 2 * H], U8, name=f"w2_{e}", align_bytes=64) for e in range(E)]
-        s2_raw = keep.tile([P, E, N_PASSES * H], U8, name="s2_raw", align_bytes=64)
-        s2_sb = [keep.tile([P, N_PASSES, H], U8, name=f"s2_{e}", align_bytes=64) for e in range(E)]
+        w2_raw = [
+            relay.tile([P, N_PASSES, 2 * H], U8, name="w2_raw_0", align_bytes=64, offset=2 * 4 * T + 2 * H),
+            keep.tile([P, N_PASSES, 2 * H], U8, name="w2_raw_1", align_bytes=64),
+        ]
+        w2_offset = rows_offset + E * 4 * PACK * C
+        w2_sb = [
+            relay.tile([P, N_PASSES, 2 * H], U8, name="w2_0", align_bytes=64, offset=w2_offset),
+            keep.tile([P, N_PASSES, 2 * H], U8, name="w2_1", align_bytes=64),
+        ]
+        s2_raw = relay.tile([P, E * N_PASSES, H], U8, name="s2_raw", align_bytes=64, offset=4 * T - 2 * H)
+        s2_sb = keep.tile([P, E * N_PASSES, H], U8, name="s2_sb", align_bytes=64)
         w1_sb = keep.tile([P, E, 2 * K], U8, name="w1_sb", align_bytes=64)
         s1_sb = keep.tile([P, E, K], U8, name="s1_sb", align_bytes=64)
 
@@ -67,44 +79,42 @@ def tile_moe_bdx_mlp_relu_kernel(tc, dyT, a, w2_words, w2_scales, w1_words, w1_s
 
         def load_w2(e):
             nc.sync.dma_start(w2_raw[e][:].bitcast(I32), w2_words[e].rearrange("s p b -> p s b").bitcast(I32))
-            load_scales(s2_raw[:, e, :].rearrange("p (s i) -> p s i", s=N_PASSES), w2_scales[e].rearrange("s f i -> f s i"))
 
-        gate_runs = keep.tile([P, SQUARE], F32, name="gate_runs", align_bytes=64)
-        nc.sync.dma_start(gate_runs[:], gate[0 : P * SQUARE // S, :].rearrange("r (b c) -> (r b) c", c=SQUARE))
+        gate_runs = relay.tile([P, E, 2 * PACK], F32, name="gate_runs", offset=w2_offset - 4 * 2 * PACK)
+        nc.sync.dma_start(gate_runs[:, :, 0:PACK], gate[0:1, :].rearrange("r (e p i) -> p (r e) i", e=E, i=PACK))
         zero = keep.tile([P, 1], F32, name="zero")
         nc.vector.memset(zero[:], 0.0)
-        nc.vector.memset(s2_raw[:].rearrange("p e i -> p (e i)").bitcast(I32), 0)
+        nc.vector.memset(s2_raw[:].rearrange("p q i -> p (q i)").bitcast(I32), 0)
         nc.vector.memset(s1_sb[:].rearrange("p e k -> p (e k)").bitcast(I32), 0)
 
         load_plane(0, 0)
         nc.sync.dma_start(offs_sb[:], offs)
+        load_scales(s2_raw[:], w2_scales.rearrange("e s f i -> f (e s) i"))
+        load_w2(0)
         for t in range(1, PACK):
             load_plane(0, t)
-        load_w2(0)
         for t in range(PACK):
             load_plane(1, t)
         load_a(0)
         load_w2(1)
-        load_a(1)
         load_scales(s1_sb[:], w1_scales.rearrange("e s f k -> f (e s) k"))
         nc.sync.dma_start(w1_sb[:].bitcast(I32), w1_words.rearrange("e s p b -> p (e s) b").bitcast(I32))
+        load_a(1)
         load_a(2)
         load_a(3)
 
         windows = {b: keep.tile([P, T], F32, name=f"window_{b}") for b in VECTOR_BLOCKS + (SHARED_BLOCK,)}
         for b in VECTOR_BLOCKS:
             nc.vector.memset(windows[b][:], 0.0)
-        nc.scalar.activation(windows[SHARED_BLOCK][:], zero[:].to_broadcast([P, T]), COPY)
-        gate_turned = keep.tile([P, SQUARE], F32, name="gate_turned", align_bytes=64)
-        nc.vector.transpose(gate_turned[:], gate_runs[:])
-        per_expert = C // SQUARE
+        identity = keep.tile([P, P], F32, name="identity")
+        make_identity(nc, identity[:])
+        nc.scalar.activation(windows[SHARED_BLOCK][:, 0:C], zero[:].to_broadcast([P, C]), COPY)
+        nc.gpsimd.memset(windows[SHARED_BLOCK][:, C:T], 0.0)
         for e in range(E):
-            spread = relay.tile([P, per_expert, SQUARE], F32, name=f"spread_{e}", align_bytes=64, offset=4 * T * (e + 1) - 2 * C)
-            nc.vector.tensor_copy(spread[:], gate_turned[:, per_expert * e : per_expert * (e + 1)].unsqueeze(2).to_broadcast([P, per_expert, SQUARE]))
-            nc.vector.transpose(gate_sb[:, C * e : C * (e + 1)], spread[:].rearrange("p b c -> p (b c)"))
-        for j, b in enumerate(SCALAR_BLOCKS):
-            windows[b] = relay.tile([P, T], F32, name=f"window_{b}", align_bytes=64, offset=4 * T * j)
-            nc.gpsimd.memset(windows[b][:], 0.0)
+            spread = psum_s.tile([P, PACK, P], F32, name="dx_s")
+            for i in range(PACK):
+                nc.tensor.transpose(spread[:, i, :], gate_runs[:, e, i : i + 1].to_broadcast([P, P]), identity[:])
+            nc.scalar.copy(gate_sb[:, C * e : C * (e + 1)].rearrange("p (n i) -> p n i", i=PACK), spread[:].rearrange("p i n -> p n i"))
 
         def by_four(grouped):
             return grouped.rearrange("p (c i) t -> p c t i", i=4)
@@ -123,49 +133,49 @@ def tile_moe_bdx_mlp_relu_kernel(tc, dyT, a, w2_words, w2_scales, w1_words, w1_s
                 rows[s][0][:, t, first : first + count], planes[s][t][:].indirect(offsets(first, count)), gate_sb[:, first : first + count], MULT
             )
 
-        def gather_plain(s, t):
-            nc.scalar.activation(rows[s][1][:, t, :], planes[s][t][:].indirect(offsets(C, C)), COPY)
+        def gather_plain(s, t, first, count):
+            e, col = divmod(first, C)
+            nc.scalar.activation(rows[s][e][:, t, col : col + count], planes[s][t][:].indirect(offsets(first, count)), COPY)
 
         def quantize(grouped, words, scale_bytes):
             nc.vector.quantize_mx(out=words.bitcast(FP8X4), scales=scale_bytes, in_=flat(grouped))
 
-        def g_codes(s, q):
-            e, h = divmod(q, 2)
-            grouped = keep.tile([P, QUARTER, PACK], BF16, name=f"gi_{s}_{q}", align_bytes=64)
-            some_rows = rows[s][e][:, :, QUARTER * h : QUARTER * (h + 1)]
-            if e == 0:
-                nc.scalar.copy(by_four(grouped[:]), rows_by_four(some_rows))
+        def interleave(s, first, count, gated, tag=None):
+            e, col = divmod(first, C)
+            grouped = keep.tile([P, count, PACK], BF16, name=f"g_grouped_{s}_{first}", tag=tag or f"g_grouped_{s}_{first}", align_bytes=64)
+            some_rows = rows_by_four(rows[s][e][:, :, col : col + count])
+            if gated:
+                nc.scalar.copy(by_four(grouped[:]), some_rows)
             else:
-                gates = gate_sb[:, QUARTER * q : QUARTER * (q + 1)].rearrange("p (c i) -> p c i", i=4)
-                nc.vector.tensor_tensor(
-                    by_four(grouped[:]), rows_by_four(some_rows), gates.unsqueeze(2).to_broadcast([P, QUARTER // 4, PACK, 4]), MULT
-                )
-            words = keep.tile([P, QUARTER], U32, name=f"codes_{s}_{q}", align_bytes=64)
-            scale_bytes = keep.tile([P, QUARTER], U8, name=f"scales_{s}_{q}", align_bytes=64)
-            quantize(grouped[:], words[:], scale_bytes[:])
-            return words, scale_bytes
+                gates = gate_sb[:, first : first + count].rearrange("p (c i) -> p c i", i=4)
+                nc.vector.tensor_tensor(by_four(grouped[:]), some_rows, gates.unsqueeze(2).to_broadcast([P, count // 4, PACK, 4]), MULT)
+            return grouped[:]
 
-        def permute_w2(e):
+        def quantize_g(s, first, grouped):
+            count = grouped.shape[1]
+            words = keep.tile([P, count], U32, name=f"g_codes_{s}_{first}", align_bytes=64)
+            scale_bytes = keep.tile([P, count], U8, name=f"g_scales_{s}_{first}", align_bytes=64)
+            quantize(grouped, words[:], scale_bytes[:])
+            for col in range(0, count, P):
+                g_codes[s, first + col] = (words[:, col : col + P], scale_bytes[:, col : col + P])
+
+        def permute_words(e):
             nc.scalar.copy(
                 w2_sb[e][:].bitcast(U16).rearrange("p s (t c i) -> p s c t i", t=PACK, i=8),
                 w2_raw[e][:].bitcast(U16).rearrange("p s (c i t) -> p s c t i", t=PACK, i=8),
             )
-            nc.vector.tensor_copy(
-                s2_sb[e][:].rearrange("p s (t c i) -> p s c t i", t=PACK, i=16),
-                s2_raw[:, e, :].rearrange("p (s c i t) -> p s c t i", s=N_PASSES, t=PACK, i=16),
-            )
 
-        def dh_pass(dh, e, s, operand, first):
-            words, scale_bytes = operand
+        def dh_pass(dh, s, first, opens):
+            e = first // C
             for t in range(PACK):
                 nc.tensor.matmul_mx(
                     out=dh[:, t, :],
                     lhsT=w2_sb[e][:, s, 2 * P * t : 2 * P * (t + 1)].bitcast(FP4X4),
-                    lhsT_scale=s2_sb[e][:, s, P * t : P * (t + 1)],
-                    rhs=words[:, first : first + P].bitcast(FP8X4),
-                    rhs_scale=scale_bytes[:, first : first + P],
-                    start=(s == 0 and t == 0),
-                    stop=(s == N_PASSES - 1 and t == PACK - 1),
+                    lhsT_scale=s2_sb[:, N_PASSES * e + s, P * t : P * (t + 1)],
+                    rhs=g_codes[s, first][0].bitcast(FP8X4),
+                    rhs_scale=g_codes[s, first][1],
+                    start=(opens and t == 0),
+                    stop=(not opens and t == PACK - 1),
                 )
 
         def mask(da, dh, q, first):
@@ -195,33 +205,46 @@ def tile_moe_bdx_mlp_relu_kernel(tc, dyT, a, w2_words, w2_scales, w1_words, w1_s
         def store(b):
             nc.sync.dma_start(out[P * b : P * (b + 1), :], windows[b][:])
 
-        codes = []
-        for s in range(N_PASSES):
-            for t in range(PACK - 1):
-                gather_gated(s, t, 0, C)
-                gather_plain(s, t)
-            for h in range(2):
-                gather_gated(s, PACK - 1, QUARTER * h, QUARTER)
-            first_codes = [g_codes(s, q) for q in range(2)]
-            gather_plain(s, PACK - 1)
-            if s == 0:
-                codes.append(first_codes + [g_codes(s, q) for q in range(2, 4)])
-                permute_w2(0)
-                banks = [psum_h.tile([P, PACK, P], F32, name="dh") for blk in range(4)]
-                for blk, dh in enumerate(banks):
-                    dh_pass(dh, 0, 0, first_codes[blk // 2], P * (blk % 2))
-            else:
-                codes.append(first_codes)
+        for t in range(PACK):
+            gather_gated(0, t, 0, C)
+            gather_plain(0, t, C, C)
+            if t == 0:
+                permute_words(0)
+                nc.vector.tensor_copy(
+                    s2_sb[:].rearrange("p q (t c i) -> p q c t i", t=PACK, i=16),
+                    s2_raw[:].rearrange("p q (c i t) -> p q c t i", t=PACK, i=16),
+                )
+                for j, b in enumerate(SCALAR_BLOCKS):
+                    windows[b] = relay.tile([P, T], F32, name=f"window_{b}", align_bytes=64, offset=4 * T * j)
+                    nc.gpsimd.memset(windows[b][:], 0.0)
+        first_pass = [interleave(0, C * e, C, e == 0) for e in range(E)]
 
-        permute_w2(1)
+        banks = [psum_h.tile([P, PACK, P], F32, name="dh") for blk in range(4)]
+        for t in range(PACK):
+            gather_gated(1, t, 0, QUARTER)
+            gather_plain(1, t, QUARTER, QUARTER)
+            if t < FREE_ROWS:
+                gather_plain(1, t, C, C)
+            if t == 0:
+                for e in range(E):
+                    quantize_g(0, C * e, first_pass[e])
+                for blk, dh in enumerate(banks):
+                    dh_pass(dh, 0, P * blk, True)
+        second_pass = [interleave(1, QUARTER * h, QUARTER, h == 0) for h in range(2)]
+        for h in range(2):
+            quantize_g(1, QUARTER * h, second_pass[h])
+        for t in range(FREE_ROWS, PACK):
+            gather_plain(1, t, C, C)
+        permute_words(1)
+
         da_codes = [keep.tile([P, C], U32, name=f"codes_da_{e}", align_bytes=64) for e in range(E)]
         da_scales = [keep.tile([P, C], U8, name=f"scales_da_{e}", align_bytes=64) for e in range(E)]
 
         early_blocks = (SHARED_BLOCK,) + SCALAR_BLOCKS
         for h in range(2):
-            da = keep.tile([P, QUARTER, PACK], BF16, name=f"da_0_{h}", align_bytes=64)
+            da = keep.tile([P, QUARTER, PACK], BF16, name=f"da_0_{h}", tag=f"da_0_{h}", align_bytes=64)
             for j in range(2):
-                dh_pass(banks[2 * h + j], 0, 1, codes[1][h], P * j)
+                dh_pass(banks[2 * h + j], 1, QUARTER * h + P * j, False)
                 mask(da, banks[2 * h + j], h, P * j)
             cols = slice(QUARTER * h, QUARTER * (h + 1))
             quantize(da[:], da_codes[0][:, cols], da_scales[0][:, cols])
@@ -236,20 +259,21 @@ def tile_moe_bdx_mlp_relu_kernel(tc, dyT, a, w2_words, w2_scales, w1_words, w1_s
             for j, b in enumerate(early_blocks):
                 scatter_scalar(b, QUARTER * h, staged[j // 2][:, j % 2, :])
 
-        da = keep.tile([P, C, PACK], BF16, name="da_1", align_bytes=64)
+        da = keep.tile([P, C, PACK], BF16, name="da_1", tag="da_1", align_bytes=64)
+        late_pass = [interleave(1, C + QUARTER * h, QUARTER, False, tag=f"da_0_{h}") for h in range(2)]
         for h in range(2):
-            late_codes = g_codes(1, 2 + h)
-            for j in range(2):
-                dh = psum_h.tile([P, PACK, P], F32, name="dh")
-                dh_pass(dh, 1, 0, codes[0][2 + h], P * j)
-                dh_pass(dh, 1, 1, late_codes, P * j)
-                mask(da[:, QUARTER * h : QUARTER * (h + 1), :], dh, 2 + h, P * j)
+            quantize_g(1, C + QUARTER * h, late_pass[h])
+        for blk in range(4):
+            dh = psum_h.tile([P, PACK, P], F32, name="dh")
+            dh_pass(dh, 1, C + P * blk, True)
+            dh_pass(dh, 0, C + P * blk, False)
+            mask(da[:, QUARTER * (blk // 2) : QUARTER * (blk // 2 + 1), :], dh, 2 + blk // 2, P * (blk % 2))
         quantize(da[:], da_codes[1][:], da_scales[1][:])
 
-        def on_vector(e, b):
+        def on_vector(e, b, tag=None):
             dx = psum_v.tile([P, C], F32, name="dx_v")
             second_product(dx[:], e, b, 0, C)
-            x = keep.tile([P, C], F32, name=f"x_{e}_{b}", align_bytes=64)
+            x = keep.tile([P, C], F32, name=f"x_{e}_{b}", tag=tag or f"x_{e}_{b}", align_bytes=64)
             nc.vector.tensor_copy(x[:], dx[:])
             nc.vector.tensor_copy(windows[b][:].indirect(offsets(C * e, C)), x[:])
 
@@ -261,8 +285,8 @@ def tile_moe_bdx_mlp_relu_kernel(tc, dyT, a, w2_words, w2_scales, w1_words, w1_s
             for h in range(2):
                 scatter_scalar(b, C + QUARTER * h, x[:, QUARTER * h : QUARTER * (h + 1)])
 
-        for b in VECTOR_BLOCKS:
-            on_vector(0, b)
+        on_vector(0, VECTOR_BLOCKS[0])
+        on_vector(0, VECTOR_BLOCKS[1], tag="da_1")
         for vector_block, scalar_block in zip((SHARED_BLOCK,) + VECTOR_BLOCKS, SCALAR_BLOCKS):
             on_vector(1, vector_block)
             store(vector_block)

@@ -140,9 +140,9 @@ def tile_moe_bdx_mlp_relu_kernel(tc, dyT, a, w2_words, w2_scales, w1_words, w1_s
         def quantize(grouped, words, scale_bytes):
             nc.vector.quantize_mx(out=words.bitcast(FP8X4), scales=scale_bytes, in_=flat(grouped))
 
-        def interleave(s, first, count, gated, tag=None):
+        def interleave(s, first, count, gated):
             e, col = divmod(first, C)
-            grouped = keep.tile([P, count, PACK], BF16, name=f"g_grouped_{s}_{first}", tag=tag or f"g_grouped_{s}_{first}", align_bytes=64)
+            grouped = keep.tile([P, count, PACK], BF16, name=f"g_grouped_{s}_{first}", align_bytes=64)
             some_rows = rows_by_four(rows[s][e][:, :, col : col + count])
             if gated:
                 nc.scalar.copy(by_four(grouped[:]), some_rows)
@@ -151,9 +151,9 @@ def tile_moe_bdx_mlp_relu_kernel(tc, dyT, a, w2_words, w2_scales, w1_words, w1_s
                 nc.vector.tensor_tensor(by_four(grouped[:]), some_rows, gates.unsqueeze(2).to_broadcast([P, count // 4, PACK, 4]), MULT)
             return grouped[:]
 
-        def quantize_g(s, first, grouped):
+        def quantize_g(s, first, grouped, tag=None):
             count = grouped.shape[1]
-            words = keep.tile([P, count], U32, name=f"g_codes_{s}_{first}", align_bytes=64)
+            words = keep.tile([P, count], U32, name=f"g_codes_{s}_{first}", tag=tag or f"g_codes_{s}_{first}", align_bytes=64)
             scale_bytes = keep.tile([P, count], U8, name=f"g_scales_{s}_{first}", align_bytes=64)
             quantize(grouped, words[:], scale_bytes[:])
             for col in range(0, count, P):
@@ -233,21 +233,26 @@ def tile_moe_bdx_mlp_relu_kernel(tc, dyT, a, w2_words, w2_scales, w1_words, w1_s
         second_pass = [interleave(1, QUARTER * h, QUARTER, h == 0) for h in range(2)]
         for h in range(2):
             quantize_g(1, QUARTER * h, second_pass[h])
+        permute_words(1)
         for t in range(FREE_ROWS, PACK):
             gather_plain(1, t, C, C)
-        permute_words(1)
 
         da_codes = [keep.tile([P, C], U32, name=f"codes_da_{e}", align_bytes=64) for e in range(E)]
         da_scales = [keep.tile([P, C], U8, name=f"scales_da_{e}", align_bytes=64) for e in range(E)]
 
         early_blocks = (SHARED_BLOCK,) + SCALAR_BLOCKS
+        da_early = keep.tile([P, C, PACK], BF16, name="da_0", tag="da_0", align_bytes=64)
         for h in range(2):
-            da = keep.tile([P, QUARTER, PACK], BF16, name=f"da_0_{h}", tag=f"da_0_{h}", align_bytes=64)
+            da = da_early[:, QUARTER * h : QUARTER * (h + 1), :]
             for j in range(2):
                 dh_pass(banks[2 * h + j], 1, QUARTER * h + P * j, False)
                 mask(da, banks[2 * h + j], h, P * j)
             cols = slice(QUARTER * h, QUARTER * (h + 1))
-            quantize(da[:], da_codes[0][:, cols], da_scales[0][:, cols])
+            quantize(da, da_codes[0][:, cols], da_scales[0][:, cols])
+            if h == 1:
+                dx_vector = [psum_v.tile([P, C], F32, name="dx_v") for b in VECTOR_BLOCKS]
+                for b, dx in zip(VECTOR_BLOCKS, dx_vector):
+                    second_product(dx[:], 0, b, 0, C)
             staged = []
             for pair in range(2):
                 dx = psum_s.tile([P, 2, QUARTER], F32, name="dx_s")
@@ -259,23 +264,18 @@ def tile_moe_bdx_mlp_relu_kernel(tc, dyT, a, w2_words, w2_scales, w1_words, w1_s
             for j, b in enumerate(early_blocks):
                 scatter_scalar(b, QUARTER * h, staged[j // 2][:, j % 2, :])
 
-        da = keep.tile([P, C, PACK], BF16, name="da_1", tag="da_1", align_bytes=64)
-        late_pass = [interleave(1, C + QUARTER * h, QUARTER, False, tag=f"da_0_{h}") for h in range(2)]
-        for h in range(2):
-            quantize_g(1, C + QUARTER * h, late_pass[h])
-        for blk in range(4):
-            dh = psum_h.tile([P, PACK, P], F32, name="dh")
-            dh_pass(dh, 1, C + P * blk, True)
-            dh_pass(dh, 0, C + P * blk, False)
-            mask(da[:, QUARTER * (blk // 2) : QUARTER * (blk // 2 + 1), :], dh, 2 + blk // 2, P * (blk % 2))
-        quantize(da[:], da_codes[1][:], da_scales[1][:])
+        def scatter_vector(e, b, dx, first, count, tag):
+            x = keep.tile([P, count], F32, name=f"x_{e}_{b}_{first}", tag=tag, align_bytes=64)
+            nc.vector.tensor_copy(x[:], dx[:, first : first + count])
+            nc.vector.tensor_copy(windows[b][:].indirect(offsets(C * e + first, count)), x[:])
 
-        def on_vector(e, b, tag=None):
+        def on_vector(e, b, tags):
             dx = psum_v.tile([P, C], F32, name="dx_v")
-            second_product(dx[:], e, b, 0, C)
-            x = keep.tile([P, C], F32, name=f"x_{e}_{b}", tag=tag or f"x_{e}_{b}", align_bytes=64)
-            nc.vector.tensor_copy(x[:], dx[:])
-            nc.vector.tensor_copy(windows[b][:].indirect(offsets(C * e, C)), x[:])
+            count = C // len(tags)
+            for j in range(len(tags)):
+                second_product(dx[:, count * j : count * (j + 1)], e, b, count * j, count)
+            for j, tag in enumerate(tags):
+                scatter_vector(e, b, dx, count * j, count, tag)
 
         def on_scalar(b):
             dx = psum_s.tile([P, C], F32, name="dx_s")
@@ -285,10 +285,31 @@ def tile_moe_bdx_mlp_relu_kernel(tc, dyT, a, w2_words, w2_scales, w1_words, w1_s
             for h in range(2):
                 scatter_scalar(b, C + QUARTER * h, x[:, QUARTER * h : QUARTER * (h + 1)])
 
-        on_vector(0, VECTOR_BLOCKS[0])
-        on_vector(0, VECTOR_BLOCKS[1], tag="da_1")
+        da = keep.tile([P, C, PACK], BF16, name="da_1", tag="da_1", align_bytes=64)
+        late_pass = keep.tile([P, C, PACK], BF16, name="g_grouped_late", tag="da_0", align_bytes=64)
+        for h in range(2):
+            cols = slice(QUARTER * h, QUARTER * (h + 1))
+            gates = gate_sb[:, C + QUARTER * h : C + QUARTER * (h + 1)].unsqueeze(2).to_broadcast([P, QUARTER, PACK])
+            nc.gpsimd.tensor_tensor(late_pass[:, cols, :], rows[1][1][:, :, cols].rearrange("p t c -> p c t"), gates, MULT)
+        late_banks = []
+        for blk in range(4):
+            dh = psum_h.tile([P, PACK, P], F32, name="dh")
+            dh_pass(dh, 0, C + P * blk, True)
+            late_banks.append(dh)
+        scatter_vector(0, VECTOR_BLOCKS[0], dx_vector[0], 0, C, "x_first")
+        dx_held = dx_vector[1]
+        scatter_vector(0, VECTOR_BLOCKS[1], dx_held, 0, QUARTER, "x_second")
+        quantize_g(1, C, late_pass[:], tag="x_second")
+        scatter_vector(0, VECTOR_BLOCKS[1], dx_held, QUARTER, QUARTER, "da_0")
+        for h in range(2):
+            cols = slice(QUARTER * h, QUARTER * (h + 1))
+            for j in range(2):
+                dh_pass(late_banks[2 * h + j], 1, C + QUARTER * h + P * j, False)
+                mask(da[:, cols, :], late_banks[2 * h + j], 2 + h, P * j)
+            quantize(da[:, cols, :], da_codes[1][:, cols], da_scales[1][:, cols])
+
         for vector_block, scalar_block in zip((SHARED_BLOCK,) + VECTOR_BLOCKS, SCALAR_BLOCKS):
-            on_vector(1, vector_block)
+            on_vector(1, vector_block, ["da_1_a", "da_1_b"] if vector_block == SHARED_BLOCK else [f"x_late_{vector_block}"])
             store(vector_block)
             on_scalar(scalar_block)
             store(scalar_block)

@@ -203,7 +203,8 @@ def tile_moe_bdx_mlp_relu_kernel(tc, dyT, a, w2_words, w2_scales, w1_words, w1_s
             nc.scalar.activation(windows[b][:].indirect(offsets(first, values.shape[1])), values, COPY)
 
         def store(b):
-            nc.sync.dma_start(out[P * b : P * (b + 1), :], windows[b][:])
+            queue = nc.scalar if b in SCALAR_BLOCKS else nc.sync
+            queue.dma_start(out[P * b : P * (b + 1), :], windows[b][:])
 
         for t in range(PACK):
             gather_gated(0, t, 0, C)
@@ -253,37 +254,37 @@ def tile_moe_bdx_mlp_relu_kernel(tc, dyT, a, w2_words, w2_scales, w1_words, w1_s
                 dx_vector = [psum_v.tile([P, C], F32, name="dx_v") for b in VECTOR_BLOCKS]
                 for b, dx in zip(VECTOR_BLOCKS, dx_vector):
                     second_product(dx[:], 0, b, 0, C)
-            staged = []
-            for pair in range(2):
-                dx = psum_s.tile([P, 2, QUARTER], F32, name="dx_s")
-                for j in range(2):
-                    second_product(dx[:, j, :], 0, early_blocks[2 * pair + j], QUARTER * h, QUARTER)
-                x = keep.tile([P, 2, QUARTER], F32, name=f"x_early_{h}_{pair}", align_bytes=64)
+            staged = {}
+            blocks = early_blocks[h:]
+            for pair in range(0, len(blocks), 2):
+                together = blocks[pair : pair + 2]
+                dx = psum_s.tile([P, len(together), QUARTER], F32, name="dx_s")
+                for j, b in enumerate(together):
+                    second_product(dx[:, j, :], 0, b, QUARTER * h, QUARTER)
+                x = keep.tile([P, len(together), QUARTER], F32, name=f"x_early_{h}_{pair}", align_bytes=64)
                 nc.scalar.copy(x[:], dx[:])
-                staged.append(x)
-            for j, b in enumerate(early_blocks):
-                scatter_scalar(b, QUARTER * h, staged[j // 2][:, j % 2, :])
+                for j, b in enumerate(together):
+                    staged[b] = x[:, j, :]
+            for b in blocks:
+                scatter_scalar(b, QUARTER * h, staged[b])
 
         def scatter_vector(e, b, dx, first, count, tag):
             x = keep.tile([P, count], F32, name=f"x_{e}_{b}_{first}", tag=tag, align_bytes=64)
             nc.vector.tensor_copy(x[:], dx[:, first : first + count])
             nc.vector.tensor_copy(windows[b][:].indirect(offsets(C * e + first, count)), x[:])
 
-        def on_vector(e, b, tags):
+        def on_vector(b):
             dx = psum_v.tile([P, C], F32, name="dx_v")
-            count = C // len(tags)
-            for j in range(len(tags)):
-                second_product(dx[:, count * j : count * (j + 1)], e, b, count * j, count)
-            for j, tag in enumerate(tags):
-                scatter_vector(e, b, dx, count * j, count, tag)
-
-        def on_scalar(b):
-            dx = psum_s.tile([P, C], F32, name="dx_s")
             second_product(dx[:], 1, b, 0, C)
-            x = keep.tile([P, C], F32, name=f"x_1_{b}", align_bytes=64)
+            scatter_vector(1, b, dx, 0, C, f"x_late_{b}")
+
+        def on_scalar(b, first, count):
+            dx = psum_s.tile([P, count], F32, name="dx_s")
+            second_product(dx[:], 1, b, first, count)
+            x = keep.tile([P, count], F32, name=f"x_1_{b}_{first}", align_bytes=64)
             nc.scalar.copy(x[:], dx[:])
-            for h in range(2):
-                scatter_scalar(b, C + QUARTER * h, x[:, QUARTER * h : QUARTER * (h + 1)])
+            for col in range(0, count, QUARTER):
+                scatter_scalar(b, C + first + col, x[:, col : col + QUARTER])
 
         da = keep.tile([P, C, PACK], BF16, name="da_1", tag="da_1", align_bytes=64)
         late_pass = keep.tile([P, C, PACK], BF16, name="g_grouped_late", tag="da_0", align_bytes=64)
@@ -297,19 +298,24 @@ def tile_moe_bdx_mlp_relu_kernel(tc, dyT, a, w2_words, w2_scales, w1_words, w1_s
             dh_pass(dh, 0, C + P * blk, True)
             late_banks.append(dh)
         scatter_vector(0, VECTOR_BLOCKS[0], dx_vector[0], 0, C, "x_first")
-        dx_held = dx_vector[1]
-        scatter_vector(0, VECTOR_BLOCKS[1], dx_held, 0, QUARTER, "x_second")
+        dx_shared = psum_v.tile([P, C], F32, name="dx_v")
+        second_product(dx_shared[:, QUARTER:C], 0, SHARED_BLOCK, QUARTER, QUARTER)
+        scatter_vector(0, SHARED_BLOCK, dx_shared, QUARTER, QUARTER, "x_second")
         quantize_g(1, C, late_pass[:], tag="x_second")
-        scatter_vector(0, VECTOR_BLOCKS[1], dx_held, QUARTER, QUARTER, "da_0")
+        scatter_vector(0, VECTOR_BLOCKS[1], dx_vector[1], 0, QUARTER, "da_0")
         for h in range(2):
             cols = slice(QUARTER * h, QUARTER * (h + 1))
             for j in range(2):
                 dh_pass(late_banks[2 * h + j], 1, C + QUARTER * h + P * j, False)
                 mask(da[:, cols, :], late_banks[2 * h + j], 2 + h, P * j)
             quantize(da[:, cols, :], da_codes[1][:, cols], da_scales[1][:, cols])
+            on_scalar(SCALAR_BLOCKS[0], QUARTER * h, QUARTER)
+        scatter_vector(0, VECTOR_BLOCKS[1], dx_vector[1], QUARTER, QUARTER, "da_1")
 
-        for vector_block, scalar_block in zip((SHARED_BLOCK,) + VECTOR_BLOCKS, SCALAR_BLOCKS):
-            on_vector(1, vector_block, ["da_1_a", "da_1_b"] if vector_block == SHARED_BLOCK else [f"x_late_{vector_block}"])
+        store(SCALAR_BLOCKS[0])
+        for vector_block, scalar_block in zip((SHARED_BLOCK,) + VECTOR_BLOCKS, SCALAR_BLOCKS[1:] + (None,)):
+            on_vector(vector_block)
             store(vector_block)
-            on_scalar(scalar_block)
-            store(scalar_block)
+            if scalar_block is not None:
+                on_scalar(scalar_block, 0, C)
+                store(scalar_block)

@@ -1,7 +1,6 @@
 from contextlib import ExitStack
 
 import concourse.mybir as mybir
-from concourse.masks import make_identity
 
 K, T, E, C, H, N = 768, 1536, 2, 512, 512, 1024
 S = E * C
@@ -10,6 +9,7 @@ PACK = 4
 N_PASSES = N // (P * PACK)
 K_BLOCKS = K // P
 QUARTER = C // 2
+SQUARE = 32
 OFFSETS_PER_COLUMN = 16
 VECTOR_BLOCKS = (0, 1)
 SHARED_BLOCK = 2
@@ -54,11 +54,7 @@ def tile_moe_bdx_mlp_relu_kernel(tc, dyT, a, w2_words, w2_scales, w1_words, w1_s
             relay.tile([P, N_PASSES, 2 * H], U8, name="w2_raw_0", align_bytes=64, offset=2 * 4 * T + 2 * H),
             keep.tile([P, N_PASSES, 2 * H], U8, name="w2_raw_1", align_bytes=64),
         ]
-        w2_offset = rows_offset + E * 4 * PACK * C
-        w2_sb = [
-            relay.tile([P, N_PASSES, 2 * H], U8, name="w2_0", align_bytes=64, offset=w2_offset),
-            keep.tile([P, N_PASSES, 2 * H], U8, name="w2_1", align_bytes=64),
-        ]
+        w2_sb = [keep.tile([P, N_PASSES, 2 * H], U8, name=f"w2_{e}", align_bytes=64) for e in range(E)]
         s2_raw = relay.tile([P, E * N_PASSES, H], U8, name="s2_raw", align_bytes=64, offset=4 * T - 2 * H)
         s2_sb = keep.tile([P, E * N_PASSES, H], U8, name="s2_sb", align_bytes=64)
         w1_sb = keep.tile([P, E, 2 * K], U8, name="w1_sb", align_bytes=64)
@@ -80,8 +76,8 @@ def tile_moe_bdx_mlp_relu_kernel(tc, dyT, a, w2_words, w2_scales, w1_words, w1_s
         def load_w2(e):
             nc.sync.dma_start(w2_raw[e][:].bitcast(I32), w2_words[e].rearrange("s p b -> p s b").bitcast(I32))
 
-        gate_runs = relay.tile([P, E, 2 * PACK], F32, name="gate_runs", offset=w2_offset - 4 * 2 * PACK)
-        nc.sync.dma_start(gate_runs[:, :, 0:PACK], gate[0:1, :].rearrange("r (e p i) -> p (r e) i", e=E, i=PACK))
+        gate_runs = keep.tile([P, SQUARE], F32, name="gate_runs", align_bytes=64)
+        nc.sync.dma_start(gate_runs[:], gate[0 : P * SQUARE // S, :].rearrange("r (b c) -> (r b) c", c=SQUARE))
         zero = keep.tile([P, 1], F32, name="zero")
         nc.vector.memset(zero[:], 0.0)
         nc.vector.memset(s2_raw[:].rearrange("p q i -> p (q i)").bitcast(I32), 0)
@@ -104,17 +100,16 @@ def tile_moe_bdx_mlp_relu_kernel(tc, dyT, a, w2_words, w2_scales, w1_words, w1_s
         load_a(3)
 
         windows = {b: keep.tile([P, T], F32, name=f"window_{b}") for b in VECTOR_BLOCKS + (SHARED_BLOCK,)}
-        for b in VECTOR_BLOCKS:
-            nc.vector.memset(windows[b][:], 0.0)
-        identity = keep.tile([P, P], F32, name="identity")
-        make_identity(nc, identity[:])
-        nc.scalar.activation(windows[SHARED_BLOCK][:, 0:C], zero[:].to_broadcast([P, C]), COPY)
-        nc.gpsimd.memset(windows[SHARED_BLOCK][:, C:T], 0.0)
-        for e in range(E):
-            spread = psum_s.tile([P, PACK, P], F32, name="dx_s")
-            for i in range(PACK):
-                nc.tensor.transpose(spread[:, i, :], gate_runs[:, e, i : i + 1].to_broadcast([P, P]), identity[:])
-            nc.scalar.copy(gate_sb[:, C * e : C * (e + 1)].rearrange("p (n i) -> p n i", i=PACK), spread[:].rearrange("p i n -> p n i"))
+        nc.vector.memset(windows[VECTOR_BLOCKS[0]][:], 0.0)
+        nc.gpsimd.memset(windows[VECTOR_BLOCKS[1]][:], 0.0)
+        nc.scalar.activation(windows[SHARED_BLOCK][:], zero[:].to_broadcast([P, T]), COPY)
+        gate_turned = keep.tile([P, SQUARE], F32, name="gate_turned", align_bytes=64)
+        nc.vector.transpose(gate_turned[:], gate_runs[:])
+        per_expert = C // SQUARE
+        for e, copy in enumerate((nc.vector.tensor_copy, nc.scalar.copy)):
+            spread = keep.tile([P, per_expert, SQUARE], F32, name=f"spread_{e}", align_bytes=64)
+            copy(spread[:], gate_turned[:, per_expert * e : per_expert * (e + 1)].unsqueeze(2).to_broadcast([P, per_expert, SQUARE]))
+            nc.vector.transpose(gate_sb[:, C * e : C * (e + 1)], spread[:].rearrange("p b c -> p (b c)"))
 
         def by_four(grouped):
             return grouped.rearrange("p (c i) t -> p c t i", i=4)

@@ -135,9 +135,10 @@ def tile_moe_bdx_mlp_relu_kernel(tc, dyT, a, w2_words, w2_scales, w1_words, w1_s
         def quantize(grouped, words, scale_bytes):
             nc.vector.quantize_mx(out=words.bitcast(FP8X4), scales=scale_bytes, in_=flat(grouped))
 
-        def interleave(s, first, count, gated):
+        def interleave(s, first, count, gated, grouped=None):
             e, col = divmod(first, C)
-            grouped = keep.tile([P, count, PACK], BF16, name=f"g_grouped_{s}_{first}", align_bytes=64)
+            if grouped is None:
+                grouped = keep.tile([P, count, PACK], BF16, name=f"g_grouped_{s}_{first}", align_bytes=64)
             some_rows = rows_by_four(rows[s][e][:, :, col : col + count])
             if gated:
                 nc.scalar.copy(by_four(grouped[:]), some_rows)
@@ -155,7 +156,8 @@ def tile_moe_bdx_mlp_relu_kernel(tc, dyT, a, w2_words, w2_scales, w1_words, w1_s
                 g_codes[s, first + col] = (words[:, col : col + P], scale_bytes[:, col : col + P])
 
         def permute_words(e):
-            nc.scalar.copy(
+            copy = nc.scalar.copy if e == 0 else nc.vector.tensor_copy
+            copy(
                 w2_sb[e][:].bitcast(U16).rearrange("p s (t c i) -> p s c t i", t=PACK, i=8),
                 w2_raw[e][:].bitcast(U16).rearrange("p s (c i t) -> p s c t i", t=PACK, i=8),
             )
@@ -226,9 +228,12 @@ def tile_moe_bdx_mlp_relu_kernel(tc, dyT, a, w2_words, w2_scales, w1_words, w1_s
                     quantize_g(0, C * e, first_pass[e])
                 for blk, dh in enumerate(banks):
                     dh_pass(dh, 0, P * blk, True)
-        second_pass = [interleave(1, QUARTER * h, QUARTER, h == 0) for h in range(2)]
-        for h in range(2):
-            quantize_g(1, QUARTER * h, second_pass[h])
+        first_blocks = [interleave(1, P * j, P, True) for j in range(2)]
+        second_quarter = keep.tile([P, QUARTER, PACK], BF16, name="g_grouped_second", align_bytes=64)
+        for j in range(2):
+            interleave(1, QUARTER + P * j, P, False, second_quarter[:, P * j : P * (j + 1), :])
+            quantize_g(1, P * j, first_blocks[j])
+        quantize_g(1, QUARTER, second_quarter[:])
         permute_words(1)
         for t in range(FREE_ROWS, PACK):
             gather_plain(1, t, C, C)

@@ -242,7 +242,16 @@ def tile_moe_bdx_mlp_relu_kernel(tc, dyT, a, w2_words, w2_scales, w1_words, w1_s
         da_scales = [keep.tile([P, C], U8, name=f"scales_da_{e}", align_bytes=64) for e in range(E)]
 
         early_blocks = (SHARED_BLOCK,) + SCALAR_BLOCKS
-        da_early = keep.tile([P, C, PACK], BF16, name="da_0", tag="da_0", align_bytes=64)
+        dx_vector = []
+
+        def vector_products(h):
+            dx = psum_v.tile([P, len(VECTOR_BLOCKS), QUARTER], F32, name="dx_v")
+            for j, b in enumerate(VECTOR_BLOCKS):
+                second_product(dx[:, j, :], 0, b, QUARTER * h, QUARTER)
+            return dx
+
+        late_offset = rows_offset + E * 4 * PACK * C
+        da_early = relay.tile([P, C, PACK], BF16, name="da_0", align_bytes=64, offset=late_offset + C * PACK)
         for h in range(2):
             da = da_early[:, QUARTER * h : QUARTER * (h + 1), :]
             for j in range(2):
@@ -251,9 +260,7 @@ def tile_moe_bdx_mlp_relu_kernel(tc, dyT, a, w2_words, w2_scales, w1_words, w1_s
             cols = slice(QUARTER * h, QUARTER * (h + 1))
             quantize(da, da_codes[0][:, cols], da_scales[0][:, cols])
             if h == 1:
-                dx_vector = [psum_v.tile([P, C], F32, name="dx_v") for b in VECTOR_BLOCKS]
-                for b, dx in zip(VECTOR_BLOCKS, dx_vector):
-                    second_product(dx[:], 0, b, 0, C)
+                dx_vector.append(vector_products(h))
             staged = {}
             blocks = early_blocks[h:]
             for pair in range(0, len(blocks), 2):
@@ -265,18 +272,23 @@ def tile_moe_bdx_mlp_relu_kernel(tc, dyT, a, w2_words, w2_scales, w1_words, w1_s
                 nc.scalar.copy(x[:], dx[:])
                 for j, b in enumerate(together):
                     staged[b] = x[:, j, :]
+            if h == 0:
+                dx_vector.append(vector_products(h))
             for b in blocks:
                 scatter_scalar(b, QUARTER * h, staged[b])
 
         def scatter_vector(e, b, dx, first, count, tag):
-            x = keep.tile([P, count], F32, name=f"x_{e}_{b}_{first}", tag=tag, align_bytes=64)
-            nc.vector.tensor_copy(x[:], dx[:, first : first + count])
+            if tag is None:
+                x = relay.tile([P, count], F32, name=f"x_{e}_{b}_{first}", align_bytes=64, offset=late_offset)
+            else:
+                x = keep.tile([P, count], F32, name=f"x_{e}_{b}_{first}", tag=tag, align_bytes=64)
+            nc.vector.tensor_copy(x[:], dx)
             nc.vector.tensor_copy(windows[b][:].indirect(offsets(C * e + first, count)), x[:])
 
         def on_vector(b):
             dx = psum_v.tile([P, C], F32, name="dx_v")
             second_product(dx[:], 1, b, 0, C)
-            scatter_vector(1, b, dx, 0, C, f"x_late_{b}")
+            scatter_vector(1, b, dx[:], 0, C, f"x_late_{b}")
 
         def on_scalar(b, first, count):
             dx = psum_s.tile([P, count], F32, name="dx_s")
@@ -287,7 +299,7 @@ def tile_moe_bdx_mlp_relu_kernel(tc, dyT, a, w2_words, w2_scales, w1_words, w1_s
                 scatter_scalar(b, C + first + col, x[:, col : col + QUARTER])
 
         da = keep.tile([P, C, PACK], BF16, name="da_1", tag="da_1", align_bytes=64)
-        late_pass = keep.tile([P, C, PACK], BF16, name="g_grouped_late", tag="da_0", align_bytes=64)
+        late_pass = relay.tile([P, C, PACK], BF16, name="g_grouped_late", align_bytes=64, offset=late_offset)
         for h in range(2):
             cols = slice(QUARTER * h, QUARTER * (h + 1))
             gates = gate_sb[:, C + QUARTER * h : C + QUARTER * (h + 1)].unsqueeze(2).to_broadcast([P, QUARTER, PACK])
@@ -297,12 +309,15 @@ def tile_moe_bdx_mlp_relu_kernel(tc, dyT, a, w2_words, w2_scales, w1_words, w1_s
             dh = psum_h.tile([P, PACK, P], F32, name="dh")
             dh_pass(dh, 0, C + P * blk, True)
             late_banks.append(dh)
-        scatter_vector(0, VECTOR_BLOCKS[0], dx_vector[0], 0, C, "x_first")
+        x_first = relay.tile([P, len(VECTOR_BLOCKS), QUARTER], F32, name="x_first", align_bytes=64, offset=late_offset + 2 * C * PACK)
+        nc.vector.tensor_copy(x_first[:], dx_vector[0][:])
+        for j, b in enumerate(VECTOR_BLOCKS):
+            nc.vector.tensor_copy(windows[b][:].indirect(offsets(0, QUARTER)), x_first[:, j, :])
         dx_shared = psum_v.tile([P, C], F32, name="dx_v")
         second_product(dx_shared[:, QUARTER:C], 0, SHARED_BLOCK, QUARTER, QUARTER)
-        scatter_vector(0, SHARED_BLOCK, dx_shared, QUARTER, QUARTER, "x_second")
+        scatter_vector(0, SHARED_BLOCK, dx_shared[:, QUARTER:C], QUARTER, QUARTER, "x_second")
         quantize_g(1, C, late_pass[:], tag="x_second")
-        scatter_vector(0, VECTOR_BLOCKS[1], dx_vector[1], 0, QUARTER, "da_0")
+        scatter_vector(0, VECTOR_BLOCKS[0], dx_vector[1][:, 0, :], QUARTER, QUARTER, None)
         for h in range(2):
             cols = slice(QUARTER * h, QUARTER * (h + 1))
             for j in range(2):
@@ -310,7 +325,7 @@ def tile_moe_bdx_mlp_relu_kernel(tc, dyT, a, w2_words, w2_scales, w1_words, w1_s
                 mask(da[:, cols, :], late_banks[2 * h + j], 2 + h, P * j)
             quantize(da[:, cols, :], da_codes[1][:, cols], da_scales[1][:, cols])
             on_scalar(SCALAR_BLOCKS[0], QUARTER * h, QUARTER)
-        scatter_vector(0, VECTOR_BLOCKS[1], dx_vector[1], QUARTER, QUARTER, "da_1")
+        scatter_vector(0, VECTOR_BLOCKS[1], dx_vector[1][:, 1, :], QUARTER, QUARTER, "da_1")
 
         store(SCALAR_BLOCKS[0])
         for vector_block, scalar_block in zip((SHARED_BLOCK,) + VECTOR_BLOCKS, SCALAR_BLOCKS[1:] + (None,)):

@@ -28,6 +28,7 @@ U8 = mybir.dt.uint8
 FP4X4 = mybir.dt.float4_e2m1fn_x4
 FP8X4 = mybir.dt.float8_e5m2_x4
 MULT = mybir.AluOpType.mult
+ADD = mybir.AluOpType.add
 IS_GT = mybir.AluOpType.is_gt
 COPY = mybir.ActivationFunctionType.Copy
 
@@ -175,10 +176,10 @@ def tile_moe_bdx_mlp_relu_kernel(tc, dyT, a, w2_words, w2_scales, w1_words, w1_s
                     stop=(not opens and t == PACK - 1),
                 )
 
-        def mask(da, dh, q, first):
+        def mask(da, dh, a_grouped, first):
             nc.vector.scalar_tensor_tensor(
                 da[:, first : first + P, :],
-                a_sb[q][:, :, first : first + P].rearrange("p t c -> p c t"),
+                a_grouped[:, first : first + P, :],
                 0.0,
                 dh[:].rearrange("p t c -> p c t"),
                 IS_GT,
@@ -200,8 +201,7 @@ def tile_moe_bdx_mlp_relu_kernel(tc, dyT, a, w2_words, w2_scales, w1_words, w1_s
             nc.scalar.activation(windows[b][:].indirect(offsets(first, values.shape[1])), values, COPY)
 
         def store(b):
-            queue = nc.scalar if b in SCALAR_BLOCKS else nc.sync
-            queue.dma_start(out[P * b : P * (b + 1), :], windows[b][:])
+            nc.sync.dma_start(out[P * b : P * (b + 1), :], windows[b][:])
 
         for t in range(PACK):
             gather_gated(0, t, 0, C)
@@ -256,13 +256,13 @@ def tile_moe_bdx_mlp_relu_kernel(tc, dyT, a, w2_words, w2_scales, w1_words, w1_s
             da = da_early[:, QUARTER * h : QUARTER * (h + 1), :]
             for j in range(2):
                 dh_pass(banks[2 * h + j], 1, QUARTER * h + P * j, False)
-                mask(da, banks[2 * h + j], h, P * j)
+                mask(da, banks[2 * h + j], a_sb[h][:].rearrange("p t c -> p c t"), P * j)
             cols = slice(QUARTER * h, QUARTER * (h + 1))
             quantize(da, da_codes[0][:, cols], da_scales[0][:, cols])
             if h == 1:
                 dx_vector.append(vector_products(h))
             staged = {}
-            blocks = early_blocks[h:]
+            blocks = early_blocks
             for pair in range(0, len(blocks), 2):
                 together = blocks[pair : pair + 2]
                 dx = psum_s.tile([P, len(together), QUARTER], F32, name="dx_s")
@@ -279,7 +279,7 @@ def tile_moe_bdx_mlp_relu_kernel(tc, dyT, a, w2_words, w2_scales, w1_words, w1_s
 
         def scatter_vector(e, b, dx, first, count, tag):
             if tag is None:
-                x = relay.tile([P, count], F32, name=f"x_{e}_{b}_{first}", align_bytes=64, offset=late_offset)
+                x = relay.tile([P, count], F32, name=f"x_{e}_{b}_{first}", align_bytes=64, offset=late_offset + C)
             else:
                 x = keep.tile([P, count], F32, name=f"x_{e}_{b}_{first}", tag=tag, align_bytes=64)
             nc.vector.tensor_copy(x[:], dx)
@@ -313,24 +313,31 @@ def tile_moe_bdx_mlp_relu_kernel(tc, dyT, a, w2_words, w2_scales, w1_words, w1_s
         nc.vector.tensor_copy(x_first[:], dx_vector[0][:])
         for j, b in enumerate(VECTOR_BLOCKS):
             nc.vector.tensor_copy(windows[b][:].indirect(offsets(0, QUARTER)), x_first[:, j, :])
-        dx_shared = psum_v.tile([P, C], F32, name="dx_v")
-        second_product(dx_shared[:, QUARTER:C], 0, SHARED_BLOCK, QUARTER, QUARTER)
-        scatter_vector(0, SHARED_BLOCK, dx_shared[:, QUARTER:C], QUARTER, QUARTER, "x_second")
+        scatter_vector(0, VECTOR_BLOCKS[0], dx_vector[1][:, 0, :], QUARTER, QUARTER, "x_second")
         quantize_g(1, C, late_pass[:], tag="x_second")
-        scatter_vector(0, VECTOR_BLOCKS[0], dx_vector[1][:, 0, :], QUARTER, QUARTER, None)
+        scatter_vector(0, VECTOR_BLOCKS[1], dx_vector[1][:, 1, :], QUARTER, QUARTER, None)
+        a_woven = []
+        for h, offset in enumerate((late_offset + 3 * C, late_offset - 7 * C)):
+            woven = relay.tile([P, QUARTER, PACK], F32, name=f"a_woven_{h}", align_bytes=64, offset=offset)
+            nc.gpsimd.tensor_scalar(woven[:], a_sb[2 + h][:].rearrange("p t c -> p c t"), 1.0, 0.0, MULT, ADD)
+            a_woven.append(woven)
+        dx_shared = []
         for h in range(2):
             cols = slice(QUARTER * h, QUARTER * (h + 1))
             for j in range(2):
                 dh_pass(late_banks[2 * h + j], 1, C + QUARTER * h + P * j, False)
-                mask(da[:, cols, :], late_banks[2 * h + j], 2 + h, P * j)
+                mask(da[:, cols, :], late_banks[2 * h + j], a_woven[h][:], P * j)
             quantize(da[:, cols, :], da_codes[1][:, cols], da_scales[1][:, cols])
-            on_scalar(SCALAR_BLOCKS[0], QUARTER * h, QUARTER)
-        scatter_vector(0, VECTOR_BLOCKS[1], dx_vector[1][:, 1, :], QUARTER, QUARTER, "da_1")
-
+            dx = psum_v.tile([P, QUARTER], F32, name="dx_v")
+            second_product(dx[:], 1, SHARED_BLOCK, QUARTER * h, QUARTER)
+            dx_shared.append(dx)
+        scatter_vector(1, SHARED_BLOCK, dx_shared[0][:], 0, QUARTER, "da_1")
+        scatter_vector(1, SHARED_BLOCK, dx_shared[1][:], QUARTER, QUARTER, "x_shared")
+        store(SHARED_BLOCK)
+        on_scalar(SCALAR_BLOCKS[0], 0, C)
         store(SCALAR_BLOCKS[0])
-        for vector_block, scalar_block in zip((SHARED_BLOCK,) + VECTOR_BLOCKS, SCALAR_BLOCKS[1:] + (None,)):
+        for vector_block, scalar_block in zip(VECTOR_BLOCKS, SCALAR_BLOCKS[1:]):
             on_vector(vector_block)
             store(vector_block)
-            if scalar_block is not None:
-                on_scalar(scalar_block, 0, C)
-                store(scalar_block)
+            on_scalar(scalar_block, 0, C)
+            store(scalar_block)

@@ -7,14 +7,21 @@ S = E * C
 P = 128
 PACK = 4
 N_PASSES = N // (P * PACK)
-K_BLOCKS = K // P
-QUARTER = C // 2
+QUARTER = S // 4
+BANKS_PER_EXPERT = C // P
 SQUARE = 32
 OFFSETS_PER_COLUMN = 16
+LINE = 16
 VECTOR_BLOCKS = (0, 1)
 SHARED_BLOCK = 2
 SCALAR_BLOCKS = (3, 4, 5)
 FREE_ROWS = 1
+
+WINDOW_BYTES = 4 * T
+ROWS_BYTES = 4 * PACK * C
+GROUPED_BYTES = 2 * PACK * C
+ROWS_OFFSET = len(SCALAR_BLOCKS) * WINDOW_BYTES
+LATE_OFFSET = ROWS_OFFSET + E * ROWS_BYTES
 
 FLOPS = 2 * S * H * (N + K)
 BYTES = 4 * N * T + 4 * H * S + E * (N * H + H * K) // 2 + E * (N * H + H * K) // 32 + 4 * S + 2 * P * S // 16 + 4 * K * T
@@ -38,25 +45,24 @@ def tile_moe_bdx_mlp_relu_kernel(tc, dyT, a, w2_words, w2_scales, w1_words, w1_s
     with ExitStack() as ctx:
         keep = ctx.enter_context(tc.tile_pool(name="keep", bufs=1))
         relay = ctx.enter_context(tc.tile_pool(name="relay", bufs=1))
-        psum_h = ctx.enter_context(tc.psum_pool(name="psum_h", bufs=4))
-        psum_s = ctx.enter_context(tc.psum_pool(name="psum_s", bufs=2))
+        psum_h = ctx.enter_context(tc.psum_pool(name="psum_h", bufs=1))
+        psum_s = ctx.enter_context(tc.psum_pool(name="psum_s", bufs=1))
         psum_v = ctx.enter_context(tc.psum_pool(name="psum_v", bufs=2))
 
         offs_sb = keep.tile([P, S // OFFSETS_PER_COLUMN], U16, name="offs_sb")
         gate_sb = keep.tile([P, S], F32, name="gate_sb", align_bytes=64)
         planes = [[keep.tile([P, T], F32, name=f"dy_{s}_{t}", align_bytes=64) for t in range(PACK)] for s in range(N_PASSES)]
-        rows_offset = len(SCALAR_BLOCKS) * 4 * T
-        rows = [[relay.tile([P, PACK, C], F32, name=f"rows_0_{e}", align_bytes=64, offset=rows_offset + 4 * PACK * C * e)[:] for e in range(E)]]
-        arena = relay.tile([P, PACK + FREE_ROWS, C], F32, name="arena", align_bytes=64, offset=rows_offset + 2 * PACK * C)
-        rows.append([arena[:, FREE_ROWS : FREE_ROWS + PACK, :], arena[:, 0:PACK, :]])
-        g_codes = {}
+        rows = [[relay.tile([P, PACK, C], F32, name=f"rows_0_{e}", align_bytes=64, offset=ROWS_OFFSET + ROWS_BYTES * e)[:] for e in range(E)]]
+        second_offset = ROWS_OFFSET + ROWS_BYTES // 2
+        second_rows = relay.tile([P, PACK + FREE_ROWS, C], F32, name="rows_1", align_bytes=64, offset=second_offset)
+        rows.append([second_rows[:, FREE_ROWS : FREE_ROWS + PACK, :], second_rows[:, 0:PACK, :]])
         a_sb = [keep.tile([P, PACK, QUARTER], F32, name=f"a_{q}") for q in range(S // QUARTER)]
         w2_raw = [
-            relay.tile([P, N_PASSES, 2 * H], U8, name="w2_raw_0", align_bytes=64, offset=2 * 4 * T + 2 * H),
+            relay.tile([P, N_PASSES, 2 * H], U8, name="w2_raw_0", align_bytes=64, offset=2 * WINDOW_BYTES),
             keep.tile([P, N_PASSES, 2 * H], U8, name="w2_raw_1", align_bytes=64),
         ]
+        s2_raw = relay.tile([P, E * N_PASSES, H], U8, name="s2_raw", align_bytes=64, offset=WINDOW_BYTES - E * N_PASSES * H // 2)
         w2_sb = [keep.tile([P, N_PASSES, 2 * H], U8, name=f"w2_{e}", align_bytes=64) for e in range(E)]
-        s2_raw = relay.tile([P, E * N_PASSES, H], U8, name="s2_raw", align_bytes=64, offset=4 * T - 2 * H)
         s2_sb = keep.tile([P, E * N_PASSES, H], U8, name="s2_sb", align_bytes=64)
         w1_sb = keep.tile([P, E, 2 * K], U8, name="w1_sb", align_bytes=64)
         s1_sb = keep.tile([P, E, K], U8, name="s1_sb", align_bytes=64)
@@ -70,9 +76,9 @@ def tile_moe_bdx_mlp_relu_kernel(tc, dyT, a, w2_words, w2_scales, w1_words, w1_s
         def load_a(q):
             nc.sync.dma_start(a_sb[q][:], a_view[:, :, QUARTER * q : QUARTER * (q + 1)])
 
-        def load_scales(rows_sb, view):
-            for q in range(4):
-                nc.sync.dma_start(rows_sb[32 * q : 32 * q + 4].bitcast(I32), view[4 * q : 4 * q + 4].bitcast(I32))
+        def load_scales(scale_tile, view):
+            for q in range(P // SQUARE):
+                nc.sync.dma_start(scale_tile[SQUARE * q : SQUARE * q + 4].bitcast(I32), view[4 * q : 4 * q + 4].bitcast(I32))
 
         def load_w2(e):
             nc.sync.dma_start(w2_raw[e][:].bitcast(I32), w2_words[e].rearrange("s p b -> p s b").bitcast(I32))
@@ -96,9 +102,8 @@ def tile_moe_bdx_mlp_relu_kernel(tc, dyT, a, w2_words, w2_scales, w1_words, w1_s
         load_w2(1)
         load_scales(s1_sb[:], w1_scales.rearrange("e s f k -> f (e s) k"))
         nc.sync.dma_start(w1_sb[:].bitcast(I32), w1_words.rearrange("e s p b -> p (e s) b").bitcast(I32))
-        load_a(1)
-        load_a(2)
-        load_a(3)
+        for q in range(1, S // QUARTER):
+            load_a(q)
 
         windows = {b: keep.tile([P, T], F32, name=f"window_{b}") for b in VECTOR_BLOCKS + (SHARED_BLOCK,)}
         nc.vector.memset(windows[VECTOR_BLOCKS[0]][:], 0.0)
@@ -106,20 +111,11 @@ def tile_moe_bdx_mlp_relu_kernel(tc, dyT, a, w2_words, w2_scales, w1_words, w1_s
         nc.scalar.activation(windows[SHARED_BLOCK][:], zero[:].to_broadcast([P, T]), COPY)
         gate_turned = keep.tile([P, SQUARE], F32, name="gate_turned", align_bytes=64)
         nc.vector.transpose(gate_turned[:], gate_runs[:])
-        per_expert = C // SQUARE
+        squares = C // SQUARE
         for e, copy in enumerate((nc.vector.tensor_copy, nc.scalar.copy)):
-            spread = keep.tile([P, per_expert, SQUARE], F32, name=f"spread_{e}", align_bytes=64)
-            copy(spread[:], gate_turned[:, per_expert * e : per_expert * (e + 1)].unsqueeze(2).to_broadcast([P, per_expert, SQUARE]))
+            spread = keep.tile([P, squares, SQUARE], F32, name=f"spread_{e}", align_bytes=64)
+            copy(spread[:], gate_turned[:, squares * e : squares * (e + 1)].unsqueeze(2).to_broadcast([P, squares, SQUARE]))
             nc.vector.transpose(gate_sb[:, C * e : C * (e + 1)], spread[:].rearrange("p b c -> p (b c)"))
-
-        def by_four(grouped):
-            return grouped.rearrange("p (c i) t -> p c t i", i=4)
-
-        def rows_by_four(some_rows):
-            return some_rows.rearrange("p t (c i) -> p c t i", i=4)
-
-        def flat(grouped):
-            return grouped.rearrange("p c t -> p (c t)")
 
         def offsets(first, count):
             return offs_sb[:, first // OFFSETS_PER_COLUMN : (first + count) // OFFSETS_PER_COLUMN]
@@ -133,72 +129,88 @@ def tile_moe_bdx_mlp_relu_kernel(tc, dyT, a, w2_words, w2_scales, w1_words, w1_s
             e, col = divmod(first, C)
             nc.scalar.activation(rows[s][e][:, t, col : col + count], planes[s][t][:].indirect(offsets(first, count)), COPY)
 
-        def quantize(grouped, words, scale_bytes):
-            nc.vector.quantize_mx(out=words.bitcast(FP8X4), scales=scale_bytes, in_=flat(grouped))
-
-        def interleave(s, first, count, gated, grouped=None):
+        def group(s, first, grouped, gated):
             e, col = divmod(first, C)
-            if grouped is None:
-                grouped = keep.tile([P, count, PACK], BF16, name=f"g_grouped_{s}_{first}", align_bytes=64)
-            some_rows = rows_by_four(rows[s][e][:, :, col : col + count])
-            if gated:
-                nc.scalar.copy(by_four(grouped[:]), some_rows)
-            else:
-                gates = gate_sb[:, first : first + count].rearrange("p (c i) -> p c i", i=4)
-                nc.vector.tensor_tensor(by_four(grouped[:]), some_rows, gates.unsqueeze(2).to_broadcast([P, count // 4, PACK, 4]), MULT)
-            return grouped[:]
-
-        def quantize_g(s, first, grouped, tag=None):
             count = grouped.shape[1]
-            words = keep.tile([P, count], U32, name=f"g_codes_{s}_{first}", tag=tag or f"g_codes_{s}_{first}", align_bytes=64)
+            side = LINE // 4
+            source = rows[s][e][:, :, col : col + count].rearrange("p t (c i) -> p c t i", i=side)
+            target = grouped.rearrange("p (c i) t -> p c t i", i=side)
+            if gated:
+                nc.scalar.copy(target, source)
+            else:
+                gates = gate_sb[:, first : first + count].rearrange("p (c i) -> p c i", i=side)
+                nc.vector.tensor_tensor(target, source, gates.unsqueeze(2).to_broadcast([P, count // side, PACK, side]), MULT)
+
+        def quantize(grouped, words, scale_bytes):
+            nc.vector.quantize_mx(out=words.bitcast(FP8X4), scales=scale_bytes, in_=grouped.rearrange("p c t -> p (c t)"))
+
+        g_codes = {}
+
+        def quantize_g(s, first, grouped, words_tag):
+            count = grouped.shape[1]
+            words = keep.tile([P, count], U32, name=f"g_words_{s}_{first}", tag=words_tag, align_bytes=64)
             scale_bytes = keep.tile([P, count], U8, name=f"g_scales_{s}_{first}", align_bytes=64)
             quantize(grouped, words[:], scale_bytes[:])
             for col in range(0, count, P):
                 g_codes[s, first + col] = (words[:, col : col + P], scale_bytes[:, col : col + P])
 
-        def permute_words(e):
-            copy = nc.scalar.copy if e == 0 else nc.vector.tensor_copy
+        def permute_words(e, copy):
             copy(
-                w2_sb[e][:].bitcast(U16).rearrange("p s (t c i) -> p s c t i", t=PACK, i=8),
-                w2_raw[e][:].bitcast(U16).rearrange("p s (c i t) -> p s c t i", t=PACK, i=8),
+                w2_sb[e][:].bitcast(U16).rearrange("p s (t c i) -> p s c t i", t=PACK, i=LINE // 2),
+                w2_raw[e][:].bitcast(U16).rearrange("p s (c i t) -> p s c t i", t=PACK, i=LINE // 2),
             )
 
-        def dh_pass(dh, s, first, opens):
+        def permute_scales():
+            nc.vector.tensor_copy(
+                s2_sb[:].rearrange("p q (t c i) -> p q c t i", t=PACK, i=LINE),
+                s2_raw[:].rearrange("p q (c i t) -> p q c t i", t=PACK, i=LINE),
+            )
+
+        def dh_pass(dh, s, first):
             e = first // C
+            words, scale_bytes = g_codes[s, first]
             for t in range(PACK):
                 nc.tensor.matmul_mx(
                     out=dh[:, t, :],
                     lhsT=w2_sb[e][:, s, 2 * P * t : 2 * P * (t + 1)].bitcast(FP4X4),
                     lhsT_scale=s2_sb[:, N_PASSES * e + s, P * t : P * (t + 1)],
-                    rhs=g_codes[s, first][0].bitcast(FP8X4),
-                    rhs_scale=g_codes[s, first][1],
-                    start=(opens and t == 0),
-                    stop=(not opens and t == PACK - 1),
+                    rhs=words.bitcast(FP8X4),
+                    rhs_scale=scale_bytes,
+                    start=(s == 0 and t == 0),
+                    stop=(s == N_PASSES - 1 and t == PACK - 1),
                 )
 
-        def mask(da, dh, a_grouped, first):
-            nc.vector.scalar_tensor_tensor(
-                da[:, first : first + P, :],
-                a_grouped[:, first : first + P, :],
-                0.0,
-                dh[:].rearrange("p t c -> p c t"),
-                IS_GT,
-                MULT,
-            )
+        def mask(da, dh, a_grouped):
+            nc.vector.scalar_tensor_tensor(da, a_grouped, 0.0, dh[:].rearrange("p t c -> p c t"), IS_GT, MULT)
 
-        def second_product(dx, e, b, first, count):
+        da_words = [keep.tile([P, C], U32, name=f"da_words_{e}", align_bytes=64) for e in range(E)]
+        da_scales = [keep.tile([P, C], U8, name=f"da_scales_{e}", align_bytes=64) for e in range(E)]
+
+        def quantize_da(e, da, h):
+            cols = slice(QUARTER * h, QUARTER * (h + 1))
+            quantize(da[:, cols, :], da_words[e][:, cols], da_scales[e][:, cols])
+
+        def dx_product(dx, e, b, col):
+            cols = slice(col, col + dx.shape[1])
             nc.tensor.matmul_mx(
                 out=dx,
                 lhsT=w1_sb[:, e, 2 * P * b : 2 * P * (b + 1)].bitcast(FP4X4),
                 lhsT_scale=s1_sb[:, e, P * b : P * (b + 1)],
-                rhs=da_codes[e][:, first : first + count].bitcast(FP8X4),
-                rhs_scale=da_scales[e][:, first : first + count],
+                rhs=da_words[e][:, cols].bitcast(FP8X4),
+                rhs_scale=da_scales[e][:, cols],
                 start=True,
                 stop=True,
             )
 
+        def dx_pair(dx, e, blocks, h):
+            for j, b in enumerate(blocks):
+                dx_product(dx[:, j, :], e, b, QUARTER * h)
+
         def scatter_scalar(b, first, values):
             nc.scalar.activation(windows[b][:].indirect(offsets(first, values.shape[1])), values, COPY)
+
+        def scatter_vector(b, first, values):
+            nc.vector.tensor_copy(windows[b][:].indirect(offsets(first, values.shape[1])), values)
 
         def store(b):
             nc.sync.dma_start(out[P * b : P * (b + 1), :], windows[b][:])
@@ -207,17 +219,16 @@ def tile_moe_bdx_mlp_relu_kernel(tc, dyT, a, w2_words, w2_scales, w1_words, w1_s
             gather_gated(0, t, 0, C)
             gather_plain(0, t, C, C)
             if t == 0:
-                permute_words(0)
-                nc.vector.tensor_copy(
-                    s2_sb[:].rearrange("p q (t c i) -> p q c t i", t=PACK, i=16),
-                    s2_raw[:].rearrange("p q (c i t) -> p q c t i", t=PACK, i=16),
-                )
+                permute_words(0, nc.scalar.copy)
+                permute_scales()
                 for j, b in enumerate(SCALAR_BLOCKS):
-                    windows[b] = relay.tile([P, T], F32, name=f"window_{b}", align_bytes=64, offset=4 * T * j)
+                    windows[b] = relay.tile([P, T], F32, name=f"window_{b}", align_bytes=64, offset=WINDOW_BYTES * j)
                     nc.gpsimd.memset(windows[b][:], 0.0)
-        first_pass = [interleave(0, C * e, C, e == 0) for e in range(E)]
+        first_pass = [keep.tile([P, C, PACK], BF16, name=f"g_grouped_0_{e}", align_bytes=64) for e in range(E)]
+        for e in range(E):
+            group(0, C * e, first_pass[e][:], gated=(e == 0))
 
-        banks = [psum_h.tile([P, PACK, P], F32, name="dh") for blk in range(4)]
+        dh_early = [psum_h.tile([P, PACK, P], F32, name=f"dh_0_{blk}", tag=f"dh_{blk}") for blk in range(BANKS_PER_EXPERT)]
         for t in range(PACK):
             gather_gated(1, t, 0, QUARTER)
             gather_plain(1, t, QUARTER, QUARTER)
@@ -225,119 +236,129 @@ def tile_moe_bdx_mlp_relu_kernel(tc, dyT, a, w2_words, w2_scales, w1_words, w1_s
                 gather_plain(1, t, C, C)
             if t == 0:
                 for e in range(E):
-                    quantize_g(0, C * e, first_pass[e])
-                for blk, dh in enumerate(banks):
-                    dh_pass(dh, 0, P * blk, True)
-        first_blocks = [interleave(1, P * j, P, True) for j in range(2)]
+                    quantize_g(0, C * e, first_pass[e][:], f"g_words_0_{e}")
+                for blk, dh in enumerate(dh_early):
+                    dh_pass(dh, 0, P * blk)
+        halves = QUARTER // P
+        first_blocks = [keep.tile([P, P, PACK], BF16, name=f"g_grouped_1_{j}", align_bytes=64) for j in range(halves)]
+        for j in range(halves):
+            group(1, P * j, first_blocks[j][:], gated=True)
         second_quarter = keep.tile([P, QUARTER, PACK], BF16, name="g_grouped_second", align_bytes=64)
-        for j in range(2):
-            interleave(1, QUARTER + P * j, P, False, second_quarter[:, P * j : P * (j + 1), :])
-            quantize_g(1, P * j, first_blocks[j])
-        quantize_g(1, QUARTER, second_quarter[:])
-        permute_words(1)
+        for j in range(halves):
+            group(1, QUARTER + P * j, second_quarter[:, P * j : P * (j + 1), :], gated=False)
+            quantize_g(1, P * j, first_blocks[j][:], f"g_words_1_{j}")
+        quantize_g(1, QUARTER, second_quarter[:], "g_words_second")
+        permute_words(1, nc.vector.tensor_copy)
         for t in range(FREE_ROWS, PACK):
             gather_plain(1, t, C, C)
 
-        da_codes = [keep.tile([P, C], U32, name=f"codes_da_{e}", align_bytes=64) for e in range(E)]
-        da_scales = [keep.tile([P, C], U8, name=f"scales_da_{e}", align_bytes=64) for e in range(E)]
-
         early_blocks = (SHARED_BLOCK,) + SCALAR_BLOCKS
+        da_early = relay.tile([P, C, PACK], BF16, name="da_0", align_bytes=64, offset=LATE_OFFSET + GROUPED_BYTES // 2)
         dx_vector = []
 
         def vector_products(h):
-            dx = psum_v.tile([P, len(VECTOR_BLOCKS), QUARTER], F32, name="dx_v")
-            for j, b in enumerate(VECTOR_BLOCKS):
-                second_product(dx[:, j, :], 0, b, QUARTER * h, QUARTER)
-            return dx
+            dx = psum_v.tile([P, 2, QUARTER], F32, name="dx_v")
+            dx_pair(dx, 0, VECTOR_BLOCKS, h)
+            dx_vector.append(dx)
 
-        late_offset = rows_offset + E * 4 * PACK * C
-        da_early = relay.tile([P, C, PACK], BF16, name="da_0", align_bytes=64, offset=late_offset + C * PACK)
         for h in range(2):
-            da = da_early[:, QUARTER * h : QUARTER * (h + 1), :]
-            for j in range(2):
-                dh_pass(banks[2 * h + j], 1, QUARTER * h + P * j, False)
-                mask(da, banks[2 * h + j], a_sb[h][:].rearrange("p t c -> p c t"), P * j)
-            cols = slice(QUARTER * h, QUARTER * (h + 1))
-            quantize(da, da_codes[0][:, cols], da_scales[0][:, cols])
+            for j in range(halves):
+                blk = halves * h + j
+                dh_pass(dh_early[blk], 1, P * blk)
+                mask(da_early[:, P * blk : P * (blk + 1), :], dh_early[blk], a_sb[h][:, :, P * j : P * (j + 1)].rearrange("p t c -> p c t"))
+            quantize_da(0, da_early, h)
             if h == 1:
-                dx_vector.append(vector_products(h))
-            staged = {}
-            blocks = early_blocks
-            for pair in range(0, len(blocks), 2):
-                together = blocks[pair : pair + 2]
-                dx = psum_s.tile([P, len(together), QUARTER], F32, name="dx_s")
-                for j, b in enumerate(together):
-                    second_product(dx[:, j, :], 0, b, QUARTER * h, QUARTER)
-                x = keep.tile([P, len(together), QUARTER], F32, name=f"x_early_{h}_{pair}", align_bytes=64)
+                vector_products(h)
+            staged = []
+            for pair in range(2):
+                dx = psum_s.tile([P, 2, QUARTER], F32, name=f"dx_s_{h}_{pair}", tag=f"dx_s_{pair}")
+                dx_pair(dx, 0, early_blocks[2 * pair : 2 * pair + 2], h)
+                x = keep.tile([P, 2, QUARTER], F32, name=f"x_early_{h}_{pair}", align_bytes=64)
                 nc.scalar.copy(x[:], dx[:])
-                for j, b in enumerate(together):
-                    staged[b] = x[:, j, :]
+                staged.extend(x[:, j, :] for j in range(2))
             if h == 0:
-                dx_vector.append(vector_products(h))
-            for b in blocks:
-                scatter_scalar(b, QUARTER * h, staged[b])
+                vector_products(h)
+            for b, values in zip(early_blocks, staged):
+                scatter_scalar(b, QUARTER * h, values)
 
-        def scatter_vector(e, b, dx, first, count, tag):
-            if tag is None:
-                x = relay.tile([P, count], F32, name=f"x_{e}_{b}_{first}", align_bytes=64, offset=late_offset + C)
-            else:
-                x = keep.tile([P, count], F32, name=f"x_{e}_{b}_{first}", tag=tag, align_bytes=64)
-            nc.vector.tensor_copy(x[:], dx)
-            nc.vector.tensor_copy(windows[b][:].indirect(offsets(C * e + first, count)), x[:])
-
-        def on_vector(b):
-            dx = psum_v.tile([P, C], F32, name="dx_v")
-            second_product(dx[:], 1, b, 0, C)
-            scatter_vector(1, b, dx[:], 0, C, f"x_late_{b}")
-
-        def on_scalar(b, first, count):
-            dx = psum_s.tile([P, count], F32, name="dx_s")
-            second_product(dx[:], 1, b, first, count)
-            x = keep.tile([P, count], F32, name=f"x_1_{b}_{first}", align_bytes=64)
-            nc.scalar.copy(x[:], dx[:])
-            for col in range(0, count, QUARTER):
-                scatter_scalar(b, C + first + col, x[:, col : col + QUARTER])
-
-        da = keep.tile([P, C, PACK], BF16, name="da_1", tag="da_1", align_bytes=64)
-        late_pass = relay.tile([P, C, PACK], BF16, name="g_grouped_late", align_bytes=64, offset=late_offset)
+        late_pass = relay.tile([P, C, PACK], BF16, name="g_grouped_late", align_bytes=64, offset=LATE_OFFSET)
         for h in range(2):
             cols = slice(QUARTER * h, QUARTER * (h + 1))
             gates = gate_sb[:, C + QUARTER * h : C + QUARTER * (h + 1)].unsqueeze(2).to_broadcast([P, QUARTER, PACK])
             nc.gpsimd.tensor_tensor(late_pass[:, cols, :], rows[1][1][:, :, cols].rearrange("p t c -> p c t"), gates, MULT)
-        late_banks = []
-        for blk in range(4):
-            dh = psum_h.tile([P, PACK, P], F32, name="dh")
-            dh_pass(dh, 0, C + P * blk, True)
-            late_banks.append(dh)
-        x_first = relay.tile([P, len(VECTOR_BLOCKS), QUARTER], F32, name="x_first", align_bytes=64, offset=late_offset + 2 * C * PACK)
+        dh_late = [psum_h.tile([P, PACK, P], F32, name=f"dh_1_{blk}", tag=f"dh_{blk}") for blk in range(BANKS_PER_EXPERT)]
+        for blk, dh in enumerate(dh_late):
+            dh_pass(dh, 0, C + P * blk)
+        x_first = relay.tile([P, 2, QUARTER], F32, name="x_first", align_bytes=64, offset=LATE_OFFSET + GROUPED_BYTES)
+        x_second = keep.tile([P, QUARTER], F32, name="x_second", tag="x_second", align_bytes=64)
+        x_third = relay.tile([P, QUARTER], F32, name="x_third", align_bytes=64, offset=second_offset)
         nc.vector.tensor_copy(x_first[:], dx_vector[0][:])
+        nc.vector.tensor_copy(x_second[:], dx_vector[1][:, 0, :])
         for j, b in enumerate(VECTOR_BLOCKS):
-            nc.vector.tensor_copy(windows[b][:].indirect(offsets(0, QUARTER)), x_first[:, j, :])
-        scatter_vector(0, VECTOR_BLOCKS[0], dx_vector[1][:, 0, :], QUARTER, QUARTER, "x_second")
-        quantize_g(1, C, late_pass[:], tag="x_second")
-        scatter_vector(0, VECTOR_BLOCKS[1], dx_vector[1][:, 1, :], QUARTER, QUARTER, None)
-        a_woven = []
-        for h, offset in enumerate((late_offset + 3 * C, late_offset - 7 * C)):
-            woven = relay.tile([P, QUARTER, PACK], F32, name=f"a_woven_{h}", align_bytes=64, offset=offset)
-            nc.gpsimd.tensor_scalar(woven[:], a_sb[2 + h][:].rearrange("p t c -> p c t"), 1.0, 0.0, MULT, ADD)
-            a_woven.append(woven)
-        dx_shared = []
-        for h in range(2):
-            cols = slice(QUARTER * h, QUARTER * (h + 1))
-            for j in range(2):
-                dh_pass(late_banks[2 * h + j], 1, C + QUARTER * h + P * j, False)
-                mask(da[:, cols, :], late_banks[2 * h + j], a_woven[h][:], P * j)
-            quantize(da[:, cols, :], da_codes[1][:, cols], da_scales[1][:, cols])
-            dx = psum_v.tile([P, QUARTER], F32, name="dx_v")
-            second_product(dx[:], 1, SHARED_BLOCK, QUARTER * h, QUARTER)
-            dx_shared.append(dx)
-        scatter_vector(1, SHARED_BLOCK, dx_shared[0][:], 0, QUARTER, "da_1")
-        scatter_vector(1, SHARED_BLOCK, dx_shared[1][:], QUARTER, QUARTER, "x_shared")
+            scatter_vector(b, 0, x_first[:, j, :])
+        scatter_vector(VECTOR_BLOCKS[0], QUARTER, x_second[:])
+        nc.vector.tensor_copy(x_third[:], dx_vector[1][:, 1, :])
+        quantize_g(1, C, late_pass[:], "x_second")
+        scatter_vector(VECTOR_BLOCKS[1], QUARTER, x_third[:])
+        a_late = []
+        for h, offset in enumerate((LATE_OFFSET + GROUPED_BYTES // 2, LATE_OFFSET - GROUPED_BYTES // 2)):
+            grouped_a = relay.tile([P, QUARTER, PACK], F32, name=f"a_late_{h}", align_bytes=64, offset=offset)
+            nc.gpsimd.tensor_scalar(grouped_a[:], a_sb[2 + h][:].rearrange("p t c -> p c t"), 1.0, 0.0, MULT, ADD)
+            a_late.append(grouped_a)
+
+        da_late = keep.tile([P, C, PACK], BF16, name="da_1", align_bytes=64)
+        x_late = keep.tile([P, 2, C], F32, name="x_late", align_bytes=64)
+
+        def late_mask(blk):
+            h, j = divmod(blk, halves)
+            dh_pass(dh_late[blk], 1, C + P * blk)
+            mask(da_late[:, P * blk : P * (blk + 1), :], dh_late[blk], a_late[h][:, P * j : P * (j + 1), :])
+
+        def late_products(h):
+            dx = psum_v.tile([P, 2, QUARTER], F32, name="dx_v")
+            dx_pair(dx, 1, (SHARED_BLOCK, VECTOR_BLOCKS[0]), h)
+            return dx
+
+        for blk in range(halves + 1):
+            late_mask(blk)
+        quantize_da(1, da_late, 0)
+        dx = late_products(0)
+        late_mask(BANKS_PER_EXPERT - 1)
+        nc.vector.tensor_copy(x_late[:, :, 0:QUARTER], dx[:])
+        quantize_da(1, da_late, 1)
+        scatter_vector(SHARED_BLOCK, C, x_late[:, 0, 0:QUARTER])
+
+        def stage_scalar(b, width, bank):
+            dx = psum_s.tile([P, C], F32, name=f"dx_late_{b}", tag=f"dx_s_{bank}")
+            dx_product(dx[:], 1, b, 0)
+            x = keep.tile([P, C], F32, name=f"x_late_{b}", align_bytes=64)
+            for col in range(0, C, width):
+                nc.scalar.copy(x[:, col : col + width], dx[:, col : col + width])
+            return x
+
+        first_block, second_block, last_block = SCALAR_BLOCKS
+        x_a = stage_scalar(first_block, QUARTER, 0)
+        dx = late_products(1)
+        for j in range(2):
+            nc.vector.tensor_copy(x_late[:, j, QUARTER:C], dx[:, j, :])
+        scatter_vector(SHARED_BLOCK, C + QUARTER, x_late[:, 0, QUARTER:C])
         store(SHARED_BLOCK)
-        on_scalar(SCALAR_BLOCKS[0], 0, C)
-        store(SCALAR_BLOCKS[0])
-        for vector_block, scalar_block in zip(VECTOR_BLOCKS, SCALAR_BLOCKS[1:]):
-            on_vector(vector_block)
-            store(vector_block)
-            on_scalar(scalar_block, 0, C)
-            store(scalar_block)
+        dx = psum_v.tile([P, C], F32, name="dx_v")
+        dx_product(dx[:], 1, VECTOR_BLOCKS[1], 0)
+        x_last = keep.tile([P, C], F32, name="x_last", align_bytes=64)
+        nc.vector.tensor_copy(x_last[:], dx[:])
+        scatter_scalar(first_block, C, x_a[:, 0:QUARTER])
+        x_b = stage_scalar(second_block, C, 1)
+        scatter_scalar(first_block, C + QUARTER, x_a[:, QUARTER:C])
+        store(first_block)
+        scatter_vector(VECTOR_BLOCKS[0], C, x_late[:, 1, :])
+        store(VECTOR_BLOCKS[0])
+        scatter_scalar(second_block, C, x_b[:, 0:QUARTER])
+        x_c = stage_scalar(last_block, C, 1)
+        scatter_scalar(second_block, C + QUARTER, x_b[:, QUARTER:C])
+        store(second_block)
+        scatter_vector(VECTOR_BLOCKS[1], C, x_last[:])
+        store(VECTOR_BLOCKS[1])
+        for col in range(0, C, QUARTER):
+            scatter_scalar(last_block, C + col, x_c[:, col : col + QUARTER])
+        store(last_block)

from contextlib import ExitStack

import concourse.mybir as mybir

K, T, E, C, H, N = 768, 1536, 2, 512, 512, 1024
S = E * C
P = 128
PACK = 4
N_PASSES = N // (P * PACK)
QUARTER = S // 4
BANKS_PER_EXPERT = C // P
SQUARE = 32
OFFSETS_PER_COLUMN = 16
LINE = 16
VECTOR_BLOCKS = (0, 1)
SHARED_BLOCK = 2
SCALAR_BLOCKS = (3, 4, 5)
FREE_ROWS = 1

WINDOW_BYTES = 4 * T
ROWS_BYTES = 4 * PACK * C
GROUPED_BYTES = 2 * PACK * C
ROWS_OFFSET = len(SCALAR_BLOCKS) * WINDOW_BYTES
LATE_OFFSET = ROWS_OFFSET + E * ROWS_BYTES

FLOPS = 2 * S * H * (N + K)
BYTES = 4 * N * T + 4 * H * S + E * (N * H + H * K) // 2 + E * (N * H + H * K) // 32 + 4 * S + 2 * P * S // 16 + 4 * K * T

F32 = mybir.dt.float32
BF16 = mybir.dt.bfloat16
I32 = mybir.dt.int32
U32 = mybir.dt.uint32
U16 = mybir.dt.uint16
U8 = mybir.dt.uint8
FP4X4 = mybir.dt.float4_e2m1fn_x4
FP8X4 = mybir.dt.float8_e5m2_x4
MULT = mybir.AluOpType.mult
ADD = mybir.AluOpType.add
IS_GT = mybir.AluOpType.is_gt
COPY = mybir.ActivationFunctionType.Copy


def tile_moe_bdx_mlp_relu_kernel(tc, dyT, a, w2_words, w2_scales, w1_words, w1_scales, gate, offs, out):
    nc = tc.nc
    with ExitStack() as ctx:
        keep = ctx.enter_context(tc.tile_pool(name="keep", bufs=1))
        relay = ctx.enter_context(tc.tile_pool(name="relay", bufs=1))
        psum_h = ctx.enter_context(tc.psum_pool(name="psum_h", bufs=1))
        psum_s = ctx.enter_context(tc.psum_pool(name="psum_s", bufs=1))
        psum_v = ctx.enter_context(tc.psum_pool(name="psum_v", bufs=2))

        offs_sb = keep.tile([P, S // OFFSETS_PER_COLUMN], U16, name="offs_sb")
        gate_sb = keep.tile([P, S], F32, name="gate_sb", align_bytes=64)
        planes = [[keep.tile([P, T], F32, name=f"dy_{s}_{t}", align_bytes=64) for t in range(PACK)] for s in range(N_PASSES)]
        rows = [[relay.tile([P, PACK, C], F32, name=f"rows_0_{e}", align_bytes=64, offset=ROWS_OFFSET + ROWS_BYTES * e)[:] for e in range(E)]]
        second_offset = ROWS_OFFSET + ROWS_BYTES // 2
        second_rows = relay.tile([P, PACK + FREE_ROWS, C], F32, name="rows_1", align_bytes=64, offset=second_offset)
        rows.append([second_rows[:, FREE_ROWS : FREE_ROWS + PACK, :], second_rows[:, 0:PACK, :]])
        a_sb = [keep.tile([P, PACK, QUARTER], F32, name=f"a_{q}") for q in range(S // QUARTER)]
        w2_raw = [
            relay.tile([P, N_PASSES, 2 * H], U8, name="w2_raw_0", align_bytes=64, offset=2 * WINDOW_BYTES),
            keep.tile([P, N_PASSES, 2 * H], U8, name="w2_raw_1", align_bytes=64),
        ]
        s2_raw = relay.tile([P, E * N_PASSES, H], U8, name="s2_raw", align_bytes=64, offset=WINDOW_BYTES - E * N_PASSES * H // 2)
        w2_sb = [keep.tile([P, N_PASSES, 2 * H], U8, name=f"w2_{e}", align_bytes=64) for e in range(E)]
        s2_sb = keep.tile([P, E * N_PASSES, H], U8, name="s2_sb", align_bytes=64)
        w1_sb = keep.tile([P, E, 2 * K], U8, name="w1_sb", align_bytes=64)
        s1_sb = keep.tile([P, E, K], U8, name="s1_sb", align_bytes=64)

        dy_view = dyT.rearrange("(s p t) c -> s t p c", p=P, t=PACK)
        a_view = a.rearrange("(p t) c -> p t c", t=PACK)

        def load_plane(s, t):
            nc.sync.dma_start(planes[s][t][:], dy_view[s, t])

        def load_a(q):
            nc.sync.dma_start(a_sb[q][:], a_view[:, :, QUARTER * q : QUARTER * (q + 1)])

        def load_scales(scale_tile, view):
            for q in range(P // SQUARE):
                nc.sync.dma_start(scale_tile[SQUARE * q : SQUARE * q + 4].bitcast(I32), view[4 * q : 4 * q + 4].bitcast(I32))

        def load_w2(e):
            nc.sync.dma_start(w2_raw[e][:].bitcast(I32), w2_words[e].rearrange("s p b -> p s b").bitcast(I32))

        gate_runs = keep.tile([P, SQUARE], F32, name="gate_runs", align_bytes=64)
        nc.sync.dma_start(gate_runs[:], gate[0 : P * SQUARE // S, :].rearrange("r (b c) -> (r b) c", c=SQUARE))
        zero = keep.tile([P, 1], F32, name="zero")
        nc.vector.memset(zero[:], 0.0)
        nc.vector.memset(s2_raw[:].rearrange("p q i -> p (q i)").bitcast(I32), 0)
        nc.vector.memset(s1_sb[:].rearrange("p e k -> p (e k)").bitcast(I32), 0)

        load_plane(0, 0)
        nc.sync.dma_start(offs_sb[:], offs)
        load_scales(s2_raw[:], w2_scales.rearrange("e s f i -> f (e s) i"))
        load_w2(0)
        for t in range(1, PACK):
            load_plane(0, t)
        for t in range(PACK):
            load_plane(1, t)
        load_a(0)
        load_w2(1)
        load_scales(s1_sb[:], w1_scales.rearrange("e s f k -> f (e s) k"))
        nc.sync.dma_start(w1_sb[:].bitcast(I32), w1_words.rearrange("e s p b -> p (e s) b").bitcast(I32))
        for q in range(1, S // QUARTER):
            load_a(q)

        windows = {b: keep.tile([P, T], F32, name=f"window_{b}") for b in VECTOR_BLOCKS + (SHARED_BLOCK,)}
        nc.vector.memset(windows[VECTOR_BLOCKS[0]][:], 0.0)
        nc.gpsimd.memset(windows[VECTOR_BLOCKS[1]][:], 0.0)
        nc.scalar.activation(windows[SHARED_BLOCK][:], zero[:].to_broadcast([P, T]), COPY)
        gate_turned = keep.tile([P, SQUARE], F32, name="gate_turned", align_bytes=64)
        nc.vector.transpose(gate_turned[:], gate_runs[:])
        squares = C // SQUARE
        for e, copy in enumerate((nc.vector.tensor_copy, nc.scalar.copy)):
            spread = keep.tile([P, squares, SQUARE], F32, name=f"spread_{e}", align_bytes=64)
            copy(spread[:], gate_turned[:, squares * e : squares * (e + 1)].unsqueeze(2).to_broadcast([P, squares, SQUARE]))
            nc.vector.transpose(gate_sb[:, C * e : C * (e + 1)], spread[:].rearrange("p b c -> p (b c)"))

        def offsets(first, count):
            return offs_sb[:, first // OFFSETS_PER_COLUMN : (first + count) // OFFSETS_PER_COLUMN]

        def gather_gated(s, t, first, count):
            nc.vector.tensor_tensor(
                rows[s][0][:, t, first : first + count], planes[s][t][:].indirect(offsets(first, count)), gate_sb[:, first : first + count], MULT
            )

        def gather_plain(s, t, first, count):
            e, col = divmod(first, C)
            nc.scalar.activation(rows[s][e][:, t, col : col + count], planes[s][t][:].indirect(offsets(first, count)), COPY)

        def group(s, first, grouped, gated):
            e, col = divmod(first, C)
            count = grouped.shape[1]
            side = LINE // 4
            source = rows[s][e][:, :, col : col + count].rearrange("p t (c i) -> p c t i", i=side)
            target = grouped.rearrange("p (c i) t -> p c t i", i=side)
            if gated:
                nc.scalar.copy(target, source)
            else:
                gates = gate_sb[:, first : first + count].rearrange("p (c i) -> p c i", i=side)
                nc.vector.tensor_tensor(target, source, gates.unsqueeze(2).to_broadcast([P, count // side, PACK, side]), MULT)

        def quantize(grouped, words, scale_bytes):
            nc.vector.quantize_mx(out=words.bitcast(FP8X4), scales=scale_bytes, in_=grouped.rearrange("p c t -> p (c t)"))

        g_codes = {}

        def quantize_g(s, first, grouped, words_tag):
            count = grouped.shape[1]
            words = keep.tile([P, count], U32, name=f"g_words_{s}_{first}", tag=words_tag, align_bytes=64)
            scale_bytes = keep.tile([P, count], U8, name=f"g_scales_{s}_{first}", align_bytes=64)
            quantize(grouped, words[:], scale_bytes[:])
            for col in range(0, count, P):
                g_codes[s, first + col] = (words[:, col : col + P], scale_bytes[:, col : col + P])

        def permute_words(e, copy):
            copy(
                w2_sb[e][:].bitcast(U16).rearrange("p s (t c i) -> p s c t i", t=PACK, i=LINE // 2),
                w2_raw[e][:].bitcast(U16).rearrange("p s (c i t) -> p s c t i", t=PACK, i=LINE // 2),
            )

        def permute_scales():
            nc.vector.tensor_copy(
                s2_sb[:].rearrange("p q (t c i) -> p q c t i", t=PACK, i=LINE),
                s2_raw[:].rearrange("p q (c i t) -> p q c t i", t=PACK, i=LINE),
            )

        def dh_pass(dh, s, first):
            e = first // C
            words, scale_bytes = g_codes[s, first]
            for t in range(PACK):
                nc.tensor.matmul_mx(
                    out=dh[:, t, :],
                    lhsT=w2_sb[e][:, s, 2 * P * t : 2 * P * (t + 1)].bitcast(FP4X4),
                    lhsT_scale=s2_sb[:, N_PASSES * e + s, P * t : P * (t + 1)],
                    rhs=words.bitcast(FP8X4),
                    rhs_scale=scale_bytes,
                    start=(s == 0 and t == 0),
                    stop=(s == N_PASSES - 1 and t == PACK - 1),
                )

        def mask(da, dh, a_grouped):
            nc.vector.scalar_tensor_tensor(da, a_grouped, 0.0, dh[:].rearrange("p t c -> p c t"), IS_GT, MULT)

        da_words = [keep.tile([P, C], U32, name=f"da_words_{e}", align_bytes=64) for e in range(E)]
        da_scales = [keep.tile([P, C], U8, name=f"da_scales_{e}", align_bytes=64) for e in range(E)]

        def quantize_da(e, da, h):
            cols = slice(QUARTER * h, QUARTER * (h + 1))
            quantize(da[:, cols, :], da_words[e][:, cols], da_scales[e][:, cols])

        def dx_product(dx, e, b, col):
            cols = slice(col, col + dx.shape[1])
            nc.tensor.matmul_mx(
                out=dx,
                lhsT=w1_sb[:, e, 2 * P * b : 2 * P * (b + 1)].bitcast(FP4X4),
                lhsT_scale=s1_sb[:, e, P * b : P * (b + 1)],
                rhs=da_words[e][:, cols].bitcast(FP8X4),
                rhs_scale=da_scales[e][:, cols],
                start=True,
                stop=True,
            )

        def dx_pair(dx, e, blocks, h):
            for j, b in enumerate(blocks):
                dx_product(dx[:, j, :], e, b, QUARTER * h)

        def scatter_scalar(b, first, values):
            nc.scalar.activation(windows[b][:].indirect(offsets(first, values.shape[1])), values, COPY)

        def scatter_vector(b, first, values):
            nc.vector.tensor_copy(windows[b][:].indirect(offsets(first, values.shape[1])), values)

        def store(b):
            nc.sync.dma_start(out[P * b : P * (b + 1), :], windows[b][:])

        for t in range(PACK):
            gather_gated(0, t, 0, C)
            gather_plain(0, t, C, C)
            if t == 0:
                permute_words(0, nc.scalar.copy)
                permute_scales()
                for j, b in enumerate(SCALAR_BLOCKS):
                    windows[b] = relay.tile([P, T], F32, name=f"window_{b}", align_bytes=64, offset=WINDOW_BYTES * j)
                    nc.gpsimd.memset(windows[b][:], 0.0)
        first_pass = [keep.tile([P, C, PACK], BF16, name=f"g_grouped_0_{e}", align_bytes=64) for e in range(E)]
        for e in range(E):
            group(0, C * e, first_pass[e][:], gated=(e == 0))

        dh_early = [psum_h.tile([P, PACK, P], F32, name=f"dh_0_{blk}", tag=f"dh_{blk}") for blk in range(BANKS_PER_EXPERT)]
        for t in range(PACK):
            gather_gated(1, t, 0, QUARTER)
            gather_plain(1, t, QUARTER, QUARTER)
            if t < FREE_ROWS:
                gather_plain(1, t, C, C)
            if t == 0:
                for e in range(E):
                    quantize_g(0, C * e, first_pass[e][:], f"g_words_0_{e}")
                for blk, dh in enumerate(dh_early):
                    dh_pass(dh, 0, P * blk)
        halves = QUARTER // P
        first_blocks = [keep.tile([P, P, PACK], BF16, name=f"g_grouped_1_{j}", align_bytes=64) for j in range(halves)]
        for j in range(halves):
            group(1, P * j, first_blocks[j][:], gated=True)
        second_quarter = keep.tile([P, QUARTER, PACK], BF16, name="g_grouped_second", align_bytes=64)
        for j in range(halves):
            group(1, QUARTER + P * j, second_quarter[:, P * j : P * (j + 1), :], gated=False)
            quantize_g(1, P * j, first_blocks[j][:], f"g_words_1_{j}")
        quantize_g(1, QUARTER, second_quarter[:], "g_words_second")
        permute_words(1, nc.vector.tensor_copy)
        for t in range(FREE_ROWS, PACK):
            gather_plain(1, t, C, C)

        early_blocks = (SHARED_BLOCK,) + SCALAR_BLOCKS
        da_early = relay.tile([P, C, PACK], BF16, name="da_0", align_bytes=64, offset=LATE_OFFSET + GROUPED_BYTES // 2)
        dx_vector = []

        def vector_products(h):
            dx = psum_v.tile([P, 2, QUARTER], F32, name="dx_v")
            dx_pair(dx, 0, VECTOR_BLOCKS, h)
            dx_vector.append(dx)

        for h in range(2):
            for j in range(halves):
                blk = halves * h + j
                dh_pass(dh_early[blk], 1, P * blk)
                mask(da_early[:, P * blk : P * (blk + 1), :], dh_early[blk], a_sb[h][:, :, P * j : P * (j + 1)].rearrange("p t c -> p c t"))
            quantize_da(0, da_early, h)
            if h == 1:
                vector_products(h)
            staged = []
            for pair in range(2):
                dx = psum_s.tile([P, 2, QUARTER], F32, name=f"dx_s_{h}_{pair}", tag=f"dx_s_{pair}")
                dx_pair(dx, 0, early_blocks[2 * pair : 2 * pair + 2], h)
                x = keep.tile([P, 2, QUARTER], F32, name=f"x_early_{h}_{pair}", align_bytes=64)
                nc.scalar.copy(x[:], dx[:])
                staged.extend(x[:, j, :] for j in range(2))
            if h == 0:
                vector_products(h)
            for b, values in zip(early_blocks, staged):
                scatter_scalar(b, QUARTER * h, values)

        late_pass = relay.tile([P, C, PACK], BF16, name="g_grouped_late", align_bytes=64, offset=LATE_OFFSET)
        for h in range(2):
            cols = slice(QUARTER * h, QUARTER * (h + 1))
            gates = gate_sb[:, C + QUARTER * h : C + QUARTER * (h + 1)].unsqueeze(2).to_broadcast([P, QUARTER, PACK])
            nc.gpsimd.tensor_tensor(late_pass[:, cols, :], rows[1][1][:, :, cols].rearrange("p t c -> p c t"), gates, MULT)
        dh_late = [psum_h.tile([P, PACK, P], F32, name=f"dh_1_{blk}", tag=f"dh_{blk}") for blk in range(BANKS_PER_EXPERT)]
        for blk, dh in enumerate(dh_late):
            dh_pass(dh, 0, C + P * blk)
        x_first = relay.tile([P, 2, QUARTER], F32, name="x_first", align_bytes=64, offset=LATE_OFFSET + GROUPED_BYTES)
        x_second = keep.tile([P, QUARTER], F32, name="x_second", tag="x_second", align_bytes=64)
        x_third = relay.tile([P, QUARTER], F32, name="x_third", align_bytes=64, offset=second_offset)
        nc.vector.tensor_copy(x_first[:], dx_vector[0][:])
        nc.vector.tensor_copy(x_second[:], dx_vector[1][:, 0, :])
        for j, b in enumerate(VECTOR_BLOCKS):
            scatter_vector(b, 0, x_first[:, j, :])
        scatter_vector(VECTOR_BLOCKS[0], QUARTER, x_second[:])
        nc.vector.tensor_copy(x_third[:], dx_vector[1][:, 1, :])
        quantize_g(1, C, late_pass[:], "x_second")
        scatter_vector(VECTOR_BLOCKS[1], QUARTER, x_third[:])
        a_late = []
        for h, offset in enumerate((LATE_OFFSET + GROUPED_BYTES // 2, LATE_OFFSET - GROUPED_BYTES // 2)):
            grouped_a = relay.tile([P, QUARTER, PACK], F32, name=f"a_late_{h}", align_bytes=64, offset=offset)
            nc.gpsimd.tensor_scalar(grouped_a[:], a_sb[2 + h][:].rearrange("p t c -> p c t"), 1.0, 0.0, MULT, ADD)
            a_late.append(grouped_a)

        da_late = keep.tile([P, C, PACK], BF16, name="da_1", align_bytes=64)
        x_late = keep.tile([P, 2, C], F32, name="x_late", align_bytes=64)

        def late_mask(blk):
            h, j = divmod(blk, halves)
            dh_pass(dh_late[blk], 1, C + P * blk)
            mask(da_late[:, P * blk : P * (blk + 1), :], dh_late[blk], a_late[h][:, P * j : P * (j + 1), :])

        def late_products(h):
            dx = psum_v.tile([P, 2, QUARTER], F32, name="dx_v")
            dx_pair(dx, 1, (SHARED_BLOCK, VECTOR_BLOCKS[0]), h)
            return dx

        for blk in range(halves + 1):
            late_mask(blk)
        quantize_da(1, da_late, 0)
        dx = late_products(0)
        late_mask(BANKS_PER_EXPERT - 1)
        nc.vector.tensor_copy(x_late[:, :, 0:QUARTER], dx[:])
        quantize_da(1, da_late, 1)
        scatter_vector(SHARED_BLOCK, C, x_late[:, 0, 0:QUARTER])

        def stage_scalar(b, width, bank):
            dx = psum_s.tile([P, C], F32, name=f"dx_late_{b}", tag=f"dx_s_{bank}")
            dx_product(dx[:], 1, b, 0)
            x = keep.tile([P, C], F32, name=f"x_late_{b}", align_bytes=64)
            for col in range(0, C, width):
                nc.scalar.copy(x[:, col : col + width], dx[:, col : col + width])
            return x

        first_block, second_block, last_block = SCALAR_BLOCKS
        x_a = stage_scalar(first_block, QUARTER, 0)
        dx = late_products(1)
        for j in range(2):
            nc.vector.tensor_copy(x_late[:, j, QUARTER:C], dx[:, j, :])
        scatter_vector(SHARED_BLOCK, C + QUARTER, x_late[:, 0, QUARTER:C])
        store(SHARED_BLOCK)
        dx = psum_v.tile([P, C], F32, name="dx_v")
        dx_product(dx[:], 1, VECTOR_BLOCKS[1], 0)
        x_last = keep.tile([P, C], F32, name="x_last", align_bytes=64)
        nc.vector.tensor_copy(x_last[:], dx[:])
        scatter_scalar(first_block, C, x_a[:, 0:QUARTER])
        x_b = stage_scalar(second_block, C, 1)
        scatter_scalar(first_block, C + QUARTER, x_a[:, QUARTER:C])
        store(first_block)
        scatter_vector(VECTOR_BLOCKS[0], C, x_late[:, 1, :])
        store(VECTOR_BLOCKS[0])
        scatter_scalar(second_block, C, x_b[:, 0:QUARTER])
        x_c = stage_scalar(last_block, C, 1)
        scatter_scalar(second_block, C + QUARTER, x_b[:, QUARTER:C])
        store(second_block)
        scatter_vector(VECTOR_BLOCKS[1], C, x_last[:])
        store(VECTOR_BLOCKS[1])
        for col in range(0, C, QUARTER):
            scatter_scalar(last_block, C + col, x_c[:, col : col + QUARTER])
        store(last_block)
